import numpy as np, ml_dtypes
CORES = [113,118,241,246]
N = 4
BF = ml_dtypes.bfloat16
def gentries(a):
    return np.ascontiguousarray(a.reshape(8, 16, -1).transpose(0, 2, 1)).reshape(8, -1)
def gtable(e):
    e = np.asarray(e); return np.ascontiguousarray(e.reshape(8, -1, 16).transpose(0, 2, 1)).reshape(128, -1).astype(np.int32)
W, O, S, D, T, RO = 1920, 160, 32, 3, 3, 3
DS = D * S; L = O + DS
H = T * (RO - 1) // 2
def parts(rng, h, q, full=False):
    th = rng.random((N, 8, W)) < rng.choice(np.array([0.2, 0.3, 0.45]), (N, 8, 1))
    th[..., :DS] = full | (rng.random((N, 8, DS)) < 0.9); th[..., W - DS:] = full | (rng.random((N, 8, DS)) < 0.85)
    rt = DS + np.argsort(rng.random((N, 8, W - DS)), axis=-1)[..., :O]
    np.put_along_axis(th, rt, True, 2)
    order = DS + np.argsort(np.where(th, 2.0, 0.0)[..., DS:] + rng.random((N, 8, W - DS)), axis=-1)
    pos = np.zeros((N, 8, W), np.int64); np.put_along_axis(pos, order, np.arange(W - DS)[None, None, :], 2)
    nv = np.maximum(W - DS - np.sum(th[..., DS:], axis=-1), 1)[..., None, None]
    p = pos[..., None] - nv; u = rng.random((N, 8, W, 16))
    deep = (rng.random((N, 8, W, 16)) < rng.choice(q, (N, 8, W, 1))) & (p > 0)
    ix = np.where(deep, nv + (u * u * u * np.maximum(p, 0)).astype(np.int64), (u * nv).astype(np.int64))
    a = np.take_along_axis(order, ix.reshape(N, 8, 16 * W), 2).reshape(N, 8, W, 16)
    a = np.where(rng.random(a.shape) < h, rng.integers(0, DS, a.shape), a)
    return th, rt, a, order, nv
def fresh(rng, th, a, r, g):
    m = DS + rng.permutation(W - 2 * DS)
    th[r, g] = True; th[r, g, m[:24]] = False
    a[r, g] = m[rng.integers(0, 24, (W, 16))]
    return a[r, g], m[24:]
def chain(x, first, cells):
    c = np.concatenate([first[None, :], cells]); x[c[:-1], 0] = c[1:]
def values(rng):
    return np.clip(rng.integers(0, 16, (N, 8, 16, W)) + rng.integers(-4, 5, (N, 8, 1, W)), 0, 15)
def pack(th, rt, a, v):
    return {"ag": np.ascontiguousarray(a.transpose(0, 1, 3, 2)).reshape(N, 128, W).astype(np.int32), "vals": np.where(th[:, :, None, :], -1, v).reshape(N, 128, W).astype(np.float32).astype(BF),
            "rts": np.stack([gtable(x) for x in rt])}
def setup_inputs(rng):
    th, rt, a, order, nv = parts(rng, rng.choice(np.array([0.01, 0.02, 0.04]), (N, 8, 1, 1)), np.array([0.0, 0.08, 0.25]))
    return pack(th, rt, a, values(rng))
def setup_inputs_room(rng):
    th, rt, a, order, nv = parts(rng, 0.0, np.array([0.0, 0.0, 0.1]), True)
    for r in range(N):
        for g in range(4):
            lanes = rng.permutation(O); at = 0
            for d in range(D):
                n = int(rng.choice(np.array([0, 1, S - 1, S])))
                if r == 0 and d == 0: n = (S, 1, 0, S - 1)[g]
                a[r, g, rt[r, g, lanes[at:at + n]], 0] = d * S + rng.permutation(S)[:n]; at += n
    q = int(rng.integers(0, N)); j = np.arange(DS); early = np.isin(j % 4, np.array([1, 2]))
    for r in range(N):
        x, m = fresh(rng, th, a, r, 4); rt[r, 4] = m[:O]; m = m[O:]; d = (q - r) % N
        if d == 0:
            chain(x, rt[r, 4], m[:O * (T + H)].reshape(T + H, O)); m = m[O * (T + H):]
            chain(x, W - DS + j, m[:DS * H].reshape(H, DS))
        elif d <= D: x[rt[r, 4, :S], 0] = (d - 1) * S + rng.permutation(S)
        x, m = fresh(rng, th, a, r, 5); rt[r, 5] = m[:O]; m = m[O:]
        c = m[:T * DS].reshape(T, DS); chain(x, rt[r, 5, :DS], c); x[c[-1], 0] = rng.permutation(DS)
        s = rt[r, 5, DS:]; y = m[T * DS:T * DS + O - DS]; k = np.arange(O - DS) % 3
        x[s[k < 2], 0] = y[k < 2]; x[y[k == 0], 0] = s[k == 0]
        x[y[k == 1], 1] = s[k == 1]; x[y[k == 1], 8] = s[k == 1]; x[s[k == 2], 1] = s[k == 2]; x[s[k == 2], 8] = s[k == 2]
        x, m = fresh(rng, th, a, r, 6); rt[r, 6] = m[:O]; m = m[O:]; th[r, 6, W - DS:] = False
        s = rt[r, 6, :DS]; c = m[:H * DS].reshape(H, DS); x[s, 0] = rng.permutation(DS); x[s, 1] = c[0]; x[s, 8] = c[0]; chain(x, c[0], c[1:])
        x, m = fresh(rng, th, a, r, 7); rt[r, 7] = m[:O]; m = m[O:]; n = DS // 2
        s = rt[r, 7, :DS]; e = W - DS + j; c = m[:T * n].reshape(T, n); m = m[T * n:]; f = m[:T * n].reshape(T, n); z = m[T * n:T * n + n]
        x[s[early], 0] = j[early]; chain(x, s[~early], c); x[c[-1], 0] = j[~early]
        chain(x, e[early], f); x[f[-1], 0] = z[j[early] // 2]; x[e[~early], 0] = z[j[~early] // 2]; x[z, 0] = z
    return pack(th, rt, a, values(rng))
def setup_inputs_crowd(rng):
    th, rt, a, order, nv = parts(rng, 0.01, np.array([0.0, 0.1]), True); n_ = np.arange(N)[:, None]
    for g in range(8):
        k = nv[:, g, :, 0] + rng.integers(0, 4, (N, O)); hot = np.take_along_axis(order[:, g], k, 1)
        if g == 1: hot = np.full((N, O), W - 1)
        if g == 2: hot[:, 1:] = rt[:, g, :-1]
        if g == 3: hot = np.where(rng.random((N, O)) < 0.5, 0, DS - 1)
        if g == 5:
            hot[:, :DS] = np.arange(DS)
            for r in range(N):
                x = a[r, g]; v0 = order[r, g, 0]
                u = order[r, g, nv[r, g, 0, 0]:]; u = u[(u < W - DS) & ~np.isin(u, rt[r, g])]; f = u[-T - 1:]
                x[np.isin(x, f)] = v0
                x[u[:4]] = np.where(x[u[:4]] >= W - DS, v0, x[u[:4]])
                x[W - DS:, 0] = f[T]; x[f[:-1], 0] = f[1:]
                hot[r, DS:] = u[rng.integers(0, 4, O - DS)]; hot[r, O - 1] = f[0]
        a[n_, g, rt[:, g], 0] = np.where((rng.random((N, O)) < 0.8) | (g == 5), hot, a[n_, g, rt[:, g], 0])
    a[:, 1, W - 1] = order[:, 1, :16]
    return pack(th, rt, a, values(rng))
def setup_inputs_halves(rng):
    th, rt, a, order, nv = parts(rng, 0.02, np.array([0.0, 0.1, 0.2]))
    o = np.argsort(rng.random((N, 8, 16, W), dtype=np.float32), axis=2); k = rng.choice(np.array([0, 7, 8, 8, 9, 9, 10, 16]), (N, 8, 1, W))
    v = np.where(o < k, rng.choice(np.array([8, 8, 15]), (N, 8, 1, W)), rng.choice(np.array([0, 7, 7]), (N, 8, 1, W)))
    a[:, 4, :, 9:] = a[:, 4, :, 8:9]; a[:, 5, :, 1:8] = a[:, 5, :, 1:2]; a[:, 6] = a[:, 6, :, 0:1]
    a[:, 7] = np.where(rng.random((N, W, 16)) < 0.1, rng.choice(np.array([0, DS - 1, DS, W - DS, W - 1]), (N, W, 16)), a[:, 7])
    return pack(th, rt, a, v)
def setup_inputs_rings(rng):
    th, rt, a, order, nv = parts(rng, 0.01, np.array([0.0, 0.1]), True); n_ = np.arange(N)[:, None]
    for g in (0, 2, 4, 6): a[n_, g, order[:, g, 1:], 0] = order[:, g, :-1]
    for g in (1, 3, 5):
        e = np.arange(0, DS, 1 if g < 4 else 2)[None, :]
        a[n_, g, W - DS + e, 0] = (e + g * S) % DS
        a[n_, g, rt[:, g, :DS], 0] = np.arange(DS)[None, :]
        x = rt[:, g, DS:DS + 8]; a[n_, g, x, 0] = x
        x = rt[:, g, DS + 8:DS + 16]; a[n_, g, x, 0] = x[:, ::-1]
    k = (DS - 1 - np.arange(DS)) % 3; n = min(DS, O - DS)
    for r in range(N):
        x, m = fresh(rng, th, a, r, 7); e = W - DS + rng.permutation(DS)
        rt[r, 7] = np.concatenate([e, m[:O - DS]]); x[m[:n], 0] = rng.permutation(DS)[:n]; m = m[O - DS:]
        x[e[k == 0], 0] = np.roll(e[k == 0], 1)
        up = e[k == 1]; chain(x, up, m[:(T - 1) * len(up)].reshape(T - 1, len(up)))
    return pack(th, rt, a, values(rng))
def setup_inputs_spread(rng):
    th, rt, a, order, nv = parts(rng, rng.choice(np.array([0.002, 0.02, 0.1]), (N, 8, 1, 1)), np.array([0.0, 0.05, 0.15, 0.5]))
    v = np.minimum((np.exp2(4 * rng.random((N, 8, 1, W))) * rng.random((N, 8, 16, W))).astype(np.int64), 15)
    return pack(th, rt, a, np.where(rng.random((N, 8, 1, W)) < 0.5, v, 15 - v))
def check_inputs(d):
    bad = []
    v = np.asarray(d["vals"]).astype(np.float32).reshape(N, 8, 16, W); r = np.stack([gentries(x) for x in d["rts"]])
    if np.min(d["ag"]) < 0 or np.max(d["ag"]) > W - 1: bad.append("range of ag")
    if not np.all((v == np.floor(v)) & (v >= -1) & (v <= 15)): bad.append("whole numbers of vals")
    if np.any(np.any(v < 0, axis=2) != np.all(v < 0, axis=2)): bad.append("thunks are -1 in all 16 rows")
    s = np.sort(r, axis=-1)
    if np.any(s[..., 1:] == s[..., :-1]): bad.append("starting cells differ")
    if np.min(r) < DS or np.max(r) > W - 1: bad.append("range of rts")
    elif not np.all(np.take_along_axis(v[:, :, 0], r.astype(np.int64), 2) == -1): bad.append("starting cells are thunks")
    return bad
def reference(ag, vals, rts):
    B = N * 8; i16 = np.arange(16)
    arg = np.stack([gentries(x) for x in ag]).reshape(B, W, 16).astype(np.int64)
    val = vals.astype(np.float32).astype(np.int16).reshape(B, 16, W)
    cur = np.full((B, L), -1, np.int64)
    cur[:, :O] = np.stack([gentries(x) for x in rts]).reshape(B, O)
    par = np.full((B, W), -1, np.int64)
    np.put_along_axis(val, cur[:, None, :O], -2, 2)
    rows = np.arange(B)[:, None]; lane = np.arange(L)[None, :]
    for rnd in range(RO):
        for step in range(T):
            act = cur >= 0; c = np.maximum(cur, 0)
            a = arg[rows, c]
            v = np.take_along_axis(val, a.reshape(B, 1, L * 16), 2).reshape(B, 16, L, 16)
            st = v[:, 0]; s = v[..., 0]; has = st[..., 0] >= 0
            many = np.sum(s >= 8, axis=1) >= 9
            need = np.where(~has[..., None], i16 == 0, np.where(many[..., None], (i16 >= 1) & (i16 < 8), i16 >= 8))
            lack = need & (st < 0); stop = np.any(lack, axis=-1); first = np.argmax(lack, axis=-1)[..., None]
            to = np.take_along_axis(a, first, 2)[..., 0]; kind = np.take_along_axis(st, first, 2)[..., 0]
            want = act & stop & (kind == -1); done = act & ~stop
            lead = np.full((B, W), L, np.int64); b, k = np.nonzero(want); np.minimum.at(lead, (b, to[b, k]), k)
            win = want & (np.take_along_axis(lead, to, 1) == lane); ent = win & (to >= DS)
            res = np.maximum(np.max(np.where(need[:, None], v, -9), axis=-1) - s, 0)
            b, k = np.nonzero(done); val[b, :, c[b, k]] = res[b, :, k]
            b, k = np.nonzero(win); val[b, :, to[b, k]] = -2
            cur = np.where(ent, to, np.where(done, np.take_along_axis(par, c, 1), cur))
            b, k = np.nonzero(ent); par[b, to[b, k]] = c[b, k]
        if rnd < RO - 1:
            old = np.array(val).reshape(N, 8, 16, W); new = np.array(old); c4 = cur.reshape(N, 8, L)
            for r in range(N):
                for d in range(1, D + 1):
                    q = (r + d) % N; lo = (d - 1) * S; e = W - DS + lo
                    asked = old[r, :, 0, lo:lo + S] == -2; ev = old[q, :, :, e:e + S]
                    home = asked & (ev[:, 0] >= 0); go = asked & (ev[:, 0] == -1)
                    new[r, :, :, lo:lo + S] = np.where(home[:, None, :], ev, old[r, :, :, lo:lo + S])
                    new[q, :, :, e:e + S] = np.where(go[:, None, :], -2, ev)
                    c4[q, :, O + lo:O + lo + S] = np.where(go, e + np.arange(S)[None, :], c4[q, :, O + lo:O + lo + S])
            val = new.reshape(B, 16, W); cur = c4.reshape(B, L)
    return {"yv": val.reshape(N, 128, W).astype(np.float32).astype(BF), "ya": np.stack([gtable(x) for x in cur.reshape(N, 8, L)]).astype(np.float32)}

@@ -1,0 +1,486 @@
+from concourse.bass import DstId, RemoteDMATransfer
+from concourse.mybir import AluOpType, ActivationFunctionType
+
+W, OWN, S, D, STEPS, ROUNDS = 1920, 160, 32, 3, 3, 3
+DS = S * D
+L = OWN + DS
+REST = W
+IDO = 2048
+CTW = 2192
+BASE, THR0, W0 = 256.0 / 150.0, 2.56, 1.0e25
+STEP = 8192.0
+SPLIT = {80: (20, 26, 18, 16), 128: (40, 42, 22, 24)}
+ENG = 4
+
+F, H, B, I, U = "float32", "float16", "bfloat16", "int32", "uint16"
+SB = {}
+for _t, _l in ((I, "agt 1936 rin 16 pc 8 pc2 8 m1 128 m2 128"),
+               (U, "tn 32 a0 16 ol 128 xu 256"),
+               (H, "bl 152 bh 152 zx 152 gg 256 x5 96 x6 96"),
+               (F, "col 48 oh 16 df 4 hs 4 k16 4 geo 16 pat 256 of 128 xs 256 d0 128 d1 128 fo 128 s1 16 s2 16 s3 16 x4 96 yo 16"),
+               (B, "vin 1920 ct 2192 dt 2048 tmpw 1920 tmp2 1920 outv 1920 i0 256 i1 256 pm 152 gh 128 kb 256 zer 256 uu 256 u1 256 "
+                   "ones 256 zd 152 mi 128 mn 128 mu 128 dec 128 cx 128 bw 128 pq 152 hb 128 r3 128 mf 128 blo 128 bhi 128 dg 256 "
+                   "bm 128 pat2 256 mp 768 thr 256 hr 160 ecol 96 sv 256 sg 256 vv 2048 rr 2048 dc0 256 dc1 256 rp 256 pp 256 "
+                   "ee 2176 sn 256 ls 256 yy 256 zz 256 ww 256 wn 256 stg0 192 stg1 192 land0 192 land1 192 gt 96 te 96 te2 96 "
+                   "x1 96 dif 96 x2 96 x3 96")):
+    _w = _l.split()
+    for _k in range(0, len(_w), 2):
+        SB[_w[_k]] = (int(_w[_k + 1]), _t)
+SCRATCH = {k: ("sbuf", [128, v[0]], v[1]) for k, v in SB.items()}
+for _k in range(8):
+    SCRATCH["pb%d" % _k] = ("psum", [128, 512], F)
+POOL = {"v": 44, "s": 30, "p": 30, "g": 8, "d": 16}
+SEMAPHORES = ["%s%d" % (e, k) for e in POOL for k in range(POOL[e])] + ["arr0", "arr1", "snt0", "snt1"]
+A = AluOpType
+AF = ActivationFunctionType
+ID = AF.Identity
+
+
+def R(name, lo=0, hi=None, step=1):
+    return (name, lo, SB[name][0] if hi is None else hi, step)
+
+
+def C(k):
+    return ("col", k, k + 1, 1)
+
+
+def P(k, lo, hi):
+    return ("pb%d" % k, lo, hi, 1)
+
+
+def ind(win, off):
+    return ("ind", win, off)
+
+
+def overlap(a, b):
+    if a[1] >= b[2] or b[1] >= a[2]:
+        return False
+    return a[3] != b[3] or a[3] == 1 or (a[1] - b[1]) % a[3] == 0
+
+
+def rank_program(g, core, T, topo):
+    rank = T.rank_of(core)
+    if rank is None:
+        return
+    Q = {"v": g.vector, "s": g.scalar, "p": g.tensor, "g": g, "y": g.sync}
+    V = g.vector
+    ops = []
+
+    def ap(x):
+        if isinstance(x, tuple):
+            if x[0] == "ind":
+                return ap(x[1]).indirect(ap(x[2]))
+            return T[x[0]][:, x[1]:x[2]:x[3]] if x[3] > 1 else T[x[0]][:, x[1]:x[2]]
+        return x
+
+    def add(eng, fn, ins, outs, kind="c", acc=False, ext=None):
+        rd = [x[2] for x in outs if x[0] == "ind"]
+        for x in ins:
+            if isinstance(x, tuple):
+                rd += [x[1], x[2]] if x[0] == "ind" else [x]
+        ops.append({"e": eng, "fn": fn, "r": rd, "w": [x[1] if x[0] == "ind" else x for x in outs], "k": kind, "acc": acc, "ext": ext})
+
+    def ts(out, in0, s1, op0, s2=None, op1=None):
+        if op1 is None:
+            add("v", lambda: V.tensor_scalar(ap(out), ap(in0), ap(s1), None, op0), [in0, s1], [out])
+        else:
+            add("v", lambda: V.tensor_scalar(ap(out), ap(in0), ap(s1), ap(s2), op0, op1), [in0, s1, s2], [out])
+
+    def tt(out, a, b, op):
+        add("v", lambda: V.tensor_tensor(ap(out), ap(a), ap(b), op), [a, b], [out])
+
+    def cp(out, a):
+        add("v", lambda: V.tensor_copy(ap(out), ap(a)), [a], [out])
+
+    def ms(out, c):
+        add("v", lambda: V.memset(ap(out), c), [], [out])
+
+    def scan(out, d0, d1, init=0.0, op0=A.add, op1=A.max):
+        add("v", lambda: V.tensor_tensor_scan(ap(out), ap(d0), ap(d1), init, op0, op1), [d0, d1], [out])
+
+    def act(out, a, f=ID, bias=0.0, scale=1.0):
+        add("s", lambda: g.scalar.activation(ap(out), ap(a), f, bias=ap(bias), scale=ap(scale)), [a, bias, scale], [out])
+
+    def fill(out, src, c):
+        act(out, src, bias=c, scale=0.0)
+
+    def mm(out, lt, rhs, start, stop):
+        add("p", lambda: g.tensor.matmul(ap(out), ap(lt), ap(rhs), start, stop), [lt, rhs], [out], acc=not start)
+
+    def iota(out, pat, base, cm):
+        if SB[out[0]][1] == I:
+            add("g", lambda: g.iota(ap(out), pat, base, cm), [], [out])
+        else:
+            add("g", lambda: g.iota(ap(out), pat, base, cm, allow_small_or_imprecise_dtypes=True), [], [out])
+
+    def load(q, out, src):
+        add(q, lambda: Q[q].dma_start(ap(out), src), [], [out], kind="d")
+
+    def store(q, dst, a):
+        add(q, lambda: Q[q].dma_start(dst, ap(a)), [a], [], kind="d")
+
+    load("y", R("vin"), T.vals[:, :])
+    load("s", R("rin", 0, 10), T.rts[:, :])
+    load("y", R("agt", 0, W), T.ag[:, :])
+
+    cR, cG, cLO, cHI, cW, cW2, cHB, cOFF, cOFF2, cHOLE, cHR, cG2, cG21, cU8, cMF, cM0, cG16 = [C(k) for k in range(17)]
+    cA = 20
+    CT, AG = R("ct"), R("agt")
+
+    def OH(j):
+        return R("oh", j, j + 1)
+    iota(R("pc", 0, 1), [[0, 1]], 0, 1)
+    iota(R("i0"), [[0, 16], [1, 16]], 0, 0)
+    iota(R("i1"), [[1, 16], [0, 16]], 0, 0)
+    iota(R("pm"), [[1, 152]], -15, -1)
+    iota(R("gh"), [[1, 16], [0, 8]], 0, 0)
+    iota(R("pq"), [[1, 152]], -15, 0)
+    iota(R("d1", 3, 64, 4), [[16, 16]], W + 1 + IDO, 0)
+    iota(R("ecol"), [[1, DS]], -DS, 0)
+    ms(R("mp"), 1.0 / 16)
+    ts(R("pc2", 0, 1), R("pc", 0, 1), 15, A.bitwise_and)
+    ts(R("pc2", 1, 2), R("pc", 0, 1), 4, A.logical_shift_right)
+    ms(R("agt", W, 1936), REST)
+    cp(R("col", 0, 2), R("pc2", 0, 2))
+    ms(R("mp", 0, 768, 8), -64.0)
+    ms(R("ct", W, CTW), 0.0)
+    ms(R("tn", 26, 32), REST)
+    ts(R("oh"), R("i0", 0, 16), cR, A.is_equal)
+    ms(R("d0"), 0.0)
+    ts(R("uu"), R("i0"), OH(0), A.mult, 1.0 / 256, A.mult)
+    ts(R("col", cA, cA + 8), R("i0", 8, 16), OH(2), A.mult, 1.0 / 256, A.mult)
+    ts(cHOLE, OH(3), 1.0 / 256, A.mult)
+    tt(R("df"), R("oh", 0, 4), R("oh", 4, 8), A.subtract)
+    ts(R("u1"), R("i1"), OH(1), A.mult, 1.0 / 256, A.mult)
+    fill(R("ones"), R("i0"), 1.0)
+    fill(R("zer"), R("i0"), 0.0)
+    fill(R("kb"), R("i0"), 1.0 / BASE)
+    fill(R("k16"), R("i0", 0, 4), 1.0 / 16)
+    fill(R("geo"), R("i0", 0, 16), BASE)
+    act(cG2, cG, scale=2.0)
+    act(cG21, cG, scale=2.0, bias=1.0)
+    act(cG16, cG, scale=16.0)
+    ts(cLO, cR, 7.5, A.is_lt)
+    tt(R("uu"), R("uu"), R("u1"), A.add)
+    ts(R("mi"), R("pm", 15, 143), 0.0, A.is_equal)
+    for a in (7, 0, 1, 2, 3, 4, 5, 6):
+        if a in (4, 6):
+            act(R("dt", 256 * a, 256 * a + 256), R("uu"), bias=C(cA + a))
+        else:
+            ts(R("dt", 256 * a, 256 * a + 256), R("uu"), C(cA + a), A.add)
+    tt(cHR, R("dt", REST, REST + 1), cHOLE, A.add)
+    ts(cHI, cR, 7.5, A.is_gt)
+    for h in range(4):
+        mm(P(3 + h, 0, 480), R("mi"), R("dt", 480 * h, 480 * h + 480), True, False)
+    act(R("hr"), R("zer", 0, 160), bias=cHR)
+    act(R("ct", REST, REST + 1), cHR)
+    ts(R("zx"), R("pm"), 0.0, A.is_equal, OH(0), A.mult)
+    ts(R("bl"), R("pm"), 0.0, A.is_equal, cLO, A.mult)
+    ts(R("bh"), R("pm"), 0.0, A.is_equal, cHI, A.mult)
+    scan(R("hs"), R("k16"), R("df"), 0.0, A.mult, A.add)
+    scan(R("s1"), R("geo"), R("oh"), 0.0, A.mult, A.add)
+    ts(R("blo"), R("gh"), cG2, A.is_equal, 2048.0, A.mult)
+    ts(R("bhi"), R("gh"), cG21, A.is_equal, 2048.0, A.mult)
+    ts(R("bm"), R("i1", 0, 128), cG, A.is_equal)
+    ts(R("dg"), R("i0"), cR, A.is_equal)
+    act(cW, R("hs", 3, 4), scale=2.0 ** 20)
+    act(cW2, R("hs", 2, 3), scale=2.0 ** 16)
+    act(cHB, R("df", 3, 4), scale=2.0 ** 96)
+    act(cOFF, cR, scale=-STEP, bias=15 * STEP)
+    act(cOFF2, cR, scale=-4.0, bias=60.0)
+    scan(R("thr"), R("kb"), R("zer"), -THR0 * W0 * BASE, A.mult, A.add)
+    cp(R("tn", 16, 26), R("rin", 0, 10))
+
+    for h in range(4):
+        lo, hi = 480 * h, 480 * h + 480
+        ts(R("tmpw", lo, hi), R("vin", lo, hi), 0.0, A.is_lt, 17.0, A.mult)
+        mm(P(3 + h, 0, 480), R("mi"), R("vin", lo, hi), False, False)
+        mm(P(3 + h, 0, 480), R("mi"), R("tmpw", lo, hi), False, True)
+        if h % 2 == 0:
+            act(R("ct", lo, hi), P(3 + h, 0, 480), bias=-16.0)
+    ts(R("ct", 480, 960), P(4, 0, 480), -16.0, A.add)
+    ts(R("zd"), R("pq"), cG16, A.is_equal, cW2, A.mult)
+    ts(R("ct", 1440, W), P(6, 0, 480), -16.0, A.add)
+    cp(ind(CT, R("tn", 16, 26)), R("hr"))
+    act(R("dec"), R("bm"), scale=cW)
+    act(R("cx"), R("i0", 0, 128), bias=-15.0 * 64, scale=64.0)
+    act(R("pat"), R("dg"), bias=STEP, scale=-(2.0 ** 20 + STEP))
+    fill(R("d1", 64, 128), R("i0", 0, 64), float(REST + IDO))
+    ts(R("d1", 67, 104, 4), R("rin", 0, 10), float(IDO), A.add)
+
+    def constants(part):
+        if part == 0:
+            act(R("hb"), R("bm"), scale=cHB)
+            act(cU8, OH(8), scale=1024.0)
+            act(R("mn"), R("mi"), scale=-1.0)
+            act(R("mu"), R("bm"), scale=cU8)
+        elif part == 1:
+            act(R("bw"), R("bm"), scale=R("s1", 15, 16))
+            act(R("pat2"), R("dg"), bias=4.0, scale=-1028.0)
+            fill(R("d1", 2, 128, 4), R("i0", 0, 32), 0.0)
+            fill(R("d1", 1, 64, 4), R("i0", 0, 16), 0.0)
+            fill(R("d1", 0, 64, 4), R("i0", 0, 16), 0.0)
+            fill(R("d0", 1, 64, 4), R("i0", 0, 16), 1.0)
+            fill(R("d0", 2, 64, 4), R("i0", 0, 16), 1.0)
+            act(R("d1", 3, 64, 4), R("d1", 3, 64, 4), bias=cR)
+        else:
+            act(cM0, OH(8), scale=-16.0)
+            act(R("r3"), R("bm"), scale=OH(3))
+            act(cMF, OH(3), scale=-256.0, bias=cM0)
+            act(R("mf"), R("bm"), scale=cMF)
+
+    def CC(k):
+        return R("d1", 67, 64 + 4 * k, 4)
+    NEXT = R("fo", 67, 128, 4)
+
+    def args(nl):
+        act(R("gg", 0, nl), ind(AG, R("tn", 16, 16 + nl // 16)))
+
+    def digits(nl, dc):
+        act(R(dc, 0, nl), ind(R("dt"), R("tn", 16, 16 + nl // 16)))
+
+    def lists(nl):
+        k, m = nl // 16, nl // 2
+        for r in range(16):
+            mm(P(0, 0, k), R("zx", 15 - r, 143 - r), R("gg", r, nl, 16), r == 0, r == 15)
+        mm(P(2, 0, m), R("bh", 23, 151), R("gg", 0, nl, 2), True, False)
+        mm(P(2, 0, m), R("bh", 15, 143), R("gg", 1, nl, 2), False, True)
+        mm(P(1, 0, m), R("bl", 15, 143), R("gg", 0, nl, 2), True, False)
+        mm(P(1, 0, m), R("bl", 7, 135), R("gg", 1, nl, 2), False, False)
+
+    def step(nl, dc, first):
+        k, m = nl // 16, nl // 2
+        hk = 2 * (k // 4)
+        hl, hm = 16 * hk, 8 * hk
+        kh = k // 2
+        h = 16 * kh
+        n = SPLIT[m]
+        c = [0, n[0], n[0] + n[1], n[0] + n[1] + n[2], m]
+        la = 2 * c[3]
+        cp(R("a0", 0, k), P(0, 0, k))
+        act(R("sg", 0, hl), ind(CT, R("a0", 0, hk)), AF.Sign, bias=8.5)
+        ts(R("sg", hl, nl), ind(CT, R("a0", hk, k)), -8.5, A.is_gt, 2.0, A.mult)
+        act(R("of", 0, hm), P(2, 0, hm), bias=2048.0)
+        act(R("of", hm, m), P(2, hm, m), bias=17 * 2048.0)
+        mm(P(1, 0, m), R("blo"), R("sg", 0, nl, 2), False, False)
+        mm(P(1, 0, m), R("bhi"), R("sg", 1, nl, 2), False, True)
+        act(R("pp", 0, nl), ind(CT, R("tn", 16, 16 + k)))
+        if not first:
+            cp(CC(16), NEXT)
+        halves = [(0, m // 2), (m // 2, m)]
+        for lo, hi in halves:
+            tt(R("m1", lo, hi), P(1, lo, hi), R("of", lo, hi), A.max)
+        for lo, hi in halves:
+            ts(R("m2", lo, hi), R("m1", lo, hi), 2047, A.bitwise_and)
+        for lo, hi in halves:
+            cp(R("ol", lo, hi), R("m2", lo, hi))
+        mm(P(3, 0, la), R("cx"), R("ones", 0, la), True, False)
+        mm(P(4, la, nl), R("cx"), R("ones", la, nl), True, False)
+        mm(P(5, 0, h), R("mi"), R("thr", 0, h), True, False)
+        mm(P(7, h, nl), R("mi"), R("thr", h, nl), True, False)
+        for r in range(16):
+            mm(P(0, 0, k), R("zd", 15 - r, 143 - r), R("pp", r, nl, 16), r == 0, r == 15)
+        for j in (0, 2, 3):
+            act(R("vv", 16 * c[j], 16 * c[j + 1]), ind(CT, R("ol", c[j], c[j + 1])), bias=1.0 / 16)
+        if first == 1:
+            constants(0)
+        act(R("sv", 0, nl), ind(CT, R("a0", 0, k)))
+        if first == 1:
+            constants(1)
+        ts(R("vv", 16 * c[1], 16 * c[2]), ind(CT, R("ol", c[1], c[2])), 1.0 / 16, A.add)
+
+        def sc(j):
+            scan(R("rr", 16 * c[j], 16 * c[j + 1]), R("mp", 0, 16 * n[j]), R("vv", 16 * c[j], 16 * c[j + 1]))
+
+        def rp(lo, hi, bank):
+            tt(R("rp", lo, hi), R("rr", 8 * lo + 7, 8 * hi, 8), R(dc, lo, hi), A.max)
+            mm(P(bank, lo, hi), R("dec"), R("rp", lo, hi), False, True)
+        sc(0)
+        sc(1)
+        sc(2)
+        rp(0, la, 3)
+        mm(P(6, 0, nl), R("mi"), R("zer", 0, nl), True, False)
+        mm(P(6, 0, la), R("mi"), R("rr", 7, 8 * la, 8), False, False)
+        sc(3)
+        ts(R("xu", 0, la), P(3, 0, la), cOFF, A.add)
+        rp(la, nl, 4)
+        scan(R("xs", 0, la), R("pat", 0, la), P(3, 0, la))
+        ts(R("xu", la, nl), P(4, la, nl), cOFF, A.add)
+        scan(R("xs", la, nl), R("pat", la, nl), P(4, la, nl))
+        mm(P(6, la, nl), R("mi"), R("rr", 8 * la + 7, 8 * nl, 8), False, False)
+        mm(P(6, 0, nl), R("mu"), R("rp", 0, nl), False, False)
+        mm(P(5, 0, h), R("hb"), R("rp", 0, h), False, False)
+        mm(P(7, h, nl), R("hb"), R("rp", h, nl), False, False)
+        mm(P(6, 0, nl), R("mn"), R("sv", 0, nl), False, True)
+        act(R("yy", 0, nl), P(6, 0, nl), bias=192.0 - 0.28)
+        act(R("zz", 0, nl), R("yy", 0, nl), AF.Relu, bias=-192.0)
+        act(R("ww", 0, nl), R("zz", 0, nl), AF.Relu, bias=16.0, scale=-1.0)
+        at = 0
+        for j in range(k):
+            w = nl - 16 * j
+            ts(R("ee", at, at + w), R("xu", 16 * j, nl), R("xs", 16 * j + 15, 16 * j + 16), A.is_equal,
+               W0 * BASE ** (-16 * j - 15), A.mult)
+            if j < kh:
+                mm(P(5, 16 * j, h), R("bw"), R("ee", at, at + h - 16 * j), False, j == kh - 1)
+                mm(P(7, h, nl), R("bw"), R("ee", at + h - 16 * j, at + w), False, False)
+            else:
+                mm(P(7, 16 * j, nl), R("bw"), R("ee", at, at + w), False, j == k - 1)
+            if j == kh - 1:
+                act(R("sn", 0, h), P(5, 0, h), AF.Sign)
+            at += w
+        act(R("sn", h, nl), P(7, h, nl), AF.Sign)
+        act(R("wn", 0, nl), R("ww", 0, nl), bias=cHOLE, scale=-1.0)
+        if first == 1:
+            constants(2)
+        X = R("xs", 15, nl, 16)
+        tt(R("d1", 64, 64 + 4 * k, 4), P(0, 0, k), CC(k), A.subtract)
+        tt(R("d1", 65, 64 + 4 * k, 4), X, CC(k), A.subtract)
+        tt(R("d0", 65, 64 + 4 * k, 4), X, CC(k), A.is_equal)
+        tt(R("d1", 0, 4 * k, 4), X, R("d1", 3, 4 * k, 4), A.subtract)
+        ts(R("d0", 66, 64 + 4 * k, 4), X, IDO + DS - 0.5, A.is_gt)
+        scan(R("ls", 0, h), R("pat2", 0, h), R("sn", 0, h))
+        scan(R("ls", h, nl), R("pat2", h, nl), R("sn", h, nl))
+        ts(R("d0", 3, 4 * k, 4), R("ls", 15, nl, 16), cOFF2, A.is_lt)
+        ts(R("d0", 67, 64 + 4 * k, 4), R("ls", 15, nl, 16), cOFF2, A.is_lt)
+        scan(R("fo"), R("d0"), R("d1"), 0.0, A.mult, A.add)
+        ts(R("tn"), R("fo", 3, 128, 4), float(IDO), A.subtract)
+
+    def scatter(nl, dc):
+        tt(ind(CT, R("tn", 0, nl // 16)), R(dc, 0, nl), R("wn", 0, nl), A.add)
+
+    def exchange(x, nx):
+        stg, land = "stg%d" % x, "land%d" % x
+        b = W - DS
+        SI, EX, GG = R("ct", 0, DS), R("ct", b, W), R("gg", OWN, L)
+        mm(P(7, 0, DS), R("r3"), SI, True, True)
+        mm(P(2, 0, DS), R("r3"), EX, True, True)
+        act(R(stg, 1, 64, 2), R("ct", b + 2 * S, b + 3 * S), bias=1.0 / 16)
+        act(R(stg, 65, 128, 2), R("ct", b + S, b + 2 * S), bias=1.0 / 16)
+        ts(R(stg, 129, 192, 2), R("ct", b, b + S), 1.0 / 16, A.add)
+        cp(CC(16), NEXT)
+        ts(R(stg, 0, 192, 2), P(7, 0, DS), 0.0, A.is_gt)
+        peers = [T.cores[(rank + d) % 4] for d in range(1, 4)]
+        masks, used = {}, []
+        for j in sorted(range(3), key=lambda j: len(topo.engines(core, peers[j]))):
+            es = [e for e in topo.engines(core, peers[j]) if e not in used][:ENG]
+            used += es
+            masks[j] = sum(1 << e for e in es)
+
+        def send():
+            tr = []
+            for j in range(3):
+                rid, pid = topo.addr(peers[j], core)
+                tr.append(RemoteDMATransfer(dst_ids=[DstId(rid=rid, pnc=pid)], dma_engine_mask=masks[j], remote_sem=T.sem["arr%d" % x],
+                                            src=ap(R(stg, 64 * j, 64 * j + 64)), dst=ap(R(land, 64 * j, 64 * j + 64))))
+            return g.remote_dma_fused(tr, local_sem=T.sem["snt%d" % x])
+        add("g", send, [R(stg)], [], kind="r")
+        act(R("gt"), P(7, 0, DS), bias=128.0, scale=-65536.0)
+        ts(R("te"), P(2, 0, DS), 0.0, A.is_equal)
+        ts(R("x2"), EX, -1.0, A.mult, cHR, A.add)
+        tt(R("x5"), R("agt", b, W), GG, A.subtract)
+        tt(R("te2"), R("te"), R("ecol"), A.mult)
+        tt(R("dif"), R("te"), R("x2"), A.mult)
+        tt(R("x5"), R("x5"), R("te"), A.mult)
+        add("v", None, [], [R(land)], kind="w", ext=("arr%d" % x, 3 * ENG))
+        ASK, G6 = R(land, 0, 192, 2), R("d1", 107, 128, 4)
+        tt(R("x6"), ASK, R("x5"), A.mult)
+        tt(R("x3"), ASK, R("te2"), A.mult)
+        tt(GG, GG, R("x6"), A.add)
+        lists(L)
+        scan(R("x4"), R("pat", 0, DS), R("x3"))
+        tt(R("x2"), ASK, R("dif"), A.mult)
+        tt(R("s2", 0, 6), R("x4", 15, DS, 16), G6, A.add)
+        tt(EX, EX, R("x2"), A.add)
+        ts(R("tn", 26, 32), R("s2", 0, 6), cOFF, A.subtract, float(IDO), A.subtract)
+        digits(L, nx)
+        for j in range(3):
+            tt(R("x1", (2 - j) * S, (3 - j) * S), R(land, 64 * j + 1, 64 * j + 64, 2), R("gt", (2 - j) * S, (3 - j) * S), A.max)
+        ts(G6, R("s2", 0, 6), cOFF, A.subtract)
+        tt(SI, SI, R("x1"), A.min)
+
+    digits(OWN, "dc0")
+    args(OWN)
+    lists(OWN)
+    t = 0
+    for rnd in range(ROUNDS):
+        nl = OWN if rnd == 0 else L
+        for st in range(STEPS):
+            dc, nx = "dc%d" % (t % 2), "dc%d" % (1 - t % 2)
+            step(nl, dc, 1 if t == 0 else 2 if st == 0 else 0)
+            if st < STEPS - 1:
+                args(nl)
+                lists(nl)
+                digits(nl, nx)
+                scatter(nl, dc)
+            elif rnd < ROUNDS - 1:
+                args(L)
+                scatter(nl, dc)
+                exchange(rnd, nx)
+            else:
+                scatter(nl, dc)
+            t += 1
+
+    cuts = [0, 320, 800, 1280, 1680, W]
+    for h in range(5):
+        lo, hi = cuts[h], cuts[h + 1]
+        ts(R("tmpw", lo, hi), R("ct", lo, hi), 208.0 - 0.06, A.add)
+        ts(R("tmp2", lo, hi), R("ct", lo, hi), 1.0 / 16, A.add, 0.0, A.max)
+        mm(P(3 + h, 0, hi - lo), R("mi"), R("tmpw", lo, hi), True, False)
+        mm(P(3 + h, 0, hi - lo), R("mf"), R("tmp2", lo, hi), False, True)
+        if h < 4:
+            act(R("outv", lo, hi), P(3 + h, 0, hi - lo), bias=-192.0)
+            store("y", T.yv[:, lo:hi], R("outv", lo, hi))
+    ts(R("s2"), NEXT, float(REST + IDO), A.is_equal, -float(REST + 1), A.mult)
+    ts(R("s3"), NEXT, float(IDO), A.subtract)
+    ts(R("outv", 1680, W), P(7, 0, W - 1680), -192.0, A.add)
+    tt(R("yo"), R("s2"), R("s3"), A.add)
+    store("y", T.yv[:, 1680:W], R("outv", 1680, W))
+    store("y", T.ya[:, :], R("yo"))
+
+    known = {e: 0 for e in Q}
+    prev = {e: 0 for e in Q}
+    done, waits, need, hist = [], [], set(), {}
+    for i, o in enumerate(ops):
+        deps, e = set(), o["e"]
+        for x in o["r"] + o["w"]:
+            wr = x in o["w"]
+            for j, y, jw in hist.get(x[0], []):
+                if x[0].startswith("pb"):
+                    if ops[j]["e"] != e or ((wr or jw) and overlap(x, y) and not o["acc"]):
+                        deps.add(j)
+                elif (wr or jw) and overlap(x, y):
+                    deps.add(j)
+        waits.append([])
+        for j in sorted(deps, reverse=True):
+            if ops[j]["k"] not in "rw" and not known[e] >> j & 1:
+                waits[i].append(j)
+                need.add(j)
+                known[e] |= done[j]
+        if o["k"] == "c":
+            prev[e] |= 1 << i
+        done.append(known[e] | (prev[e] if o["k"] == "c" else 1 << i))
+        for x in o["r"]:
+            hist.setdefault(x[0], []).append((i, x, False))
+        for x in o["w"]:
+            hist.setdefault(x[0], []).append((i, x, True))
+    tok, cnt, nxt = {}, {}, {e: 0 for e in POOL}
+    for i, o in enumerate(ops):
+        q = Q[o["e"]]
+        for j in waits[i]:
+            q.wait_ge(T.sem[tok[j][0]], tok[j][1])
+        if o["k"] == "w":
+            q.wait_ge(T.sem[o["ext"][0]], o["ext"][1])
+            continue
+        ins = o["fn"]()
+        if o["k"] == "d" or i in need:
+            e, by = ("d", 16) if o["k"] == "d" else (o["e"], 1)
+            s = "%s%d" % (e, nxt[e] % POOL[e])
+            nxt[e] += 1
+            cnt[s] = cnt.get(s, 0) + by
+            ins.then_inc(T.sem[s], by)
+            tok[i] = (s, cnt[s])
+    for i, o in enumerate(ops):
+        if o["k"] == "d" and i not in need:
+            g.sync.wait_ge(T.sem[tok[i][0]], 16)
+    for x in range(ROUNDS - 1):
+        g.wait_ge(T.sem["snt%d" % x], 3 * ENG)

@@ -5,27 +5,31 @@ W, OWN, S, D, STEPS, ROUNDS = 1920, 160, 32, 3, 3, 3
 DS = S * D
 L = OWN + DS
 REST = W
-IDO = 2048
-CTW = 2192
+C0 = 256
+CTW = C0 + W + 16
+V0 = 1158.0
+U = 1.0 / 1024
 BASE, THR0, W0 = 256.0 / 150.0, 2.56, 1.0e25
-STEP = 8192.0
-SPLIT = {80: (20, 26, 18, 16), 128: (40, 42, 22, 24)}
+HUGE = 1.0e29
+FIX, PEF = 50, 0.5
+WAKE, SAME = 160, 120
 ENG = 4
+PIECES = {OWN: ((80, 128, None), (32, 80, None), (0, 32, None)), L: ((128, 200, None), (48, 128, None), (0, 48, None))}
+SCUT = {OWN: 64, L: 128}
 
-F, H, B, I, U = "float32", "float16", "bfloat16", "int32", "uint16"
+F, H, B, I, U16 = "float32", "float16", "bfloat16", "int32", "uint16"
 SB = {}
 for _t, _l in ((I, "agt 1936 rin 16 pc 8 pc2 8 m1 128 m2 128"),
-               (U, "tn 32 a0 16 ol 128 xu 256"),
-               (H, "bl 152 bh 152 zx 152 gg 256 x5 96 x6 96"),
-               (F, "col 48 oh 16 df 4 hs 4 k16 4 geo 16 pat 256 of 128 xs 256 d0 128 d1 128 fo 128 s1 16 s2 16 s3 16 x4 96 yo 16"),
-               (B, "vin 1920 ct 2192 dt 2048 tmpw 1920 tmp2 1920 outv 1920 i0 256 i1 256 pm 152 gh 128 kb 256 zer 256 uu 256 u1 256 "
-                   "ones 256 zd 152 mi 128 mn 128 mu 128 dec 128 cx 128 bw 128 pq 152 hb 128 r3 128 mf 128 blo 128 bhi 128 dg 256 "
-                   "bm 128 pat2 256 mp 768 thr 256 hr 160 ecol 96 sv 256 sg 256 vv 2048 rr 2048 dc0 256 dc1 256 rp 256 pp 256 "
-                   "ee 2176 sn 256 ls 256 yy 256 zz 256 ww 256 wn 256 stg0 192 stg1 192 land0 192 land1 192 gt 96 te 96 te2 96 "
-                   "x1 96 dif 96 x2 96 x3 96")):
+               (U16, "tn 16 th 16 a0 16 ol 128"),
+               (H, "bl 152 bh 152 zx 152 zd 152 gg 256 mh 128 mn 128 mu 128 dec 128 mp 1024 vv 2048 rr 2048 rp 256 sv 256 pp 256 xu 256 tr 256 "
+                   "t1 1920 stg0 192 stg1 192 land0 192 land1 192 hm 96 x1 96 ta 96 tb 96 te 96 tm 96 x3 96 ecol 96"),
+               (F, "ct %d col 32 oh 16 geo 16 s1 16 s2 16 s3 16 wl0 16 wl 16 pz 16 nl 16 cur 16 yp 16 dy 16 yo 16 of 128 xs 256 ls 256 "
+                   "w2 160 d0 80 f0 32 fo 32 dc0 256 dc1 256 ww 256 hr 160 dif 96 x2 96 x4 96" % CTW),
+               (B, "vin 1920 dt 2048 ya 1920 outv 1920 i0 256 i1 256 pm 152 gh 128 kb 256 zer 256 uu 256 u1 256 ones 480 m10 128 mi 128 mv 128 "
+                   "bw 128 pq 152 blo 128 bhi 128 dg 256 bm 128 pat 256 mk 256 mkx 256 thr0 256 thr 256 sg 256 ee 2176")):
     _w = _l.split()
     for _k in range(0, len(_w), 2):
-        SB[_w[_k]] = (int(_w[_k + 1]), _t)
+        SB["ab" if _w[_k] == "ya" else _w[_k]] = (int(_w[_k + 1]), _t)
 SCRATCH = {k: ("sbuf", [128, v[0]], v[1]) for k, v in SB.items()}
 for _k in range(8):
     SCRATCH["pb%d" % _k] = ("psum", [128, 512], F)
@@ -34,6 +38,7 @@ SEMAPHORES = ["%s%d" % (e, k) for e in POOL for k in range(POOL[e])] + ["arr0", 
 A = AluOpType
 AF = ActivationFunctionType
 ID = AF.Identity
+bL, bLO, bHI, bX, bM, bF0, bF1, bR = range(8)
 
 
 def R(name, lo=0, hi=None, step=1):
@@ -58,6 +63,85 @@ def overlap(a, b):
     return a[3] != b[3] or a[3] == 1 or (a[1] - b[1]) % a[3] == 0
 
 
+def width(x):
+    return 16 * width(x[2]) if x[0] == "ind" else len(range(x[1], x[2], x[3]))
+
+
+def cycles(eng, kind, ins, outs, both):
+    if kind == "d":
+        x = (outs or ins)[0]
+        return 50, 1300 + 0.85 * width(x) * (1 if SB[x[0]][1] == B else 2)
+    if kind != "c":
+        return (300, 2800) if kind == "r" else (0, 0)
+    n = width(outs[0])
+    sides = [x for x in ins + outs if isinstance(x, tuple)]
+    if eng == "g":
+        c = 160 + 2 * n
+    elif outs[0][0] == "ind":
+        c = 60 + 3.8 * n
+    elif any(x[0] == "ind" for x in sides):
+        c = 70 + 1.56 * n
+    elif eng == "p":
+        c = max(64, n) * PEF
+    elif eng != "v":
+        c = max(64, n) + FIX
+    elif both:
+        c = max(64, n if any(x[0][:2] == "pb" for x in sides[:2]) else 2 * n) + FIX
+    else:
+        c = max(64, n if any(x[0][:2] == "pb" or (SB[x[0]][1] in (F, I) and width(x) == n) for x in sides) else n / 2) + FIX
+    return c, c
+
+
+def conflicts(ops):
+    hist, out = {}, []
+    for i, o in enumerate(ops):
+        deps, e = {}, o["e"]
+        for x in o["r"] + o["w"]:
+            wr = x in o["w"]
+            for j, y, jw in hist.get(x[0], []):
+                if x[0].startswith("pb"):
+                    sem = ops[j]["e"] != e or ((wr or jw) and overlap(x, y) and not o["acc"])
+                    deps[j] = deps.get(j, False) or sem
+                elif (wr or jw) and overlap(x, y):
+                    deps[j] = True
+        out.append(deps)
+        for x in o["r"]:
+            hist.setdefault(x[0], []).append((i, x, False))
+        for x in o["w"]:
+            hist.setdefault(x[0], []).append((i, x, True))
+    return out
+
+
+def arrange(ops):
+    deps = conflicts(ops)
+    for i, o in enumerate(ops):
+        if o["k"] == "w":
+            deps[i][max(j for j in range(i) if ops[j]["k"] == "r")] = True
+        if o["k"] == "d" and o["w"]:
+            deps[i].update({j: False for j in range(i) if ops[j]["k"] == "d"})
+
+    def lag(j, i):
+        if ops[i]["k"] == "d" and ops[j]["k"] == "d":
+            return ops[j]["c"][1] - 1300
+        return ops[j]["c"][1] + (0 if not deps[i][j] else SAME if ops[i]["e"] == ops[j]["e"] else WAKE)
+    rest = [o["c"][1] for o in ops]
+    for i in range(len(ops) - 1, -1, -1):
+        for j in deps[i]:
+            rest[j] = max(rest[j], lag(j, i) + rest[i])
+    start, busy = {}, {}
+    for i in sorted(range(len(ops)), key=lambda i: (-rest[i], i)):
+        t, c = max([start[j] + lag(j, i) for j in deps[i]] + [0]), ops[i]["c"][0]
+        q = busy.setdefault(ops[i]["e"], [])
+        at = 0
+        for at in range(len(q) + 1):
+            if at == len(q) or t + c <= q[at][0]:
+                break
+            t = max(t, q[at][1])
+        q.insert(at, (t, t + c))
+        start[i] = t
+    return [ops[i] for i in sorted(range(len(ops)), key=lambda i: (start[i], i))]
+
+
 def rank_program(g, core, T, topo):
     rank = T.rank_of(core)
     if rank is None:
@@ -73,12 +157,12 @@ def rank_program(g, core, T, topo):
             return T[x[0]][:, x[1]:x[2]:x[3]] if x[3] > 1 else T[x[0]][:, x[1]:x[2]]
         return x
 
-    def add(eng, fn, ins, outs, kind="c", acc=False, ext=None):
+    def add(eng, fn, ins, outs, kind="c", acc=False, ext=None, both=False):
         rd = [x[2] for x in outs if x[0] == "ind"]
         for x in ins:
             if isinstance(x, tuple):
                 rd += [x[1], x[2]] if x[0] == "ind" else [x]
-        ops.append({"e": eng, "fn": fn, "r": rd, "w": [x[1] if x[0] == "ind" else x for x in outs], "k": kind, "acc": acc, "ext": ext})
+        ops.append({"e": eng, "fn": fn, "c": cycles(eng, kind, ins, outs, both), "r": rd, "w": [x[1] if x[0] == "ind" else x for x in outs], "k": kind, "acc": acc, "ext": ext})
 
     def ts(out, in0, s1, op0, s2=None, op1=None):
         if op1 is None:
@@ -87,7 +171,7 @@ def rank_program(g, core, T, topo):
             add("v", lambda: V.tensor_scalar(ap(out), ap(in0), ap(s1), ap(s2), op0, op1), [in0, s1, s2], [out])
 
     def tt(out, a, b, op):
-        add("v", lambda: V.tensor_tensor(ap(out), ap(a), ap(b), op), [a, b], [out])
+        add("v", lambda: V.tensor_tensor(ap(out), ap(a), ap(b), op), [a, b], [out], both=True)
 
     def cp(out, a):
         add("v", lambda: V.tensor_copy(ap(out), ap(a)), [a], [out])
@@ -123,242 +207,268 @@ def rank_program(g, core, T, topo):
     load("s", R("rin", 0, 10), T.rts[:, :])
     load("y", R("agt", 0, W), T.ag[:, :])
 
-    cR, cG, cLO, cHI, cW, cW2, cHB, cOFF, cOFF2, cHOLE, cHR, cG2, cG21, cU8, cMF, cM0, cG16 = [C(k) for k in range(17)]
+    cR, cG, cLO, cHI, cW, cW2, cHB, cHR, cG2, cG21, cG16, cU, cR16, cT = [C(k) for k in range(14)]
     cA = 20
-    CT, AG = R("ct"), R("agt")
+    CT, CELLS, AG, DT = R("ct"), R("ct", C0, CTW), R("agt"), R("dt")
+    ZR = (REST + C0) / 16.0
 
     def OH(j):
         return R("oh", j, j + 1)
+
+    def slot(k, lo=0, hi=16):
+        return R("w2", 10 * lo + k, 10 * hi, 10)
+    XV, Y = slot(4), slot(5)
     iota(R("pc", 0, 1), [[0, 1]], 0, 1)
     iota(R("i0"), [[0, 16], [1, 16]], 0, 0)
     iota(R("i1"), [[1, 16], [0, 16]], 0, 0)
     iota(R("pm"), [[1, 152]], -15, -1)
     iota(R("gh"), [[1, 16], [0, 8]], 0, 0)
     iota(R("pq"), [[1, 152]], -15, 0)
-    iota(R("d1", 3, 64, 4), [[16, 16]], W + 1 + IDO, 0)
-    iota(R("ecol"), [[1, DS]], -DS, 0)
-    ms(R("mp"), 1.0 / 16)
+    iota(R("ecol"), [[-1, DS]], DS, 0)
     ts(R("pc2", 0, 1), R("pc", 0, 1), 15, A.bitwise_and)
     ts(R("pc2", 1, 2), R("pc", 0, 1), 4, A.logical_shift_right)
-    ms(R("agt", W, 1936), REST)
+    ms(R("ones"), 1.0)
     cp(R("col", 0, 2), R("pc2", 0, 2))
-    ms(R("mp", 0, 768, 8), -64.0)
-    ms(R("ct", W, CTW), 0.0)
-    ms(R("tn", 26, 32), REST)
+    ms(R("m10"), -10.0)
+    ms(R("agt", W, 1936), REST)
+    ms(R("mp"), 1.0 / 16)
     ts(R("oh"), R("i0", 0, 16), cR, A.is_equal)
-    ms(R("d0"), 0.0)
-    ts(R("uu"), R("i0"), OH(0), A.mult, 1.0 / 256, A.mult)
-    ts(R("col", cA, cA + 8), R("i0", 8, 16), OH(2), A.mult, 1.0 / 256, A.mult)
-    ts(cHOLE, OH(3), 1.0 / 256, A.mult)
-    tt(R("df"), R("oh", 0, 4), R("oh", 4, 8), A.subtract)
-    ts(R("u1"), R("i1"), OH(1), A.mult, 1.0 / 256, A.mult)
-    fill(R("ones"), R("i0"), 1.0)
-    fill(R("zer"), R("i0"), 0.0)
-    fill(R("kb"), R("i0"), 1.0 / BASE)
-    fill(R("k16"), R("i0", 0, 4), 1.0 / 16)
-    fill(R("geo"), R("i0", 0, 16), BASE)
+    ms(R("mp", 0, 1024, 8), -4096.0)
+    ts(R("uu"), R("i0"), OH(0), A.mult, U, A.mult)
+    ts(R("col", cA, cA + 8), R("i0", 1, 9), OH(2), A.mult, U, A.mult)
+    ts(R("u1"), R("i1"), OH(1), A.mult, U, A.mult)
+    ts(R("col", cA, cA + 8), R("col", cA, cA + 8), -1.0 / 32, A.add)
+    tt(R("uu"), R("uu"), R("u1"), A.add)
+    ts(R("mi"), R("pm", 15, 143), 0.0, A.is_equal)
+    fill(R("ct", 0, C0), R("i0"), 0.0)
+    fill(R("ct", C0 + W, CTW), R("i0", 0, 16), 0.0)
+    act(cHB, OH(3), scale=8 * U, bias=5.0 / 128)
     act(cG2, cG, scale=2.0)
     act(cG21, cG, scale=2.0, bias=1.0)
     act(cG16, cG, scale=16.0)
-    ts(cLO, cR, 7.5, A.is_lt)
-    tt(R("uu"), R("uu"), R("u1"), A.add)
-    ts(R("mi"), R("pm", 15, 143), 0.0, A.is_equal)
-    for a in (7, 0, 1, 2, 3, 4, 5, 6):
-        if a in (4, 6):
+    act(cR16, cR, scale=1.0 / 16)
+    act(R("mv"), R("mi"), scale=-1280.0)
+    for a in range(8):
+        if a in (5, 6):
             act(R("dt", 256 * a, 256 * a + 256), R("uu"), bias=C(cA + a))
         else:
             ts(R("dt", 256 * a, 256 * a + 256), R("uu"), C(cA + a), A.add)
-    tt(cHR, R("dt", REST, REST + 1), cHOLE, A.add)
-    ts(cHI, cR, 7.5, A.is_gt)
     for h in range(4):
-        mm(P(3 + h, 0, 480), R("mi"), R("dt", 480 * h, 480 * h + 480), True, False)
-    act(R("hr"), R("zer", 0, 160), bias=cHR)
-    act(R("ct", REST, REST + 1), cHR)
+        mm(P(3 + h, 0, 480), R("m10"), R("ones"), True, False)
+        mm(P(3 + h, 0, 480), R("mi"), R("dt", 480 * h, 480 * h + 480), False, False)
+    ts(cLO, cR, 7.5, A.is_lt)
+    ts(cHI, cR, 7.5, A.is_gt)
+    tt(cHR, R("dt", REST, REST + 1), cHB, A.add)
     ts(R("zx"), R("pm"), 0.0, A.is_equal, OH(0), A.mult)
-    ts(R("bl"), R("pm"), 0.0, A.is_equal, cLO, A.mult)
-    ts(R("bh"), R("pm"), 0.0, A.is_equal, cHI, A.mult)
-    scan(R("hs"), R("k16"), R("df"), 0.0, A.mult, A.add)
-    scan(R("s1"), R("geo"), R("oh"), 0.0, A.mult, A.add)
-    ts(R("blo"), R("gh"), cG2, A.is_equal, 2048.0, A.mult)
-    ts(R("bhi"), R("gh"), cG21, A.is_equal, 2048.0, A.mult)
-    ts(R("bm"), R("i1", 0, 128), cG, A.is_equal)
-    ts(R("dg"), R("i0"), cR, A.is_equal)
-    act(cW, R("hs", 3, 4), scale=2.0 ** 20)
-    act(cW2, R("hs", 2, 3), scale=2.0 ** 16)
-    act(cHB, R("df", 3, 4), scale=2.0 ** 96)
-    act(cOFF, cR, scale=-STEP, bias=15 * STEP)
-    act(cOFF2, cR, scale=-4.0, bias=60.0)
-    scan(R("thr"), R("kb"), R("zer"), -THR0 * W0 * BASE, A.mult, A.add)
-    cp(R("tn", 16, 26), R("rin", 0, 10))
+    ms(R("tn", 10, 16), REST)
+    cp(R("tn", 0, 10), R("rin", 0, 10))
 
     for h in range(4):
         lo, hi = 480 * h, 480 * h + 480
-        ts(R("tmpw", lo, hi), R("vin", lo, hi), 0.0, A.is_lt, 17.0, A.mult)
-        mm(P(3 + h, 0, 480), R("mi"), R("vin", lo, hi), False, False)
-        mm(P(3 + h, 0, 480), R("mi"), R("tmpw", lo, hi), False, True)
-        if h % 2 == 0:
-            act(R("ct", lo, hi), P(3 + h, 0, 480), bias=-16.0)
-    ts(R("ct", 480, 960), P(4, 0, 480), -16.0, A.add)
-    ts(R("zd"), R("pq"), cG16, A.is_equal, cW2, A.mult)
-    ts(R("ct", 1440, W), P(6, 0, 480), -16.0, A.add)
-    cp(ind(CT, R("tn", 16, 26)), R("hr"))
-    act(R("dec"), R("bm"), scale=cW)
-    act(R("cx"), R("i0", 0, 128), bias=-15.0 * 64, scale=64.0)
-    act(R("pat"), R("dg"), bias=STEP, scale=-(2.0 ** 20 + STEP))
-    fill(R("d1", 64, 128), R("i0", 0, 64), float(REST + IDO))
-    ts(R("d1", 67, 104, 4), R("rin", 0, 10), float(IDO), A.add)
+        act(R("t1", lo, hi), R("vin", lo, hi), scale=4.0, bias=-V0)
+        mm(P(3 + h, 0, 480), R("mv"), R("vin", lo, hi), False, True)
+        tt(R("ct", C0 + lo, C0 + hi), P(3 + h, 0, 480), R("t1", lo, hi), A.max)
+    fill(R("hr"), R("i0", 0, 160), cHR)
+    act(R("ct", C0 + REST, C0 + REST + 1), cHR)
+    cp(ind(CELLS, R("tn", 0, 10)), R("hr"))
+    ts(R("bl"), R("pm"), 0.0, A.is_equal, cLO, A.mult)
+    ts(R("bh"), R("pm"), 0.0, A.is_equal, cHI, A.mult)
+    ts(R("blo"), R("gh"), cG2, A.is_equal, 4096.0, A.mult)
+    ts(R("bhi"), R("gh"), cG21, A.is_equal, 4096.0, A.mult)
 
     def constants(part):
         if part == 0:
-            act(R("hb"), R("bm"), scale=cHB)
-            act(cU8, OH(8), scale=1024.0)
-            act(R("mn"), R("mi"), scale=-1.0)
-            act(R("mu"), R("bm"), scale=cU8)
+            act(cW2, OH(0), scale=64.0)
+            act(cT, OH(1), scale=1024.0, bias=cW2)
+            act(cW2, OH(2), scale=16384.0, bias=cT)
+            act(cT, OH(4), scale=-17472.0, bias=cW2)
+            act(cW2, cT)
+            act(cW, OH(3), scale=-32768.0, bias=cT)
+            act(cT, OH(4), scale=32768.0, bias=cW)
+            act(cW, cT)
+            act(cU, OH(4), scale=8192.0)
+            fill(R("kb"), R("i0"), 1.0 / BASE)
+            fill(R("zer"), R("i0"), 0.0)
+            fill(R("geo"), R("i0", 0, 16), BASE)
+            fill(R("s2"), R("i0", 0, 16), BASE ** -16)
+            fill(R("pat"), R("i0"), 0.0)
+            fill(R("pat", 0, 256, 16), R("i0", 0, 16), -2 * HUGE)
         elif part == 1:
+            ts(R("bm"), R("i1", 0, 128), cG, A.is_equal)
+            ts(R("dg"), R("i0"), cR, A.is_equal)
+            ts(R("zd"), R("pq"), cG16, A.is_equal, cW2, A.mult)
+            scan(R("thr0"), R("kb"), R("zer"), -THR0 * W0 * BASE, A.mult, A.add)
+            scan(R("s1"), R("geo"), R("oh"), 0.0, A.mult, A.add)
+            scan(R("wl0"), R("s2"), R("zer", 0, 16), W0 * BASE, A.mult, A.add)
+            ms(R("w2"), 0.0)
+            ms(R("d0"), 0.0)
+        elif part == 2:
+            act(R("mk"), R("dg"), scale=HUGE, bias=-HUGE)
+            act(R("mkx"), R("mk"), bias=-64.0)
+            act(R("dec"), R("bm"), scale=cW)
             act(R("bw"), R("bm"), scale=R("s1", 15, 16))
-            act(R("pat2"), R("dg"), bias=4.0, scale=-1028.0)
-            fill(R("d1", 2, 128, 4), R("i0", 0, 32), 0.0)
-            fill(R("d1", 1, 64, 4), R("i0", 0, 16), 0.0)
-            fill(R("d1", 0, 64, 4), R("i0", 0, 16), 0.0)
-            fill(R("d0", 1, 64, 4), R("i0", 0, 16), 1.0)
-            fill(R("d0", 2, 64, 4), R("i0", 0, 16), 1.0)
-            act(R("d1", 3, 64, 4), R("d1", 3, 64, 4), bias=cR)
-        else:
-            act(cM0, OH(8), scale=-16.0)
-            act(R("r3"), R("bm"), scale=OH(3))
-            act(cMF, OH(3), scale=-256.0, bias=cM0)
-            act(R("mf"), R("bm"), scale=cMF)
-
-    def CC(k):
-        return R("d1", 67, 64 + 4 * k, 4)
-    NEXT = R("fo", 67, 128, 4)
+            mm(P(bR, 0, 256), R("mi"), R("thr0"), True, False)
+            mm(P(bR, 0, 256), R("mi"), R("mk"), False, True)
+            act(R("mn"), R("mi"), scale=-1.0)
+            act(R("thr"), P(bR, 0, 256))
+        elif part == 3:
+            ts(R("mh"), R("mi"), 1.0, A.mult)
+            ts(R("mu"), R("bm"), cU, A.mult)
+            ts(slot(8), R("i0", 0, 16), cR16, A.add)
+            ms(R("f0"), 0.0)
+            ms(R("pz"), 64.0)
+            cp(R("wl"), R("wl0"))
+            ms(R("cur"), ZR)
+            ts(R("cur", 0, 10), R("rin", 0, 10), 1.0 / 16, A.mult, C0 / 16.0, A.add)
+            cp(R("yp"), R("cur"))
+            cp(Y, R("cur"))
 
     def args(nl):
-        act(R("gg", 0, nl), ind(AG, R("tn", 16, 16 + nl // 16)))
+        act(R("gg", 0, nl), ind(AG, R("tn", 0, nl // 16)))
 
     def digits(nl, dc):
-        act(R(dc, 0, nl), ind(R("dt"), R("tn", 16, 16 + nl // 16)))
+        act(R(dc, 0, nl), ind(DT, R("tn", 0, nl // 16)), bias=cHB)
 
     def lists(nl):
         k, m = nl // 16, nl // 2
         for r in range(16):
-            mm(P(0, 0, k), R("zx", 15 - r, 143 - r), R("gg", r, nl, 16), r == 0, r == 15)
-        mm(P(2, 0, m), R("bh", 23, 151), R("gg", 0, nl, 2), True, False)
-        mm(P(2, 0, m), R("bh", 15, 143), R("gg", 1, nl, 2), False, True)
-        mm(P(1, 0, m), R("bl", 15, 143), R("gg", 0, nl, 2), True, False)
-        mm(P(1, 0, m), R("bl", 7, 135), R("gg", 1, nl, 2), False, False)
+            mm(P(bL, 0, k), R("zx", 15 - r, 143 - r), R("gg", r, nl, 16), r == 0, r == 15)
+        mm(P(bHI, 0, m), R("bh", 23, 151), R("gg", 0, nl, 2), True, False)
+        mm(P(bHI, 0, m), R("bh", 15, 143), R("gg", 1, nl, 2), False, True)
+        mm(P(bLO, 0, m), R("bl", 15, 143), R("gg", 0, nl, 2), True, False)
+        mm(P(bLO, 0, m), R("bl", 7, 135), R("gg", 1, nl, 2), False, False)
 
-    def step(nl, dc, first):
-        k, m = nl // 16, nl // 2
-        hk = 2 * (k // 4)
-        hl, hm = 16 * hk, 8 * hk
-        kh = k // 2
-        h = 16 * kh
-        n = SPLIT[m]
-        c = [0, n[0], n[0] + n[1], n[0] + n[1] + n[2], m]
-        la = 2 * c[3]
-        cp(R("a0", 0, k), P(0, 0, k))
-        act(R("sg", 0, hl), ind(CT, R("a0", 0, hk)), AF.Sign, bias=8.5)
-        ts(R("sg", hl, nl), ind(CT, R("a0", hk, k)), -8.5, A.is_gt, 2.0, A.mult)
-        act(R("of", 0, hm), P(2, 0, hm), bias=2048.0)
-        act(R("of", hm, m), P(2, hm, m), bias=17 * 2048.0)
-        mm(P(1, 0, m), R("blo"), R("sg", 0, nl, 2), False, False)
-        mm(P(1, 0, m), R("bhi"), R("sg", 1, nl, 2), False, True)
-        act(R("pp", 0, nl), ind(CT, R("tn", 16, 16 + k)))
-        if not first:
-            cp(CC(16), NEXT)
-        halves = [(0, m // 2), (m // 2, m)]
+    def state():
+        tt(R("dy"), Y, R("yp"), A.subtract)
+        tt(R("wl"), R("wl0"), R("nl"), A.mult)
+        tt(R("dy"), R("dy"), R("nl"), A.mult)
+        act(R("pz"), R("nl"), scale=1024.0, bias=-960.0)
+        tt(R("cur"), R("yp"), R("dy"), A.add)
+        cp(R("yp"), Y)
+
+    def choose(nl, t, between):
+        k, m, sc = nl // 16, nl // 2, SCUT[nl]
+        cp(R("a0", 0, k), P(bL, 0, k))
+        act(R("sv", 0, sc), ind(CELLS, R("a0", 0, sc // 16)))
+        cp(R("sv", sc, nl), ind(CELLS, R("a0", sc // 16, k)))
+        act(R("of", 0, m), P(bHI, 0, m), bias=17 * 2048.0)
+        ts(R("sg", 0, nl), R("sv", 0, nl), 30.0 - V0, A.is_gt)
+        mm(P(bLO, 0, m), R("blo"), R("sg", 0, nl, 2), False, False)
+        mm(P(bLO, 0, m), R("bhi"), R("sg", 1, nl, 2), False, True)
+        between()
+        act(R("pp", 0, nl), ind(CELLS, R("tn", 0, k)))
+        halves = [(m // 2, m), (0, m // 2)]
         for lo, hi in halves:
-            tt(R("m1", lo, hi), P(1, lo, hi), R("of", lo, hi), A.max)
+            tt(R("m1", lo, hi), P(bLO, lo, hi), R("of", lo, hi), A.max)
         for lo, hi in halves:
             ts(R("m2", lo, hi), R("m1", lo, hi), 2047, A.bitwise_and)
         for lo, hi in halves:
             cp(R("ol", lo, hi), R("m2", lo, hi))
-        mm(P(3, 0, la), R("cx"), R("ones", 0, la), True, False)
-        mm(P(4, la, nl), R("cx"), R("ones", la, nl), True, False)
-        mm(P(5, 0, h), R("mi"), R("thr", 0, h), True, False)
-        mm(P(7, h, nl), R("mi"), R("thr", h, nl), True, False)
-        for r in range(16):
-            mm(P(0, 0, k), R("zd", 15 - r, 143 - r), R("pp", r, nl, 16), r == 0, r == 15)
-        for j in (0, 2, 3):
-            act(R("vv", 16 * c[j], 16 * c[j + 1]), ind(CT, R("ol", c[j], c[j + 1])), bias=1.0 / 16)
-        if first == 1:
-            constants(0)
-        act(R("sv", 0, nl), ind(CT, R("a0", 0, k)))
-        if first == 1:
-            constants(1)
-        ts(R("vv", 16 * c[1], 16 * c[2]), ind(CT, R("ol", c[1], c[2])), 1.0 / 16, A.add)
 
-        def sc(j):
-            scan(R("rr", 16 * c[j], 16 * c[j + 1]), R("mp", 0, 16 * n[j]), R("vv", 16 * c[j], 16 * c[j + 1]))
-
-        def rp(lo, hi, bank):
-            tt(R("rp", lo, hi), R("rr", 8 * lo + 7, 8 * hi, 8), R(dc, lo, hi), A.max)
-            mm(P(bank, lo, hi), R("dec"), R("rp", lo, hi), False, True)
-        sc(0)
-        sc(1)
-        sc(2)
-        rp(0, la, 3)
-        mm(P(6, 0, nl), R("mi"), R("zer", 0, nl), True, False)
-        mm(P(6, 0, la), R("mi"), R("rr", 7, 8 * la, 8), False, False)
-        sc(3)
-        ts(R("xu", 0, la), P(3, 0, la), cOFF, A.add)
-        rp(la, nl, 4)
-        scan(R("xs", 0, la), R("pat", 0, la), P(3, 0, la))
-        ts(R("xu", la, nl), P(4, la, nl), cOFF, A.add)
-        scan(R("xs", la, nl), R("pat", la, nl), P(4, la, nl))
-        mm(P(6, la, nl), R("mi"), R("rr", 8 * la + 7, 8 * nl, 8), False, False)
-        mm(P(6, 0, nl), R("mu"), R("rp", 0, nl), False, False)
-        mm(P(5, 0, h), R("hb"), R("rp", 0, h), False, False)
-        mm(P(7, h, nl), R("hb"), R("rp", h, nl), False, False)
-        mm(P(6, 0, nl), R("mn"), R("sv", 0, nl), False, True)
-        act(R("yy", 0, nl), P(6, 0, nl), bias=192.0 - 0.28)
-        act(R("zz", 0, nl), R("yy", 0, nl), AF.Relu, bias=-192.0)
-        act(R("ww", 0, nl), R("zz", 0, nl), AF.Relu, bias=16.0, scale=-1.0)
-        at = 0
-        for j in range(k):
-            w = nl - 16 * j
-            ts(R("ee", at, at + w), R("xu", 16 * j, nl), R("xs", 16 * j + 15, 16 * j + 16), A.is_equal,
-               W0 * BASE ** (-16 * j - 15), A.mult)
-            if j < kh:
-                mm(P(5, 16 * j, h), R("bw"), R("ee", at, at + h - 16 * j), False, j == kh - 1)
-                mm(P(7, h, nl), R("bw"), R("ee", at + h - 16 * j, at + w), False, False)
-            else:
-                mm(P(7, 16 * j, nl), R("bw"), R("ee", at, at + w), False, j == k - 1)
-            if j == kh - 1:
-                act(R("sn", 0, h), P(5, 0, h), AF.Sign)
-            at += w
-        act(R("sn", h, nl), P(7, h, nl), AF.Sign)
-        act(R("wn", 0, nl), R("ww", 0, nl), bias=cHOLE, scale=-1.0)
-        if first == 1:
+    def step(nl, t, last):
+        k = nl // 16
+        h = 16 * (k // 2)
+        if t == 0:
             constants(2)
-        X = R("xs", 15, nl, 16)
-        tt(R("d1", 64, 64 + 4 * k, 4), P(0, 0, k), CC(k), A.subtract)
-        tt(R("d1", 65, 64 + 4 * k, 4), X, CC(k), A.subtract)
-        tt(R("d0", 65, 64 + 4 * k, 4), X, CC(k), A.is_equal)
-        tt(R("d1", 0, 4 * k, 4), X, R("d1", 3, 4 * k, 4), A.subtract)
-        ts(R("d0", 66, 64 + 4 * k, 4), X, IDO + DS - 0.5, A.is_gt)
-        scan(R("ls", 0, h), R("pat2", 0, h), R("sn", 0, h))
-        scan(R("ls", h, nl), R("pat2", h, nl), R("sn", h, nl))
-        ts(R("d0", 3, 4 * k, 4), R("ls", 15, nl, 16), cOFF2, A.is_lt)
-        ts(R("d0", 67, 64 + 4 * k, 4), R("ls", 15, nl, 16), cOFF2, A.is_lt)
-        scan(R("fo"), R("d0"), R("d1"), 0.0, A.mult, A.add)
-        ts(R("tn"), R("fo", 3, 128, 4), float(IDO), A.subtract)
+        mm(P(bF0, 0, h), R("mi"), R("thr", 0, h), True, False)
+        mm(P(bF1, h, nl), R("mi"), R("thr", h, nl), True, False)
+        mm(P(bR, 0, nl), R("mn"), R("sv", 0, nl), True, False)
+        for r in range(16):
+            mm(P(bL, 16, 16 + k), R("zd", 15 - r, 143 - r), R("pp", r, nl, 16), r == 0, r == 15)
 
-    def scatter(nl, dc):
-        tt(ind(CT, R("tn", 0, nl // 16)), R(dc, 0, nl), R("wn", 0, nl), A.add)
+        def gather(e, lo, hi):
+            if lo < hi:
+                (act if e == "s" else cp)(R("vv", 8 * lo, 8 * hi), ind(CELLS, R("ol", lo // 2, hi // 2)))
 
-    def exchange(x, nx):
+        def sc(lo, hi):
+            if lo < hi:
+                scan(R("rr", 8 * lo, 8 * hi), R("mp", 0, 8 * (hi - lo)), R("vv", 8 * lo, 8 * hi))
+
+        def decode(lo, hi):
+            ts(R("rp", lo, hi), R("rr", 8 * lo + 7, 8 * hi, 8), -0.25, A.max)
+            mm(P(bM, lo, hi), R("mi"), R("mkx", lo, hi), True, False)
+            mm(P(bM, lo, hi), R("dec"), R("rp", lo, hi), False, True)
+            mm(P(bX, lo, hi), R("dec"), R("rp", lo, hi), True, True)
+            scan(R("xs", lo, hi), R("pat", lo, hi), P(bM, lo, hi))
+
+        at = [0]
+
+        def compare(j):
+            w, a = nl - 16 * j, at[0]
+            ts(R("ee", a, a + w), R("xu", 16 * j, nl), R("xs", 16 * j + 15, 16 * j + 16), A.is_equal, R("wl", j, j + 1), A.mult)
+            if 16 * j < h:
+                mm(P(bF1, h, nl), R("bw"), R("ee", a + h - 16 * j, a + w), False, j == 0)
+                mm(P(bF0, 16 * j, h), R("bw"), R("ee", a, a + h - 16 * j), False, j == 0)
+            else:
+                mm(P(bF1, 16 * j, nl), R("bw"), R("ee", a, a + w), False, False)
+            at[0] += w
+
+        def results(lo, hi, stop):
+            mm(P(bR, lo, hi), R("mh"), R("rr", 8 * lo + 7, 8 * hi, 8), False, False)
+            mm(P(bR, lo, hi), R("mu"), R("rp", lo, hi), False, stop)
+        ps = PIECES[nl]
+        tops = [nl] + [p[0] for p in ps]
+        gather("s", ps[0][0], ps[0][1])
+        gather("v", ps[0][1], nl)
+        if t == 0:
+            constants(3)
+        sc(ps[0][1], nl)
+        for i, (lo, vcut, _) in enumerate(ps):
+            hi = tops[i]
+            if i + 1 < len(ps):
+                gather("s", ps[i + 1][0], ps[i + 1][1])
+            sc(lo, vcut)
+            decode(lo, hi)
+            act(R("xu", lo, hi), P(bX, lo, hi), bias=-64.0)
+            if i == 0:
+                tt(slot(0, 0, k), P(bL, 16, 16 + k), R("yp", 0, k), A.subtract)
+                tt(slot(6), R("yp"), slot(8), A.subtract)
+            if i + 1 < len(ps):
+                gather("v", ps[i + 1][1], lo)
+                sc(ps[i + 1][1], lo)
+            js = list(range(hi // 16 - 1, lo // 16 - 1, -1))
+            if i + 1 < len(ps):
+                results(lo, hi, False)
+                for j in js:
+                    compare(j)
+            else:
+                for j in js:
+                    compare(j)
+                results(lo, hi, True)
+        act(R("tr", 0, nl), P(bR, 0, nl), AF.Relu, bias=2048.0)
+        act(R("ww", 0, nl), R("tr", 0, nl), AF.Relu, bias=V0, scale=-1.0)
+        X = slot(4, 0, k)
+        tt(X, R("xs", 15, nl, 16), R("pz", 0, k), A.add)
+        tt(slot(2, 0, k), R("cur", 0, k), X, A.subtract)
+        ts(R("d0", 1, 5 * k, 5), X, 0.0, A.is_equal)
+        ts(R("d0", 2, 5 * k, 5), X, (DS + C0 - 0.5) / 16, A.is_lt)
+        ts(R("d0", 4, 5 * k, 5), X, 0.0, A.is_equal)
+        scan(R("w2", 1, 10 * k, 2), R("d0", 0, 5 * k), R("w2", 0, 10 * k, 2), 0.0, A.mult, A.add)
+        scan(R("ls", h, nl), R("pat", h, nl), P(bF1, h, nl))
+        if not last:
+            ts(R("tn", 0, k), slot(5, 0, k), 16.0, A.mult, float(C0), A.subtract)
+        scan(R("ls", 0, h), R("pat", 0, h), P(bF0, 0, h))
+        if not last:
+            args(nl)
+            lists(nl)
+        ts(R("f0", 1, 2 * k, 2), R("ls", 15, nl, 16), 0.0, A.is_lt)
+        scan(R("fo", 0, 2 * k), R("f0", 0, 2 * k), R("w2", 4, 10 * k, 5), 0.0, A.mult, A.max)
+        ts(R("th", 0, k), R("fo", 1, 2 * k, 2), 16.0, A.mult)
+        dc = "dc%d" % (t % 2)
+        tt(ind(CT, R("th", 0, k)), R(dc, 0, nl), R("ww", 0, nl), A.subtract)
+
+    def kept(nl):
+        k = nl // 16
+        tt(R("nl", 0, k), slot(4, 0, k), R("fo", 1, 2 * k, 2), A.is_le)
+
+    def exchange(x, nl, nx):
         stg, land = "stg%d" % x, "land%d" % x
-        b = W - DS
-        SI, EX, GG = R("ct", 0, DS), R("ct", b, W), R("gg", OWN, L)
-        mm(P(7, 0, DS), R("r3"), SI, True, True)
-        mm(P(2, 0, DS), R("r3"), EX, True, True)
+        b = C0 + W - DS
+        SI, EX = R("ct", C0, C0 + DS), R("ct", b, b + DS)
+        ts(R(stg, 0, 192, 2), SI, 0.0, A.is_gt)
         act(R(stg, 1, 64, 2), R("ct", b + 2 * S, b + 3 * S), bias=1.0 / 16)
         act(R(stg, 65, 128, 2), R("ct", b + S, b + 2 * S), bias=1.0 / 16)
         ts(R(stg, 129, 192, 2), R("ct", b, b + S), 1.0 / 16, A.add)
-        cp(CC(16), NEXT)
-        ts(R(stg, 0, 192, 2), P(7, 0, DS), 0.0, A.is_gt)
         peers = [T.cores[(rank + d) % 4] for d in range(1, 4)]
         masks, used = {}, []
         for j in sorted(range(3), key=lambda j: len(topo.engines(core, peers[j]))):
@@ -374,82 +484,89 @@ def rank_program(g, core, T, topo):
                                             src=ap(R(stg, 64 * j, 64 * j + 64)), dst=ap(R(land, 64 * j, 64 * j + 64))))
             return g.remote_dma_fused(tr, local_sem=T.sem["snt%d" % x])
         add("g", send, [R(stg)], [], kind="r")
-        act(R("gt"), P(7, 0, DS), bias=128.0, scale=-65536.0)
-        ts(R("te"), P(2, 0, DS), 0.0, A.is_equal)
+        ts(R("ta"), EX, -0.5, A.is_gt)
+        ts(R("tb"), EX, 0.0, A.is_gt)
+        if nl < L:
+            ms(R("nl"), 1.0)
+        tt(R("te"), R("ta"), R("tb"), A.subtract)
+        kept(nl)
+        tt(R("dy"), Y, R("yp"), A.subtract)
+        tt(R("dy"), R("dy"), R("nl"), A.mult)
+        tt(Y, R("yp"), R("dy"), A.add)
+        ms(R("nl"), 1.0)
+        tt(R("tm"), R("te"), R("dg", 0, DS), A.mult)
         ts(R("x2"), EX, -1.0, A.mult, cHR, A.add)
-        tt(R("x5"), R("agt", b, W), GG, A.subtract)
-        tt(R("te2"), R("te"), R("ecol"), A.mult)
-        tt(R("dif"), R("te"), R("x2"), A.mult)
-        tt(R("x5"), R("x5"), R("te"), A.mult)
-        add("v", None, [], [R(land)], kind="w", ext=("arr%d" % x, 3 * ENG))
-        ASK, G6 = R(land, 0, 192, 2), R("d1", 107, 128, 4)
-        tt(R("x6"), ASK, R("x5"), A.mult)
-        tt(R("x3"), ASK, R("te2"), A.mult)
-        tt(GG, GG, R("x6"), A.add)
-        lists(L)
+        tt(R("x3"), R("tm"), R("ecol"), A.mult)
+        ts(R("hm"), SI, 0.0, A.is_gt)
         scan(R("x4"), R("pat", 0, DS), R("x3"))
-        tt(R("x2"), ASK, R("dif"), A.mult)
-        tt(R("s2", 0, 6), R("x4", 15, DS, 16), G6, A.add)
-        tt(EX, EX, R("x2"), A.add)
-        ts(R("tn", 26, 32), R("s2", 0, 6), cOFF, A.subtract, float(IDO), A.subtract)
+        tt(R("dif"), R("te"), R("x2"), A.mult)
+        ts(R("s3", 0, 6), R("x4", 15, DS, 16), -1.0 / 16, A.mult)
+        tt(slot(5, 10, 16), slot(5, 10, 16), R("s3", 0, 6), A.add)
+        ts(R("tn"), Y, 16.0, A.mult, float(C0), A.subtract)
+        args(L)
+        lists(L)
         digits(L, nx)
+        add("v", None, [], [R(land)], kind="w", ext=("arr%d" % x, 3 * ENG))
+        ASK = R(land, 0, 192, 2)
         for j in range(3):
-            tt(R("x1", (2 - j) * S, (3 - j) * S), R(land, 64 * j + 1, 64 * j + 64, 2), R("gt", (2 - j) * S, (3 - j) * S), A.max)
-        ts(G6, R("s2", 0, 6), cOFF, A.subtract)
+            tt(R("x1", (2 - j) * S, (3 - j) * S), R(land, 64 * j + 1, 64 * j + 64, 2), R("hm", (2 - j) * S, (3 - j) * S), A.mult)
         tt(SI, SI, R("x1"), A.min)
 
-    digits(OWN, "dc0")
+        def late():
+            tt(R("x2"), ASK, R("dif"), A.mult)
+            tt(R("x3"), R("tm"), ASK, A.is_gt)
+            tt(EX, EX, R("x2"), A.add)
+            scan(R("x4"), R("pat", 0, DS), R("x3"))
+            tt(R("nl", 10, 16), R("nl", 10, 16), R("x4", 15, DS, 16), A.subtract)
+            state()
+        return late
+
+    constants(0)
     args(OWN)
     lists(OWN)
+    digits(OWN, "dc0")
+    constants(1)
     t = 0
+    between = lambda: None
     for rnd in range(ROUNDS):
         nl = OWN if rnd == 0 else L
         for st in range(STEPS):
-            dc, nx = "dc%d" % (t % 2), "dc%d" % (1 - t % 2)
-            step(nl, dc, 1 if t == 0 else 2 if st == 0 else 0)
+            nx = "dc%d" % (1 - t % 2)
+            choose(nl, t, between)
+            step(nl, t, st == STEPS - 1)
             if st < STEPS - 1:
-                args(nl)
-                lists(nl)
                 digits(nl, nx)
-                scatter(nl, dc)
+
+                def between(nl=nl):
+                    if nl < L:
+                        ms(R("nl"), 1.0)
+                    kept(nl)
+                    state()
             elif rnd < ROUNDS - 1:
-                args(L)
-                scatter(nl, dc)
-                exchange(rnd, nx)
-            else:
-                scatter(nl, dc)
+                between = exchange(rnd, nl, nx)
             t += 1
 
-    cuts = [0, 320, 800, 1280, 1680, W]
+    kept(L)
+    state()
+    cuts = [0, 256, 704, 1152, 1600, W]
     for h in range(5):
         lo, hi = cuts[h], cuts[h + 1]
-        ts(R("tmpw", lo, hi), R("ct", lo, hi), 208.0 - 0.06, A.add)
-        ts(R("tmp2", lo, hi), R("ct", lo, hi), 1.0 / 16, A.add, 0.0, A.max)
-        mm(P(3 + h, 0, hi - lo), R("mi"), R("tmpw", lo, hi), True, False)
-        mm(P(3 + h, 0, hi - lo), R("mf"), R("tmp2", lo, hi), False, True)
-        if h < 4:
-            act(R("outv", lo, hi), P(3 + h, 0, hi - lo), bias=-192.0)
-            store("y", T.yv[:, lo:hi], R("outv", lo, hi))
-    ts(R("s2"), NEXT, float(REST + IDO), A.is_equal, -float(REST + 1), A.mult)
-    ts(R("s3"), NEXT, float(IDO), A.subtract)
-    ts(R("outv", 1680, W), P(7, 0, W - 1680), -192.0, A.add)
-    tt(R("yo"), R("s2"), R("s3"), A.add)
-    store("y", T.yv[:, 1680:W], R("outv", 1680, W))
-    store("y", T.ya[:, :], R("yo"))
+        act(R("ab", lo, hi), R("ct", C0 + lo, C0 + hi), AF.Abs, bias=145.5, scale=0.25)
+        if h == 0:
+            ts(R("s2"), R("cur"), ZR, A.is_equal, -float(REST + 1), A.mult)
+            ts(R("s3"), R("cur"), 16.0, A.mult, float(C0), A.subtract)
+        ts(R("outv", lo, hi), R("ab", lo, hi), -1.0, A.mult, 144.0, A.add)
+        store("y", T.yv[:, lo:hi], R("outv", lo, hi))
+        if h == 0:
+            tt(R("yo"), R("s2"), R("s3"), A.add)
+            store("y", T.ya[:, :], R("yo"))
 
+    ops[:] = arrange(ops)
     known = {e: 0 for e in Q}
     prev = {e: 0 for e in Q}
-    done, waits, need, hist = [], [], set(), {}
-    for i, o in enumerate(ops):
-        deps, e = set(), o["e"]
-        for x in o["r"] + o["w"]:
-            wr = x in o["w"]
-            for j, y, jw in hist.get(x[0], []):
-                if x[0].startswith("pb"):
-                    if ops[j]["e"] != e or ((wr or jw) and overlap(x, y) and not o["acc"]):
-                        deps.add(j)
-                elif (wr or jw) and overlap(x, y):
-                    deps.add(j)
+    done, waits, need = [], [], set()
+    for i, (o, cf) in enumerate(zip(ops, conflicts(ops))):
+        deps, e = [j for j in cf if cf[j]], o["e"]
         waits.append([])
         for j in sorted(deps, reverse=True):
             if ops[j]["k"] not in "rw" and not known[e] >> j & 1:
@@ -459,10 +576,6 @@ def rank_program(g, core, T, topo):
         if o["k"] == "c":
             prev[e] |= 1 << i
         done.append(known[e] | (prev[e] if o["k"] == "c" else 1 << i))
-        for x in o["r"]:
-            hist.setdefault(x[0], []).append((i, x, False))
-        for x in o["w"]:
-            hist.setdefault(x[0], []).append((i, x, True))
     tok, cnt, nxt = {}, {}, {e: 0 for e in POOL}
     for i, o in enumerate(ops):
         q = Q[o["e"]]

@@ -1,3 +1,4 @@
+import math
 from concourse.bass import DstId, RemoteDMATransfer
 from concourse.mybir import AluOpType, ActivationFunctionType
 
@@ -7,29 +8,30 @@ L = OWN + DS
 REST = W
 C0 = 256
 CTW = C0 + W + 16
-V0 = 1158.0
 U = 1.0 / 1024
 BASE, THR0, W0 = 256.0 / 150.0, 2.56, 1.0e25
-HUGE = 1.0e29
-FIX, PEF = 50, 0.5
-WAKE, SAME = 160, 120
+HUGE, FLOOR = 1.0e29, -512.0
+FIX, PEF = 0, 0.5
+WAKE, SAME = 240, 240
 ENG = 4
-PIECES = {OWN: ((80, 128, None), (32, 80, None), (0, 32, None)), L: ((128, 200, None), (48, 128, None), (0, 48, None))}
+PIECES = {OWN: ((80, 120), (0, 48)), L: ((128, 184), (48, 96), (0, 48))}
 SCUT = {OWN: 64, L: 128}
+HALVES = 2
+CUTS = [0, 256, 704, 1152, 1600, W]
 
 F, H, B, I, U16 = "float32", "float16", "bfloat16", "int32", "uint16"
 SB = {}
 for _t, _l in ((I, "agt 1936 rin 16 pc 8 pc2 8 m1 128 m2 128"),
                (U16, "tn 16 th 16 a0 16 ol 128"),
-               (H, "bl 152 bh 152 zx 152 zd 152 gg 256 mh 128 mn 128 mu 128 dec 128 mp 1024 vv 2048 rr 2048 rp 256 sv 256 pp 256 xu 256 tr 256 "
+               (H, "bl 152 bh 152 zx 152 zd 152 gg 256 mh 128 mn 128 mu 128 dec 128 mp 2048 vv 2048 rr 2048 rp 256 sv 256 pp 256 xu 256 tr 256 "
                    "t1 1920 stg0 192 stg1 192 land0 192 land1 192 hm 96 x1 96 ta 96 tb 96 te 96 tm 96 x3 96 ecol 96"),
-               (F, "ct %d col 32 oh 16 geo 16 s1 16 s2 16 s3 16 wl0 16 wl 16 pz 16 nl 16 cur 16 yp 16 dy 16 yo 16 of 128 xs 256 ls 256 "
-                   "w2 160 d0 80 f0 32 fo 32 dc0 256 dc1 256 ww 256 hr 160 dif 96 x2 96 x4 96" % CTW),
-               (B, "vin 1920 dt 2048 ya 1920 outv 1920 i0 256 i1 256 pm 152 gh 128 kb 256 zer 256 uu 256 u1 256 ones 480 m10 128 mi 128 mv 128 "
-                   "bw 128 pq 152 blo 128 bhi 128 dg 256 bm 128 pat 256 mk 256 mkx 256 thr0 256 thr 256 sg 256 ee 2176")):
+               (F, "ct %d col 40 oh 16 geo 16 s1 16 s2 16 s3 16 wl0 16 wl 16 pz 16 pz3 16 lim 16 lim2 16 nl 16 cur 16 yq 16 dy 16 yo 16 of 128 xs 256 "
+                   "w0 848 w1 848 d0 128 f0 48 fo 48 dc0 256 dc1 256 ww 256 hr 160 dif 96 x2 96 x4 96" % CTW),
+               (B, "vin 1920 dt 2048 ab 1920 outv 1920 i0 256 i1 256 pm 152 gh 128 kb 256 zer 256 uu 256 u1 256 ones 480 m14 128 mi 128 mv 128 "
+                   "bw 128 pq 152 blo 128 bhi 128 dg 256 bm 128 pat 256 pat2 256 mk 256 mkx 256 thr0 256 thr 256 sg 256 ee 2176")):
     _w = _l.split()
     for _k in range(0, len(_w), 2):
-        SB["ab" if _w[_k] == "ya" else _w[_k]] = (int(_w[_k + 1]), _t)
+        SB[_w[_k]] = (int(_w[_k + 1]), _t)
 SCRATCH = {k: ("sbuf", [128, v[0]], v[1]) for k, v in SB.items()}
 for _k in range(8):
     SCRATCH["pb%d" % _k] = ("psum", [128, 512], F)
@@ -58,9 +60,7 @@ def ind(win, off):
 
 
 def overlap(a, b):
-    if a[1] >= b[2] or b[1] >= a[2]:
-        return False
-    return a[3] != b[3] or a[3] == 1 or (a[1] - b[1]) % a[3] == 0
+    return a[1] < b[2] and b[1] < a[2] and (a[1] - b[1]) % math.gcd(a[3], b[3]) == 0
 
 
 def width(x):
@@ -96,13 +96,12 @@ def conflicts(ops):
     hist, out = {}, []
     for i, o in enumerate(ops):
         deps, e = {}, o["e"]
-        for x in o["r"] + o["w"]:
-            wr = x in o["w"]
+        for x, wr in [(x, False) for x in o["r"]] + [(x, True) for x in o["w"]]:
             for j, y, jw in hist.get(x[0], []):
+                hit = (wr or jw) and overlap(x, y)
                 if x[0].startswith("pb"):
-                    sem = ops[j]["e"] != e or ((wr or jw) and overlap(x, y) and not o["acc"])
-                    deps[j] = deps.get(j, False) or sem
-                elif (wr or jw) and overlap(x, y):
+                    deps[j] = deps.get(j, False) or ops[j]["e"] != e or (hit and not o["acc"])
+                elif hit:
                     deps[j] = True
         out.append(deps)
         for x in o["r"]:
@@ -123,7 +122,7 @@ def arrange(ops):
     def lag(j, i):
         if ops[i]["k"] == "d" and ops[j]["k"] == "d":
             return ops[j]["c"][1] - 1300
-        return ops[j]["c"][1] + (0 if not deps[i][j] else SAME if ops[i]["e"] == ops[j]["e"] else WAKE)
+        return ops[j]["c"][1] + (0 if not deps[i][j] or ops[j]["k"] == "w" else SAME if ops[i]["e"] == ops[j]["e"] else WAKE)
     rest = [o["c"][1] for o in ops]
     for i in range(len(ops) - 1, -1, -1):
         for j in deps[i]:
@@ -162,7 +161,8 @@ def rank_program(g, core, T, topo):
         for x in ins:
             if isinstance(x, tuple):
                 rd += [x[1], x[2]] if x[0] == "ind" else [x]
-        ops.append({"e": eng, "fn": fn, "c": cycles(eng, kind, ins, outs, both), "r": rd, "w": [x[1] if x[0] == "ind" else x for x in outs], "k": kind, "acc": acc, "ext": ext})
+        ops.append({"e": eng, "fn": fn, "c": cycles(eng, kind, ins, outs, both), "r": rd,
+                    "w": [x[1] if x[0] == "ind" else x for x in outs], "k": kind, "acc": acc, "ext": ext})
 
     def ts(out, in0, s1, op0, s2=None, op1=None):
         if op1 is None:
@@ -207,17 +207,17 @@ def rank_program(g, core, T, topo):
     load("s", R("rin", 0, 10), T.rts[:, :])
     load("y", R("agt", 0, W), T.ag[:, :])
 
-    cR, cG, cLO, cHI, cW, cW2, cHB, cHR, cG2, cG21, cG16, cU, cR16, cT = [C(k) for k in range(14)]
-    cA = 20
+    cR, cG, cLO, cHI, cHB, cHR, cG2, cG21, cG16, cU, cR16, cK, cKI, cV0, cNV0, cMANY, cNMANY = [C(k) for k in range(17)]
+    cA, cD = 20, 28
     CT, CELLS, AG, DT = R("ct"), R("ct", C0, CTW), R("agt"), R("dt")
     ZR = (REST + C0) / 16.0
 
     def OH(j):
         return R("oh", j, j + 1)
 
-    def slot(k, lo=0, hi=16):
-        return R("w2", 10 * lo + k, 10 * hi, 10)
-    XV, Y = slot(4), slot(5)
+    def slot(t, at, lo=0, hi=16):
+        return R("w%d" % (t % 2), 48 * lo + at, 48 * (hi - 1) + at + 1, 48)
+    sOWN, sDUM, sPAR, sCX, sX, sY = 31, 37, 49, 55, 61, 95
     iota(R("pc", 0, 1), [[0, 1]], 0, 1)
     iota(R("i0"), [[0, 16], [1, 16]], 0, 0)
     iota(R("i1"), [[1, 16], [0, 16]], 0, 0)
@@ -229,32 +229,39 @@ def rank_program(g, core, T, topo):
     ts(R("pc2", 1, 2), R("pc", 0, 1), 4, A.logical_shift_right)
     ms(R("ones"), 1.0)
     cp(R("col", 0, 2), R("pc2", 0, 2))
-    ms(R("m10"), -10.0)
+    ms(R("m14"), -14.0)
     ms(R("agt", W, 1936), REST)
-    ms(R("mp"), 1.0 / 16)
+    ms(R("mp", 0, 2048, 8), -4096.0)
+    for j in range(1, 8):
+        ms(R("mp", j, 2048, 8), 1.0 / 16)
     ts(R("oh"), R("i0", 0, 16), cR, A.is_equal)
-    ms(R("mp", 0, 1024, 8), -4096.0)
     ts(R("uu"), R("i0"), OH(0), A.mult, U, A.mult)
-    ts(R("col", cA, cA + 8), R("i0", 1, 9), OH(2), A.mult, U, A.mult)
+    ts(R("s3", 0, 8), R("i0", 1, 9), OH(2), A.mult, U, A.mult)
     ts(R("u1"), R("i1"), OH(1), A.mult, U, A.mult)
-    ts(R("col", cA, cA + 8), R("col", cA, cA + 8), -1.0 / 32, A.add)
+    ts(R("col", cA, cA + 8), R("s3", 0, 8), -1.0 / 32, A.add)
     tt(R("uu"), R("uu"), R("u1"), A.add)
     ts(R("mi"), R("pm", 15, 143), 0.0, A.is_equal)
     fill(R("ct", 0, C0), R("i0"), 0.0)
     fill(R("ct", C0 + W, CTW), R("i0", 0, 16), 0.0)
+    act(cK, OH(9), scale=2.0, bias=4.0)
+    act(cNV0, OH(9), scale=-579.0, bias=-1158.0)
+    act(cV0, OH(9), scale=579.0, bias=1158.0)
+    act(cKI, OH(9), scale=1.0 / 6 - 0.25, bias=0.25)
+    act(cMANY, OH(9), scale=-564.0, bias=-1128.0)
+    act(cNMANY, OH(9), scale=564.0, bias=1128.0)
     act(cHB, OH(3), scale=8 * U, bias=5.0 / 128)
     act(cG2, cG, scale=2.0)
     act(cG21, cG, scale=2.0, bias=1.0)
     act(cG16, cG, scale=16.0)
     act(cR16, cR, scale=1.0 / 16)
-    act(R("mv"), R("mi"), scale=-1280.0)
+    act(R("mv"), R("mi"), scale=-1792.0)
     for a in range(8):
         if a in (5, 6):
             act(R("dt", 256 * a, 256 * a + 256), R("uu"), bias=C(cA + a))
         else:
             ts(R("dt", 256 * a, 256 * a + 256), R("uu"), C(cA + a), A.add)
     for h in range(4):
-        mm(P(3 + h, 0, 480), R("m10"), R("ones"), True, False)
+        mm(P(3 + h, 0, 480), R("m14"), R("ones"), True, False)
         mm(P(3 + h, 0, 480), R("mi"), R("dt", 480 * h, 480 * h + 480), False, False)
     ts(cLO, cR, 7.5, A.is_lt)
     ts(cHI, cR, 7.5, A.is_gt)
@@ -265,7 +272,7 @@ def rank_program(g, core, T, topo):
 
     for h in range(4):
         lo, hi = 480 * h, 480 * h + 480
-        act(R("t1", lo, hi), R("vin", lo, hi), scale=4.0, bias=-V0)
+        act(R("t1", lo, hi), R("vin", lo, hi), scale=cK, bias=cNV0)
         mm(P(3 + h, 0, 480), R("mv"), R("vin", lo, hi), False, True)
         tt(R("ct", C0 + lo, C0 + hi), P(3 + h, 0, 480), R("t1", lo, hi), A.max)
     fill(R("hr"), R("i0", 0, 160), cHR)
@@ -273,55 +280,50 @@ def rank_program(g, core, T, topo):
     cp(ind(CELLS, R("tn", 0, 10)), R("hr"))
     ts(R("bl"), R("pm"), 0.0, A.is_equal, cLO, A.mult)
     ts(R("bh"), R("pm"), 0.0, A.is_equal, cHI, A.mult)
-    ts(R("blo"), R("gh"), cG2, A.is_equal, 4096.0, A.mult)
-    ts(R("bhi"), R("gh"), cG21, A.is_equal, 4096.0, A.mult)
-
-    def constants(part):
-        if part == 0:
-            act(cW2, OH(0), scale=64.0)
-            act(cT, OH(1), scale=1024.0, bias=cW2)
-            act(cW2, OH(2), scale=16384.0, bias=cT)
-            act(cT, OH(4), scale=-17472.0, bias=cW2)
-            act(cW2, cT)
-            act(cW, OH(3), scale=-32768.0, bias=cT)
-            act(cT, OH(4), scale=32768.0, bias=cW)
-            act(cW, cT)
-            act(cU, OH(4), scale=8192.0)
-            fill(R("kb"), R("i0"), 1.0 / BASE)
-            fill(R("zer"), R("i0"), 0.0)
-            fill(R("geo"), R("i0", 0, 16), BASE)
-            fill(R("s2"), R("i0", 0, 16), BASE ** -16)
-            fill(R("pat"), R("i0"), 0.0)
-            fill(R("pat", 0, 256, 16), R("i0", 0, 16), -2 * HUGE)
-        elif part == 1:
-            ts(R("bm"), R("i1", 0, 128), cG, A.is_equal)
-            ts(R("dg"), R("i0"), cR, A.is_equal)
-            ts(R("zd"), R("pq"), cG16, A.is_equal, cW2, A.mult)
-            scan(R("thr0"), R("kb"), R("zer"), -THR0 * W0 * BASE, A.mult, A.add)
-            scan(R("s1"), R("geo"), R("oh"), 0.0, A.mult, A.add)
-            scan(R("wl0"), R("s2"), R("zer", 0, 16), W0 * BASE, A.mult, A.add)
-            ms(R("w2"), 0.0)
-            ms(R("d0"), 0.0)
-        elif part == 2:
-            act(R("mk"), R("dg"), scale=HUGE, bias=-HUGE)
-            act(R("mkx"), R("mk"), bias=-64.0)
-            act(R("dec"), R("bm"), scale=cW)
-            act(R("bw"), R("bm"), scale=R("s1", 15, 16))
-            mm(P(bR, 0, 256), R("mi"), R("thr0"), True, False)
-            mm(P(bR, 0, 256), R("mi"), R("mk"), False, True)
-            act(R("mn"), R("mi"), scale=-1.0)
-            act(R("thr"), P(bR, 0, 256))
-        elif part == 3:
-            ts(R("mh"), R("mi"), 1.0, A.mult)
-            ts(R("mu"), R("bm"), cU, A.mult)
-            ts(slot(8), R("i0", 0, 16), cR16, A.add)
-            ms(R("f0"), 0.0)
-            ms(R("pz"), 64.0)
-            cp(R("wl"), R("wl0"))
-            ms(R("cur"), ZR)
-            ts(R("cur", 0, 10), R("rin", 0, 10), 1.0 / 16, A.mult, C0 / 16.0, A.add)
-            cp(R("yp"), R("cur"))
-            cp(Y, R("cur"))
+    ts(R("blo"), R("gh"), cG2, A.is_equal, 2048.0, A.mult)
+    ts(R("bhi"), R("gh"), cG21, A.is_equal, 2048.0, A.mult)
+    chain = ((0, 64.0), (1, 1024.0), (2, 16384.0), (4, -17472.0), (3, -32768.0), (4, 32768.0), (8, -32768.0), (9, 32768.0))
+    for j, (r, w) in enumerate(chain):
+        act(C(cD + j), OH(r), scale=w, bias=C(cD + j - 1) if j else 0.0)
+    cW2, cW = C(cD + 3), C(cD + 7)
+    act(cU, OH(4), scale=8192.0)
+    fill(R("kb"), R("i0"), 1.0 / BASE)
+    fill(R("zer"), R("i0"), 0.0)
+    fill(R("geo"), R("i0", 0, 16), BASE)
+    fill(R("s2"), R("i0", 0, 16), BASE ** -16)
+    ts(R("pat"), R("i0"), 0.0, A.is_equal, -2 * HUGE, A.mult)
+    ts(R("u1"), R("i0"), 0.0, A.is_gt, HUGE, A.mult)
+    act(R("pat2"), R("u1"), bias=FLOOR)
+    ts(R("bm"), R("i1", 0, 128), cG, A.is_equal)
+    ts(R("dg"), R("i0"), cR, A.is_equal)
+    ts(R("zd"), R("pq"), cG16, A.is_equal, cW2, A.mult)
+    scan(R("thr0"), R("kb"), R("zer"), -THR0 * W0 * BASE, A.mult, A.add)
+    scan(R("s1"), R("geo"), R("oh"), 0.0, A.mult, A.add)
+    scan(R("wl0"), R("s2"), R("zer", 0, 16), W0 * BASE, A.mult, A.add)
+    act(R("mk"), R("dg"), scale=HUGE, bias=-HUGE)
+    act(R("mkx"), R("mk"), bias=-16.0)
+    act(R("dec"), R("bm"), scale=cW)
+    act(R("bw"), R("bm"), scale=R("s1", 15, 16))
+    mm(P(bR, 0, 256), R("mi"), R("thr0"), True, False)
+    mm(P(bR, 0, 256), R("mi"), R("mk"), False, True)
+    act(R("mn"), R("mi"), scale=-1.0)
+    act(R("thr"), P(bR, 0, 256))
+    act(R("mh"), R("mi"))
+    act(R("mu"), R("bm"), scale=cU)
+    ms(R("d0"), 0.0)
+    ms(R("d0", 2, 128, 8), -1.0)
+    ms(R("f0", 0, 48, 3), 0.0)
+    ms(R("f0", 2, 48, 3), -1.0)
+    ts(R("dy"), R("wl0"), R("s1", 15, 16), A.mult)
+    add("v", lambda: V.reciprocal(ap(R("yq")), ap(R("dy"))), [R("dy")], [R("yq")])
+    ts(R("f0", 1, 48, 3), R("yq"), -4000.0, A.mult)
+    for t in range(2):
+        fill(R("w%d" % t, 31, 799, 6), R("i0", 0, 128), 0.0)
+        act(slot(t, sDUM), R("i0", 0, 16), bias=cR16)
+        fill(slot(t, sY, 10, 16), R("i0", 0, 6), ZR)
+    act(slot(1, sY, 0, 10), R("rin", 0, 10), scale=1.0 / 16, bias=C0 / 16.0)
+    act(slot(0, sY, 0, 10), R("rin", 0, 10), scale=1.0 / 16, bias=C0 / 16.0)
+    ms(R("nl"), 1.0)
 
     def args(nl):
         act(R("gg", 0, nl), ind(AG, R("tn", 0, nl // 16)))
@@ -338,130 +340,100 @@ def rank_program(g, core, T, topo):
         mm(P(bLO, 0, m), R("bl", 15, 143), R("gg", 0, nl, 2), True, False)
         mm(P(bLO, 0, m), R("bl", 7, 135), R("gg", 1, nl, 2), False, False)
 
-    def state():
-        tt(R("dy"), Y, R("yp"), A.subtract)
+    def state(t):
         tt(R("wl"), R("wl0"), R("nl"), A.mult)
-        tt(R("dy"), R("dy"), R("nl"), A.mult)
-        act(R("pz"), R("nl"), scale=1024.0, bias=-960.0)
-        tt(R("cur"), R("yp"), R("dy"), A.add)
-        cp(R("yp"), Y)
+        act(R("pz"), R("nl"), scale=1024.0, bias=-1008.0)
+        act(R("pz3"), R("nl"), scale=-4096.0, bias=4080.0)
+        act(R("lim"), R("nl"), scale=9500.0, bias=-10000.0)
+        act(R("lim2"), R("nl"), scale=(DS - 0.5) / 16 - 1024.0, bias=1024.0)
+        act(R("yq"), slot(t - 1, sY), bias=1008.0)
+        tt(R("dy"), slot(t, sY), R("pz3"), A.add)
+        tt(R("cur"), R("dy"), R("yq"), A.min)
 
-    def choose(nl, t, between):
+    def choose(nl, between):
         k, m, sc = nl // 16, nl // 2, SCUT[nl]
         cp(R("a0", 0, k), P(bL, 0, k))
-        act(R("sv", 0, sc), ind(CELLS, R("a0", 0, sc // 16)))
-        cp(R("sv", sc, nl), ind(CELLS, R("a0", sc // 16, k)))
-        act(R("of", 0, m), P(bHI, 0, m), bias=17 * 2048.0)
-        ts(R("sg", 0, nl), R("sv", 0, nl), 30.0 - V0, A.is_gt)
+        act(R("sg", 0, sc), ind(CELLS, R("a0", 0, sc // 16)), AF.Sign, bias=cNMANY)
+        ts(R("sg", sc, nl), ind(CELLS, R("a0", sc // 16, k)), cMANY, A.is_gt, 2.0, A.mult)
+        act(R("of", 0, sc // 2), P(bHI, 0, sc // 2), bias=2048.0)
+        act(R("of", sc // 2, m), P(bHI, sc // 2, m), bias=17 * 2048.0)
         mm(P(bLO, 0, m), R("blo"), R("sg", 0, nl, 2), False, False)
         mm(P(bLO, 0, m), R("bhi"), R("sg", 1, nl, 2), False, True)
         between()
         act(R("pp", 0, nl), ind(CELLS, R("tn", 0, k)))
-        halves = [(m // 2, m), (0, m // 2)]
-        for lo, hi in halves:
+        act(R("sv", 0, nl), ind(CELLS, R("a0", 0, k)))
+        for lo, hi in ([(m // 2, m), (0, m // 2)] if HALVES == 2 else [(0, m)]):
             tt(R("m1", lo, hi), P(bLO, lo, hi), R("of", lo, hi), A.max)
-        for lo, hi in halves:
             ts(R("m2", lo, hi), R("m1", lo, hi), 2047, A.bitwise_and)
-        for lo, hi in halves:
             cp(R("ol", lo, hi), R("m2", lo, hi))
 
     def step(nl, t, last):
         k = nl // 16
         h = 16 * (k // 2)
-        if t == 0:
-            constants(2)
+        wb = "w%d" % (t % 2)
         mm(P(bF0, 0, h), R("mi"), R("thr", 0, h), True, False)
         mm(P(bF1, h, nl), R("mi"), R("thr", h, nl), True, False)
         mm(P(bR, 0, nl), R("mn"), R("sv", 0, nl), True, False)
         for r in range(16):
             mm(P(bL, 16, 16 + k), R("zd", 15 - r, 143 - r), R("pp", r, nl, 16), r == 0, r == 15)
-
-        def gather(e, lo, hi):
-            if lo < hi:
-                (act if e == "s" else cp)(R("vv", 8 * lo, 8 * hi), ind(CELLS, R("ol", lo // 2, hi // 2)))
-
-        def sc(lo, hi):
-            if lo < hi:
-                scan(R("rr", 8 * lo, 8 * hi), R("mp", 0, 8 * (hi - lo)), R("vv", 8 * lo, 8 * hi))
-
-        def decode(lo, hi):
-            ts(R("rp", lo, hi), R("rr", 8 * lo + 7, 8 * hi, 8), -0.25, A.max)
+        tt(slot(t, sPAR, 0, k), P(bL, 16, 16 + k), slot(t - 1, sY, 0, k), A.subtract)
+        tt(slot(t, sOWN, 0, k), slot(t - 1, sY, 0, k), slot(t, sDUM, 0, k), A.subtract)
+        at, hi = 0, nl
+        for lo, cut in PIECES[nl]:
+            for e, a, b in ((act, lo, cut), (cp, cut, hi)):
+                if a < b:
+                    e(R("vv", 8 * a, 8 * b), ind(CELLS, R("ol", a // 2, b // 2)))
+                    scan(R("rr", 8 * a, 8 * b), R("mp", 0, 8 * (b - a)), R("vv", 8 * a, 8 * b))
+            RR = R("rr", 8 * lo + 7, 8 * hi, 8)
             mm(P(bM, lo, hi), R("mi"), R("mkx", lo, hi), True, False)
-            mm(P(bM, lo, hi), R("dec"), R("rp", lo, hi), False, True)
-            mm(P(bX, lo, hi), R("dec"), R("rp", lo, hi), True, True)
-            scan(R("xs", lo, hi), R("pat", lo, hi), P(bM, lo, hi))
-
-        at = [0]
-
-        def compare(j):
-            w, a = nl - 16 * j, at[0]
-            ts(R("ee", a, a + w), R("xu", 16 * j, nl), R("xs", 16 * j + 15, 16 * j + 16), A.is_equal, R("wl", j, j + 1), A.mult)
-            if 16 * j < h:
-                mm(P(bF1, h, nl), R("bw"), R("ee", a + h - 16 * j, a + w), False, j == 0)
-                mm(P(bF0, 16 * j, h), R("bw"), R("ee", a, a + h - 16 * j), False, j == 0)
-            else:
-                mm(P(bF1, 16 * j, nl), R("bw"), R("ee", a, a + w), False, False)
-            at[0] += w
-
-        def results(lo, hi, stop):
-            mm(P(bR, lo, hi), R("mh"), R("rr", 8 * lo + 7, 8 * hi, 8), False, False)
-            mm(P(bR, lo, hi), R("mu"), R("rp", lo, hi), False, stop)
-        ps = PIECES[nl]
-        tops = [nl] + [p[0] for p in ps]
-        gather("s", ps[0][0], ps[0][1])
-        gather("v", ps[0][1], nl)
-        if t == 0:
-            constants(3)
-        sc(ps[0][1], nl)
-        for i, (lo, vcut, _) in enumerate(ps):
-            hi = tops[i]
-            if i + 1 < len(ps):
-                gather("s", ps[i + 1][0], ps[i + 1][1])
-            sc(lo, vcut)
-            decode(lo, hi)
-            act(R("xu", lo, hi), P(bX, lo, hi), bias=-64.0)
-            if i == 0:
-                tt(slot(0, 0, k), P(bL, 16, 16 + k), R("yp", 0, k), A.subtract)
-                tt(slot(6), R("yp"), slot(8), A.subtract)
-            if i + 1 < len(ps):
-                gather("v", ps[i + 1][1], lo)
-                sc(ps[i + 1][1], lo)
-            js = list(range(hi // 16 - 1, lo // 16 - 1, -1))
-            if i + 1 < len(ps):
-                results(lo, hi, False)
-                for j in js:
-                    compare(j)
-            else:
-                for j in js:
-                    compare(j)
-                results(lo, hi, True)
-        act(R("tr", 0, nl), P(bR, 0, nl), AF.Relu, bias=2048.0)
-        act(R("ww", 0, nl), R("tr", 0, nl), AF.Relu, bias=V0, scale=-1.0)
-        X = slot(4, 0, k)
-        tt(X, R("xs", 15, nl, 16), R("pz", 0, k), A.add)
-        tt(slot(2, 0, k), R("cur", 0, k), X, A.subtract)
-        ts(R("d0", 1, 5 * k, 5), X, 0.0, A.is_equal)
-        ts(R("d0", 2, 5 * k, 5), X, (DS + C0 - 0.5) / 16, A.is_lt)
-        ts(R("d0", 4, 5 * k, 5), X, 0.0, A.is_equal)
-        scan(R("w2", 1, 10 * k, 2), R("d0", 0, 5 * k), R("w2", 0, 10 * k, 2), 0.0, A.mult, A.add)
-        scan(R("ls", h, nl), R("pat", h, nl), P(bF1, h, nl))
+            mm(P(bM, lo, hi), R("dec"), RR, False, True)
+            mm(P(bX, lo, hi), R("dec"), RR, True, True)
+            scan(R("xs", lo, hi), R("pat2", lo, hi), P(bM, lo, hi), FLOOR, A.min, A.max)
+            act(R("xu", lo, hi), P(bX, lo, hi), AF.Relu, bias=-16.0)
+            for j in range(hi // 16 - 1, lo // 16 - 1, -1):
+                w = nl - 16 * j
+                ts(R("ee", at, at + w), R("xu", 16 * j, nl), R("xs", 16 * j + 15, 16 * j + 16), A.is_equal, R("wl", j, j + 1), A.mult)
+                if 16 * j < h:
+                    mm(P(bF1, h, nl), R("bw"), R("ee", at + h - 16 * j, at + w), False, j == 0)
+                    mm(P(bF0, 16 * j, h), R("bw"), R("ee", at, at + h - 16 * j), False, j == 0)
+                else:
+                    mm(P(bF1, 16 * j, nl), R("bw"), R("ee", at, at + w), False, False)
+                at += w
+            hi = lo
+        RR = R("rr", 7, 8 * nl, 8)
+        act(R("rp", 0, nl), RR, AF.Relu, bias=0.25)
+        mm(P(bR, 0, nl), R("mh"), RR, False, False)
+        mm(P(bR, 0, nl), R("mu"), R("rp", 0, nl), False, True)
+        act(R("tr", 0, nl), P(bR, 0, nl), AF.Relu)
+        act(R("ww", 0, nl), R("tr", 0, nl), AF.Relu, bias=cV0, scale=-1.0)
+        XS = R("xs", 15, nl, 16)
+        tt(slot(t, sX, 0, k), XS, R("pz", 0, k), A.add)
+        tt(slot(t, sCX, 0, k), R("cur", 0, k), XS, A.subtract)
+        tt(R("d0", 1, 8 * k, 8), XS, R("lim", 0, k), A.is_lt)
+        tt(R("d0", 4, 8 * k, 8), XS, R("lim", 0, k), A.is_lt)
+        tt(R("d0", 5, 8 * k, 8), XS, R("lim2", 0, k), A.is_lt)
+        scan(R(wb, 65, 65 + 48 * k, 6), R("d0", 0, 8 * k), R(wb, 31, 31 + 48 * k, 6), 0.0, A.mult, A.add)
         if not last:
-            ts(R("tn", 0, k), slot(5, 0, k), 16.0, A.mult, float(C0), A.subtract)
-        scan(R("ls", 0, h), R("pat", 0, h), P(bF0, 0, h))
-        if not last:
+            ts(R("tn", 0, k), slot(t, sY, 0, k), 16.0, A.mult, float(C0), A.subtract)
             args(nl)
             lists(nl)
-        ts(R("f0", 1, 2 * k, 2), R("ls", 15, nl, 16), 0.0, A.is_lt)
-        scan(R("fo", 0, 2 * k), R("f0", 0, 2 * k), R("w2", 4, 10 * k, 5), 0.0, A.mult, A.max)
-        ts(R("th", 0, k), R("fo", 1, 2 * k, 2), 16.0, A.mult)
-        dc = "dc%d" % (t % 2)
-        tt(ind(CT, R("th", 0, k)), R(dc, 0, nl), R("ww", 0, nl), A.subtract)
+        scan(R(wb, 3 * h, 3 * nl, 3), R("pat", h, nl), P(bF1, h, nl))
+        scan(R(wb, 0, 3 * h, 3), R("pat", 0, h), P(bF0, 0, h))
+        scan(R("fo", 0, 3 * k), R("f0", 0, 3 * k), R(wb, 45, 45 + 48 * k, 16), 0.0, A.mult, A.min)
+        ts(R("th", 0, k), R("fo", 2, 3 * k, 3), -16.0, A.mult)
+        tt(ind(CT, R("th", 0, k)), R("dc%d" % (t % 2), 0, nl), R("ww", 0, nl), A.subtract)
 
-    def kept(nl):
+    def kept(nl, t):
         k = nl // 16
-        tt(R("nl", 0, k), slot(4, 0, k), R("fo", 1, 2 * k, 2), A.is_le)
+        tt(R("nl", 0, k), R("fo", 1, 3 * k, 3), slot(t, sX, 0, k), A.is_equal)
 
-    def exchange(x, nl, nx):
+    def back(nl, t, out):
+        kept(nl, t)
+        tt(R("dy"), slot(t, sY), slot(t - 1, sY), A.subtract)
+        tt(R("yq"), R("dy"), R("nl"), A.mult)
+        tt(out, slot(t - 1, sY), R("yq"), A.add)
+
+    def exchange(x, nl, t):
         stg, land = "stg%d" % x, "land%d" % x
         b = C0 + W - DS
         SI, EX = R("ct", C0, C0 + DS), R("ct", b, b + DS)
@@ -484,16 +456,11 @@ def rank_program(g, core, T, topo):
                                             src=ap(R(stg, 64 * j, 64 * j + 64)), dst=ap(R(land, 64 * j, 64 * j + 64))))
             return g.remote_dma_fused(tr, local_sem=T.sem["snt%d" % x])
         add("g", send, [R(stg)], [], kind="r")
+        back(nl, t, slot(t, sY))
+        ms(R("nl"), 1.0)
         ts(R("ta"), EX, -0.5, A.is_gt)
         ts(R("tb"), EX, 0.0, A.is_gt)
-        if nl < L:
-            ms(R("nl"), 1.0)
         tt(R("te"), R("ta"), R("tb"), A.subtract)
-        kept(nl)
-        tt(R("dy"), Y, R("yp"), A.subtract)
-        tt(R("dy"), R("dy"), R("nl"), A.mult)
-        tt(Y, R("yp"), R("dy"), A.add)
-        ms(R("nl"), 1.0)
         tt(R("tm"), R("te"), R("dg", 0, DS), A.mult)
         ts(R("x2"), EX, -1.0, A.mult, cHR, A.add)
         tt(R("x3"), R("tm"), R("ecol"), A.mult)
@@ -501,11 +468,11 @@ def rank_program(g, core, T, topo):
         scan(R("x4"), R("pat", 0, DS), R("x3"))
         tt(R("dif"), R("te"), R("x2"), A.mult)
         ts(R("s3", 0, 6), R("x4", 15, DS, 16), -1.0 / 16, A.mult)
-        tt(slot(5, 10, 16), slot(5, 10, 16), R("s3", 0, 6), A.add)
-        ts(R("tn"), Y, 16.0, A.mult, float(C0), A.subtract)
+        tt(slot(t, sY, 10, 16), slot(t, sY, 10, 16), R("s3", 0, 6), A.add)
+        ts(R("tn"), slot(t, sY), 16.0, A.mult, float(C0), A.subtract)
         args(L)
         lists(L)
-        digits(L, nx)
+        digits(L, "dc%d" % (1 - t % 2))
         add("v", None, [], [R(land)], kind="w", ext=("arr%d" % x, 3 * ENG))
         ASK = R(land, 0, 192, 2)
         for j in range(3):
@@ -517,49 +484,42 @@ def rank_program(g, core, T, topo):
             tt(R("x3"), R("tm"), ASK, A.is_gt)
             tt(EX, EX, R("x2"), A.add)
             scan(R("x4"), R("pat", 0, DS), R("x3"))
-            tt(R("nl", 10, 16), R("nl", 10, 16), R("x4", 15, DS, 16), A.subtract)
-            state()
+            ts(R("nl", 10, 16), R("x4", 15, DS, 16), 0.5, A.is_lt)
+            state(t)
         return late
 
-    constants(0)
     args(OWN)
     lists(OWN)
     digits(OWN, "dc0")
-    constants(1)
     t = 0
-    between = lambda: None
+    between = lambda: state(-1)
     for rnd in range(ROUNDS):
         nl = OWN if rnd == 0 else L
         for st in range(STEPS):
-            nx = "dc%d" % (1 - t % 2)
-            choose(nl, t, between)
+            choose(nl, between)
             step(nl, t, st == STEPS - 1)
             if st < STEPS - 1:
-                digits(nl, nx)
+                digits(nl, "dc%d" % (1 - t % 2))
 
-                def between(nl=nl):
-                    if nl < L:
-                        ms(R("nl"), 1.0)
-                    kept(nl)
-                    state()
+                def between(nl=nl, t=t):
+                    kept(nl, t)
+                    state(t)
             elif rnd < ROUNDS - 1:
-                between = exchange(rnd, nl, nx)
+                between = exchange(rnd, nl, t)
             t += 1
 
-    kept(L)
-    state()
-    cuts = [0, 256, 704, 1152, 1600, W]
-    for h in range(5):
-        lo, hi = cuts[h], cuts[h + 1]
-        act(R("ab", lo, hi), R("ct", C0 + lo, C0 + hi), AF.Abs, bias=145.5, scale=0.25)
-        if h == 0:
-            ts(R("s2"), R("cur"), ZR, A.is_equal, -float(REST + 1), A.mult)
-            ts(R("s3"), R("cur"), 16.0, A.mult, float(C0), A.subtract)
+    back(L, t - 1, R("cur"))
+    ts(R("s2"), R("cur"), ZR, A.is_equal, -float(REST + 1), A.mult)
+    ts(R("s3"), R("cur"), 16.0, A.mult, float(C0), A.subtract)
+    tt(R("yo"), R("s2"), R("s3"), A.add)
+    store("y", T.ya[:, :], R("yo"))
+
+    def out(lo, hi):
+        act(R("ab", lo, hi), R("ct", C0 + lo, C0 + hi), AF.Abs, bias=145.5, scale=cKI)
         ts(R("outv", lo, hi), R("ab", lo, hi), -1.0, A.mult, 144.0, A.add)
         store("y", T.yv[:, lo:hi], R("outv", lo, hi))
-        if h == 0:
-            tt(R("yo"), R("s2"), R("s3"), A.add)
-            store("y", T.ya[:, :], R("yo"))
+    for lo, hi in zip(CUTS, CUTS[1:]):
+        out(lo, hi)
 
     ops[:] = arrange(ops)
     known = {e: 0 for e in Q}

@@ -11,23 +11,24 @@ CTW = C0 + W + 16
 U = 1.0 / 1024
 BASE, THR0, W0 = 256.0 / 150.0, 2.56, 1.0e25
 HUGE, FLOOR = 1.0e29, -512.0
-FIX, PEF = 0, 0.5
-WAKE, SAME = 240, 240
+FIX, PEF, GATH, SCAT, ONEF = 0, 0.5, 1.56, 3.8, False
+WAKE, SAME = 220, 220
 ENG = 4
-PIECES = {OWN: ((80, 120), (0, 48)), L: ((128, 184), (48, 96), (0, 48))}
-SCUT = {OWN: 64, L: 128}
+PIECES = {OWN: ((96, 128), (32, 64), (0, 32)), L: ((160, 208), (64, 128), (0, 48))}
+SCUT = {OWN: 0, L: 0}
+LIFT = 1.002
 HALVES = 2
 CUTS = [0, 256, 704, 1152, 1600, W]
 
 F, H, B, I, U16 = "float32", "float16", "bfloat16", "int32", "uint16"
 SB = {}
 for _t, _l in ((I, "agt 1936 rin 16 pc 8 pc2 8 m1 128 m2 128"),
-               (U16, "tn 16 th 16 a0 16 ol 128"),
+               (U16, "tn 16 th 16 tb 16 a0 16 ol 128"),
                (H, "bl 152 bh 152 zx 152 zd 152 gg 256 mh 128 mn 128 mu 128 dec 128 mp 2048 vv 2048 rr 2048 rp 256 sv 256 pp 256 xu 256 tr 256 "
-                   "t1 1920 stg0 192 stg1 192 land0 192 land1 192 hm 96 x1 96 ta 96 tb 96 te 96 tm 96 x3 96 ecol 96"),
-               (F, "ct %d col 40 oh 16 geo 16 s1 16 s2 16 s3 16 wl0 16 wl 16 pz 16 pz3 16 lim 16 lim2 16 nl 16 cur 16 yq 16 dy 16 yo 16 of 128 xs 256 "
+                   "t1 1920 stg0 96 stg1 96 stg2 96 stg3 96 land0 96 land1 96 land2 96 land3 96 hm 96 x1 96 ta 96 tc 96 te 96 tm 96 x3 96 ones 480 md 128"),
+               (F, "ct %d col 40 gz 16 xm 16 pz4 16 dum 16 b0 48 bo 48 oh 16 geo 16 s1 16 s2 16 s3 16 wl0 16 wl 16 pz 16 pz3 16 lim 16 lim2 16 nl 16 cur 16 yq 16 dy 16 yo 16 of 128 xs 848 "
                    "w0 848 w1 848 d0 128 f0 48 fo 48 dc0 256 dc1 256 ww 256 hr 160 dif 96 x2 96 x4 96" % CTW),
-               (B, "vin 1920 dt 2048 ab 1920 outv 1920 i0 256 i1 256 pm 152 gh 128 kb 256 zer 256 uu 256 u1 256 ones 480 m14 128 mi 128 mv 128 "
+               (B, "vin 1920 dt 2048 ab 1920 outv 2192 two 256 i0 256 i1 256 pm 152 gh 128 kb 256 zer 256 uu 256 u1 256 mi 128 mv 128 "
                    "bw 128 pq 152 blo 128 bhi 128 dg 256 bm 128 pat 256 pat2 256 mk 256 mkx 256 thr0 256 thr 256 sg 256 ee 2176")):
     _w = _l.split()
     for _k in range(0, len(_w), 2):
@@ -35,12 +36,13 @@ for _t, _l in ((I, "agt 1936 rin 16 pc 8 pc2 8 m1 128 m2 128"),
 SCRATCH = {k: ("sbuf", [128, v[0]], v[1]) for k, v in SB.items()}
 for _k in range(8):
     SCRATCH["pb%d" % _k] = ("psum", [128, 512], F)
-POOL = {"v": 44, "s": 30, "p": 30, "g": 8, "d": 16}
-SEMAPHORES = ["%s%d" % (e, k) for e in POOL for k in range(POOL[e])] + ["arr0", "arr1", "snt0", "snt1"]
+POOL = {"v": 44, "s": 30, "p": 30, "g": 8, "d": 8}
+SEMAPHORES = ["%s%d" % (e, k) for e in POOL for k in range(POOL[e])] + [w + str(k) for w in ("arr", "snt") for k in range(4)]
 A = AluOpType
 AF = ActivationFunctionType
 ID = AF.Identity
-bL, bLO, bHI, bX, bM, bF0, bF1, bR = range(8)
+bL, bLO, bHI, bF0, bF1, bR = 0, 1, 2, 5, 6, 7
+DEC = ((3, 4), (1, 2))
 
 
 def R(name, lo=0, hi=None, step=1):
@@ -78,9 +80,9 @@ def cycles(eng, kind, ins, outs, both):
     if eng == "g":
         c = 160 + 2 * n
     elif outs[0][0] == "ind":
-        c = 60 + 3.8 * n
+        c = 60 + SCAT * n
     elif any(x[0] == "ind" for x in sides):
-        c = 70 + 1.56 * n
+        c = 70 + GATH * n
     elif eng == "p":
         c = max(64, n) * PEF
     elif eng != "v":
@@ -115,7 +117,7 @@ def arrange(ops):
     deps = conflicts(ops)
     for i, o in enumerate(ops):
         if o["k"] == "w":
-            deps[i][max(j for j in range(i) if ops[j]["k"] == "r")] = True
+            deps[i][max(j for j in range(i) if ops[j]["k"] == "r" and ops[j]["ext"] == o["ext"])] = True
         if o["k"] == "d" and o["w"]:
             deps[i].update({j: False for j in range(i) if ops[j]["k"] == "d"})
 
@@ -127,6 +129,7 @@ def arrange(ops):
     for i in range(len(ops) - 1, -1, -1):
         for j in deps[i]:
             rest[j] = max(rest[j], lag(j, i) + rest[i])
+    rest = [r + (1e9 if o["k"] == "d" and o["w"] else 0) for r, o in zip(rest, ops)]
     start, busy = {}, {}
     for i in sorted(range(len(ops)), key=lambda i: (-rest[i], i)):
         t, c = max([start[j] + lag(j, i) for j in deps[i]] + [0]), ops[i]["c"][0]
@@ -183,7 +186,10 @@ def rank_program(g, core, T, topo):
         add("v", lambda: V.tensor_tensor_scan(ap(out), ap(d0), ap(d1), init, op0, op1), [d0, d1], [out])
 
     def act(out, a, f=ID, bias=0.0, scale=1.0):
-        add("s", lambda: g.scalar.activation(ap(out), ap(a), f, bias=ap(bias), scale=ap(scale)), [a, bias, scale], [out])
+        if out[0] == "ind":
+            add("s", lambda: g.scalar.activation(ap(out), ap(a), f), [a], [out])
+        else:
+            add("s", lambda: g.scalar.activation(ap(out), ap(a), f, bias=ap(bias), scale=ap(scale)), [a, bias, scale], [out])
 
     def fill(out, src, c):
         act(out, src, bias=c, scale=0.0)
@@ -203,12 +209,12 @@ def rank_program(g, core, T, topo):
     def store(q, dst, a):
         add(q, lambda: Q[q].dma_start(dst, ap(a)), [a], [], kind="d")
 
-    load("y", R("vin"), T.vals[:, :])
     load("s", R("rin", 0, 10), T.rts[:, :])
+    load("y", R("vin"), T.vals[:, :])
     load("y", R("agt", 0, W), T.ag[:, :])
 
-    cR, cG, cLO, cHI, cHB, cHR, cG2, cG21, cG16, cU, cR16, cK, cKI, cV0, cNV0, cMANY, cNMANY = [C(k) for k in range(17)]
-    cA, cD = 20, 28
+    cR, cG, cLO, cHI, cHB, cHR, cG2, cG21, cG16, cU, cR16, cK, cKI, cV0, cNV0, cMANY, cNMANY, cNKI, cVD, cVH, cVL = [C(k) for k in range(21)]
+    cA, cD = 24, 32
     CT, CELLS, AG, DT = R("ct"), R("ct", C0, CTW), R("agt"), R("dt")
     ZR = (REST + C0) / 16.0
 
@@ -217,19 +223,17 @@ def rank_program(g, core, T, topo):
 
     def slot(t, at, lo=0, hi=16):
         return R("w%d" % (t % 2), 48 * lo + at, 48 * (hi - 1) + at + 1, 48)
-    sOWN, sDUM, sPAR, sCX, sX, sY = 31, 37, 49, 55, 61, 95
+    sPAR, sCX, sX, sY, sDUM = 37, 49, 61, 62, 77
     iota(R("pc", 0, 1), [[0, 1]], 0, 1)
     iota(R("i0"), [[0, 16], [1, 16]], 0, 0)
     iota(R("i1"), [[1, 16], [0, 16]], 0, 0)
     iota(R("pm"), [[1, 152]], -15, -1)
     iota(R("gh"), [[1, 16], [0, 8]], 0, 0)
     iota(R("pq"), [[1, 152]], -15, 0)
-    iota(R("ecol"), [[-1, DS]], DS, 0)
     ts(R("pc2", 0, 1), R("pc", 0, 1), 15, A.bitwise_and)
     ts(R("pc2", 1, 2), R("pc", 0, 1), 4, A.logical_shift_right)
     ms(R("ones"), 1.0)
     cp(R("col", 0, 2), R("pc2", 0, 2))
-    ms(R("m14"), -14.0)
     ms(R("agt", W, 1936), REST)
     ms(R("mp", 0, 2048, 8), -4096.0)
     for j in range(1, 8):
@@ -247,9 +251,13 @@ def rank_program(g, core, T, topo):
     act(cNV0, OH(9), scale=-579.0, bias=-1158.0)
     act(cV0, OH(9), scale=579.0, bias=1158.0)
     act(cKI, OH(9), scale=1.0 / 6 - 0.25, bias=0.25)
-    act(cMANY, OH(9), scale=-564.0, bias=-1128.0)
-    act(cNMANY, OH(9), scale=564.0, bias=1128.0)
-    act(cHB, OH(3), scale=8 * U, bias=5.0 / 128)
+    act(cMANY, OH(9), scale=15.0, bias=30.0)
+    act(cNMANY, OH(9), scale=-15.0, bias=-30.0)
+    act(cVD, OH(9), scale=579.0, bias=1158.0 - 1792.0)
+    act(cVH, OH(9), scale=579.0, bias=1158.0 + 5.0 / 128)
+    act(cVL, OH(9), scale=579.0, bias=1158.0 - 0.5)
+    act(cHB, OH(3), scale=8 * U, bias=cVH)
+    act(R("md"), R("mi"), scale=cVD)
     act(cG2, cG, scale=2.0)
     act(cG21, cG, scale=2.0, bias=1.0)
     act(cG16, cG, scale=16.0)
@@ -261,7 +269,7 @@ def rank_program(g, core, T, topo):
         else:
             ts(R("dt", 256 * a, 256 * a + 256), R("uu"), C(cA + a), A.add)
     for h in range(4):
-        mm(P(3 + h, 0, 480), R("m14"), R("ones"), True, False)
+        mm(P(3 + h, 0, 480), R("md"), R("ones"), True, False)
         mm(P(3 + h, 0, 480), R("mi"), R("dt", 480 * h, 480 * h + 480), False, False)
     ts(cLO, cR, 7.5, A.is_lt)
     ts(cHI, cR, 7.5, A.is_gt)
@@ -272,7 +280,7 @@ def rank_program(g, core, T, topo):
 
     for h in range(4):
         lo, hi = 480 * h, 480 * h + 480
-        act(R("t1", lo, hi), R("vin", lo, hi), scale=cK, bias=cNV0)
+        act(R("t1", lo, hi), R("vin", lo, hi), scale=cK)
         mm(P(3 + h, 0, 480), R("mv"), R("vin", lo, hi), False, True)
         tt(R("ct", C0 + lo, C0 + hi), P(3 + h, 0, 480), R("t1", lo, hi), A.max)
     fill(R("hr"), R("i0", 0, 160), cHR)
@@ -286,7 +294,7 @@ def rank_program(g, core, T, topo):
     for j, (r, w) in enumerate(chain):
         act(C(cD + j), OH(r), scale=w, bias=C(cD + j - 1) if j else 0.0)
     cW2, cW = C(cD + 3), C(cD + 7)
-    act(cU, OH(4), scale=8192.0)
+    act(cU, OH(4), AF.Silu, scale=8192.0)
     fill(R("kb"), R("i0"), 1.0 / BASE)
     fill(R("zer"), R("i0"), 0.0)
     fill(R("geo"), R("i0", 0, 16), BASE)
@@ -311,19 +319,29 @@ def rank_program(g, core, T, topo):
     act(R("mh"), R("mi"))
     act(R("mu"), R("bm"), scale=cU)
     ms(R("d0"), 0.0)
-    ms(R("d0", 2, 128, 8), -1.0)
+    ms(R("b0", 0, 48, 3), HUGE)
+    ms(R("b0", 2, 48, 3), -HUGE)
+    act(R("dum"), R("i0", 0, 16), bias=cR16)
+    act(R("xs", 61, 782, 48), R("dum"), scale=-1.0, bias=-300.0)
+    fill(R("xs", 77, 798, 48), R("dum"), HUGE)
     ms(R("f0", 0, 48, 3), 0.0)
     ms(R("f0", 2, 48, 3), -1.0)
     ts(R("dy"), R("wl0"), R("s1", 15, 16), A.mult)
     add("v", lambda: V.reciprocal(ap(R("yq")), ap(R("dy"))), [R("dy")], [R("yq")])
     ts(R("f0", 1, 48, 3), R("yq"), -4000.0, A.mult)
     for t in range(2):
-        fill(R("w%d" % t, 31, 799, 6), R("i0", 0, 128), 0.0)
-        act(slot(t, sDUM), R("i0", 0, 16), bias=cR16)
+        fill(slot(t, 73), R("dum"), 0.0)
+        act(slot(t, sDUM), R("dum"), scale=-1.0)
         fill(slot(t, sY, 10, 16), R("i0", 0, 6), ZR)
     act(slot(1, sY, 0, 10), R("rin", 0, 10), scale=1.0 / 16, bias=C0 / 16.0)
     act(slot(0, sY, 0, 10), R("rin", 0, 10), scale=1.0 / 16, bias=C0 / 16.0)
     ms(R("nl"), 1.0)
+    ms(R("gz", 0, 10), 0.0)
+    ts(R("gz", 10, 16), R("dum", 0, 6), -DS / 16.0, A.add)
+    act(cNKI, cKI, scale=-1.0)
+    ms(R("two"), -2.0)
+    ms(R("outv", 0, C0), 0.0)
+    ms(R("outv", C0 + W, CTW), 0.0)
 
     def args(nl):
         act(R("gg", 0, nl), ind(AG, R("tn", 0, nl // 16)))
@@ -342,6 +360,8 @@ def rank_program(g, core, T, topo):
 
     def state(t):
         tt(R("wl"), R("wl0"), R("nl"), A.mult)
+        act(R("pz4"), R("nl"), scale=-10000.0, bias=9700.0)
+        tt(R("b0", 1, 48, 3), R("pz4"), slot(t, sY), A.subtract)
         act(R("pz"), R("nl"), scale=1024.0, bias=-1008.0)
         act(R("pz3"), R("nl"), scale=-4096.0, bias=4080.0)
         act(R("lim"), R("nl"), scale=9500.0, bias=-10000.0)
@@ -350,18 +370,17 @@ def rank_program(g, core, T, topo):
         tt(R("dy"), slot(t, sY), R("pz3"), A.add)
         tt(R("cur"), R("dy"), R("yq"), A.min)
 
-    def choose(nl, between):
+    def choose(nl):
         k, m, sc = nl // 16, nl // 2, SCUT[nl]
         cp(R("a0", 0, k), P(bL, 0, k))
-        act(R("sg", 0, sc), ind(CELLS, R("a0", 0, sc // 16)), AF.Sign, bias=cNMANY)
+        if sc:
+            act(R("sg", 0, sc), ind(CELLS, R("a0", 0, sc // 16)), AF.Sign, bias=cNMANY)
+            act(R("of", 0, sc // 2), P(bHI, 0, sc // 2), bias=2048.0)
         ts(R("sg", sc, nl), ind(CELLS, R("a0", sc // 16, k)), cMANY, A.is_gt, 2.0, A.mult)
-        act(R("of", 0, sc // 2), P(bHI, 0, sc // 2), bias=2048.0)
         act(R("of", sc // 2, m), P(bHI, sc // 2, m), bias=17 * 2048.0)
         mm(P(bLO, 0, m), R("blo"), R("sg", 0, nl, 2), False, False)
         mm(P(bLO, 0, m), R("bhi"), R("sg", 1, nl, 2), False, True)
-        between()
-        act(R("pp", 0, nl), ind(CELLS, R("tn", 0, k)))
-        act(R("sv", 0, nl), ind(CELLS, R("a0", 0, k)))
+        act(R("sv", 0, nl), ind(CELLS, R("a0", 0, k)), bias=cNV0)
         for lo, hi in ([(m // 2, m), (0, m // 2)] if HALVES == 2 else [(0, m)]):
             tt(R("m1", lo, hi), P(bLO, lo, hi), R("of", lo, hi), A.max)
             ts(R("m2", lo, hi), R("m1", lo, hi), 2047, A.bitwise_and)
@@ -369,157 +388,174 @@ def rank_program(g, core, T, topo):
 
     def step(nl, t, last):
         k = nl // 16
-        h = 16 * (k // 2)
+        h = 0 if ONEF else 16 * (k // 2)
         wb = "w%d" % (t % 2)
-        mm(P(bF0, 0, h), R("mi"), R("thr", 0, h), True, False)
+        if h:
+            mm(P(bF0, 0, h), R("mi"), R("thr", 0, h), True, False)
         mm(P(bF1, h, nl), R("mi"), R("thr", h, nl), True, False)
         mm(P(bR, 0, nl), R("mn"), R("sv", 0, nl), True, False)
+        act(R("pp", 0, nl), ind(CELLS, R("tn", 0, k)), bias=cNV0)
         for r in range(16):
             mm(P(bL, 16, 16 + k), R("zd", 15 - r, 143 - r), R("pp", r, nl, 16), r == 0, r == 15)
         tt(slot(t, sPAR, 0, k), P(bL, 16, 16 + k), slot(t - 1, sY, 0, k), A.subtract)
-        tt(slot(t, sOWN, 0, k), slot(t - 1, sY, 0, k), slot(t, sDUM, 0, k), A.subtract)
         at, hi = 0, nl
-        for lo, cut in PIECES[nl]:
-            for e, a, b in ((act, lo, cut), (cp, cut, hi)):
+        for i, (lo, cut) in enumerate(PIECES[nl]):
+            bM, bX = DEC[i % len(DEC)]
+            for e, a, b in (("s", lo, cut), ("v", cut, hi)):
                 if a < b:
-                    e(R("vv", 8 * a, 8 * b), ind(CELLS, R("ol", a // 2, b // 2)))
+                    if e == "s":
+                        act(R("vv", 8 * a, 8 * b), ind(CELLS, R("ol", a // 2, b // 2)), bias=cNV0)
+                    else:
+                        ts(R("vv", 8 * a, 8 * b), ind(CELLS, R("ol", a // 2, b // 2)), cNV0, A.add)
                     scan(R("rr", 8 * a, 8 * b), R("mp", 0, 8 * (b - a)), R("vv", 8 * a, 8 * b))
             RR = R("rr", 8 * lo + 7, 8 * hi, 8)
             mm(P(bM, lo, hi), R("mi"), R("mkx", lo, hi), True, False)
             mm(P(bM, lo, hi), R("dec"), RR, False, True)
             mm(P(bX, lo, hi), R("dec"), RR, True, True)
-            scan(R("xs", lo, hi), R("pat2", lo, hi), P(bM, lo, hi), FLOOR, A.min, A.max)
+            scan(R("xs", 3 * lo, 3 * hi, 3), R("pat2", lo, hi), P(bM, lo, hi), FLOOR, A.min, A.max)
             act(R("xu", lo, hi), P(bX, lo, hi), AF.Relu, bias=-16.0)
             for j in range(hi // 16 - 1, lo // 16 - 1, -1):
                 w = nl - 16 * j
-                ts(R("ee", at, at + w), R("xu", 16 * j, nl), R("xs", 16 * j + 15, 16 * j + 16), A.is_equal, R("wl", j, j + 1), A.mult)
+                ts(R("ee", at, at + w), R("xu", 16 * j, nl), R("xs", 48 * j + 45, 48 * j + 46), A.is_equal, R("wl", j, j + 1), A.mult)
                 if 16 * j < h:
                     mm(P(bF1, h, nl), R("bw"), R("ee", at + h - 16 * j, at + w), False, j == 0)
                     mm(P(bF0, 16 * j, h), R("bw"), R("ee", at, at + h - 16 * j), False, j == 0)
                 else:
-                    mm(P(bF1, 16 * j, nl), R("bw"), R("ee", at, at + w), False, False)
+                    mm(P(bF1, 16 * j, nl), R("bw"), R("ee", at, at + w), False, j == 0)
                 at += w
             hi = lo
         RR = R("rr", 7, 8 * nl, 8)
-        act(R("rp", 0, nl), RR, AF.Relu, bias=0.25)
-        mm(P(bR, 0, nl), R("mh"), RR, False, False)
-        mm(P(bR, 0, nl), R("mu"), R("rp", 0, nl), False, True)
-        act(R("tr", 0, nl), P(bR, 0, nl), AF.Relu)
-        act(R("ww", 0, nl), R("tr", 0, nl), AF.Relu, bias=cV0, scale=-1.0)
-        XS = R("xs", 15, nl, 16)
+        final = t == ROUNDS * STEPS - 1
+        mm(P(bR, 0, nl), R("mh"), RR, False, True)
+        scan(R("bo", 0, 3 * k), R("b0", 0, 3 * k), R("xs", 45, 45 + 48 * k, 16), 0.0, A.max, A.min)
+        if final:
+            act(R("rp", 0, nl), RR, AF.Relu, bias=0.25)
+            act(R("tr", 0, nl), P(bR, 0, nl), AF.Relu)
+            mm(P(bR, 0, nl), R("mn"), R("tr", 0, nl), True, False)
+            mm(P(bR, 0, nl), R("mu"), R("rp", 0, nl), False, True)
+            act(R("sg", 0, nl), P(bR, 0, nl), AF.Relu, bias=2.0, scale=cNKI)
+            ts(slot(t, sDUM), R("bo", 1, 3 * k, 3), 300.0, A.add)
+        else:
+            act(R("ww", 0, nl), P(bR, 0, nl), AF.Relu)
+            ts(R("tb", 0, k), R("bo", 1, 3 * k, 3), -16.0, A.mult, 4800.0, A.subtract)
+            act(ind(CT, R("tb", 0, k)), R("ww", 0, nl), AF.Silu)
+        XS = R("xs", 45, 48 * k, 48)
         tt(slot(t, sX, 0, k), XS, R("pz", 0, k), A.add)
         tt(slot(t, sCX, 0, k), R("cur", 0, k), XS, A.subtract)
-        tt(R("d0", 1, 8 * k, 8), XS, R("lim", 0, k), A.is_lt)
-        tt(R("d0", 4, 8 * k, 8), XS, R("lim", 0, k), A.is_lt)
-        tt(R("d0", 5, 8 * k, 8), XS, R("lim2", 0, k), A.is_lt)
-        scan(R(wb, 65, 65 + 48 * k, 6), R("d0", 0, 8 * k), R(wb, 31, 31 + 48 * k, 6), 0.0, A.mult, A.add)
+        tt(R("d0", 1, 4 * k, 4), XS, R("lim", 0, k), A.is_lt)
+        tt(R("d0", 2, 4 * k, 4), XS, R("lim2", 0, k), A.is_lt)
+        scan(R(wb, 38, 38 + 48 * k, 12), R("d0", 0, 4 * k), R(wb, 37, 37 + 48 * k, 12), 0.0, A.mult, A.add)
         if not last:
             ts(R("tn", 0, k), slot(t, sY, 0, k), 16.0, A.mult, float(C0), A.subtract)
             args(nl)
             lists(nl)
+            choose(nl)
+        elif not final:
+            before(t // STEPS, t)
         scan(R(wb, 3 * h, 3 * nl, 3), R("pat", h, nl), P(bF1, h, nl))
-        scan(R(wb, 0, 3 * h, 3), R("pat", 0, h), P(bF0, 0, h))
+        if h:
+            scan(R(wb, 0, 3 * h, 3), R("pat", 0, h), P(bF0, 0, h))
         scan(R("fo", 0, 3 * k), R("f0", 0, 3 * k), R(wb, 45, 45 + 48 * k, 16), 0.0, A.mult, A.min)
         ts(R("th", 0, k), R("fo", 2, 3 * k, 3), -16.0, A.mult)
-        tt(ind(CT, R("th", 0, k)), R("dc%d" % (t % 2), 0, nl), R("ww", 0, nl), A.subtract)
+        if final:
+            for lo, hi in zip(CUTS, CUTS[1:]):
+                act(R("ab", lo, hi), R("ct", C0 + lo, C0 + hi), AF.Abs, bias=-144.0, scale=cKI)
+                ts(R("outv", C0 + lo, C0 + hi), R("ab", lo, hi), -1.0, A.mult, 144.0, A.add)
+            tt(ind(R("outv"), R("th", 0, k)), R("sg", 0, nl), R("two"), A.add)
+        else:
+            cp(ind(CT, R("th", 0, k)), R("dc%d" % (t % 2), 0, nl))
 
     def kept(nl, t):
         k = nl // 16
-        tt(R("nl", 0, k), R("fo", 1, 3 * k, 3), slot(t, sX, 0, k), A.is_equal)
+        act(R("xm", 0, k), slot(t, sX, 0, k), bias=-(DS + C0 - 0.5) / 16)
+        tt(R("nl", 0, k), R("fo", 1, 3 * k, 3), R("xm", 0, k), A.is_ge)
 
-    def back(nl, t, out):
-        kept(nl, t)
-        tt(R("dy"), slot(t, sY), slot(t - 1, sY), A.subtract)
-        tt(R("yq"), R("dy"), R("nl"), A.mult)
-        tt(out, slot(t - 1, sY), R("yq"), A.add)
+    SI, EX = R("ct", C0, C0 + DS), R("ct", C0 + W - DS, C0 + W)
+    peers = [T.cores[(rank + d) % 4] for d in range(1, 4)]
+    masks, used = {}, []
+    for j in sorted(range(3), key=lambda j: len(topo.engines(core, peers[j]))):
+        es = [e for e in topo.engines(core, peers[j]) if e not in used][:ENG]
+        used += es
+        masks[j] = sum(1 << e for e in es)
 
-    def exchange(x, nl, t):
-        stg, land = "stg%d" % x, "land%d" % x
-        b = C0 + W - DS
-        SI, EX = R("ct", C0, C0 + DS), R("ct", b, b + DS)
-        ts(R(stg, 0, 192, 2), SI, 0.0, A.is_gt)
-        act(R(stg, 1, 64, 2), R("ct", b + 2 * S, b + 3 * S), bias=1.0 / 16)
-        act(R(stg, 65, 128, 2), R("ct", b + S, b + 2 * S), bias=1.0 / 16)
-        ts(R(stg, 129, 192, 2), R("ct", b, b + S), 1.0 / 16, A.add)
-        peers = [T.cores[(rank + d) % 4] for d in range(1, 4)]
-        masks, used = {}, []
-        for j in sorted(range(3), key=lambda j: len(topo.engines(core, peers[j]))):
-            es = [e for e in topo.engines(core, peers[j]) if e not in used][:ENG]
-            used += es
-            masks[j] = sum(1 << e for e in es)
-
-        def send():
+    def send(x, blocks):
+        def call():
             tr = []
-            for j in range(3):
+            for j, b in enumerate(blocks):
                 rid, pid = topo.addr(peers[j], core)
                 tr.append(RemoteDMATransfer(dst_ids=[DstId(rid=rid, pnc=pid)], dma_engine_mask=masks[j], remote_sem=T.sem["arr%d" % x],
-                                            src=ap(R(stg, 64 * j, 64 * j + 64)), dst=ap(R(land, 64 * j, 64 * j + 64))))
+                                            src=ap(R("stg%d" % x, S * b, S * b + S)), dst=ap(R("land%d" % x, S * b, S * b + S))))
             return g.remote_dma_fused(tr, local_sem=T.sem["snt%d" % x])
-        add("g", send, [R(stg)], [], kind="r")
-        back(nl, t, slot(t, sY))
-        ms(R("nl"), 1.0)
-        ts(R("ta"), EX, -0.5, A.is_gt)
-        ts(R("tb"), EX, 0.0, A.is_gt)
-        tt(R("te"), R("ta"), R("tb"), A.subtract)
-        tt(R("tm"), R("te"), R("dg", 0, DS), A.mult)
-        ts(R("x2"), EX, -1.0, A.mult, cHR, A.add)
-        tt(R("x3"), R("tm"), R("ecol"), A.mult)
-        ts(R("hm"), SI, 0.0, A.is_gt)
-        scan(R("x4"), R("pat", 0, DS), R("x3"))
-        tt(R("dif"), R("te"), R("x2"), A.mult)
-        ts(R("s3", 0, 6), R("x4", 15, DS, 16), -1.0 / 16, A.mult)
-        tt(slot(t, sY, 10, 16), slot(t, sY, 10, 16), R("s3", 0, 6), A.add)
+        add("g", call, [R("stg%d" % x)], [], kind="r", ext=x)
+
+    def arrived(x):
+        add("v", None, [], [R("land%d" % x)], kind="w", ext=x)
+        return R("land%d" % x)
+
+    def before(x, t):
+        act(R("stg%d" % (2 * x)), EX, scale=LIFT)
+        send(2 * x, (2, 1, 0))
+        ts(R("s3"), slot(t, sY), ZR, A.is_equal)
+        tt(R("s2"), R("s3"), R("gz"), A.mult)
+        act(R("s1"), R("s3"), scale=ZR)
+        tt(slot(t, sY), slot(t, sY), R("s2"), A.add)
+        tt(slot(t - 1, sY), slot(t - 1, sY), R("s1"), A.max)
         ts(R("tn"), slot(t, sY), 16.0, A.mult, float(C0), A.subtract)
         args(L)
         lists(L)
-        digits(L, "dc%d" % (1 - t % 2))
-        add("v", None, [], [R(land)], kind="w", ext=("arr%d" % x, 3 * ENG))
-        ASK = R(land, 0, 192, 2)
-        for j in range(3):
-            tt(R("x1", (2 - j) * S, (3 - j) * S), R(land, 64 * j + 1, 64 * j + 64, 2), R("hm", (2 - j) * S, (3 - j) * S), A.mult)
-        tt(SI, SI, R("x1"), A.min)
 
-        def late():
-            tt(R("x2"), ASK, R("dif"), A.mult)
-            tt(R("x3"), R("tm"), ASK, A.is_gt)
-            tt(EX, EX, R("x2"), A.add)
-            scan(R("x4"), R("pat", 0, DS), R("x3"))
-            ts(R("nl", 10, 16), R("x4", 15, DS, 16), 0.5, A.is_lt)
-            state(t)
-        return late
+    def exchange(x, nl, t):
+        ts(R("stg%d" % (2 * x + 1)), SI, cV0, A.is_gt)
+        send(2 * x + 1, (0, 1, 2))
+        kept(nl, t)
+        tt(R("s2", 10, 16), R("nl", 10, 16), R("s3", 10, 16), A.subtract)
+        ts(R("ta"), EX, cVL, A.is_gt)
+        ts(R("tc"), EX, cV0, A.is_gt)
+        tt(R("te"), R("ta"), R("tc"), A.subtract)
+        tt(R("tm"), R("te"), R("dg", 0, DS), A.mult)
+        ts(R("x2"), EX, -1.0, A.mult, cHR, A.add)
+        ts(R("hm"), SI, cV0, A.is_le, 4096.0, A.mult)
+        tt(R("dif"), R("te"), R("x2"), A.mult)
+        digits(L, "dc%d" % (1 - t % 2))
+        tt(R("x1"), arrived(2 * x), R("hm"), A.add)
+        tt(SI, SI, R("x1"), A.min)
+        choose(L)
+        ASK = arrived(2 * x + 1)
+        tt(R("x2"), ASK, R("dif"), A.mult)
+        tt(R("x3"), R("tm"), ASK, A.mult)
+        tt(EX, EX, R("x2"), A.add)
+        scan(R("x4"), R("pat", 0, DS), R("x3"))
+        tt(R("nl", 10, 16), R("x4", 15, DS, 16), R("s2", 10, 16), A.add)
+        state(t)
 
     args(OWN)
     lists(OWN)
     digits(OWN, "dc0")
+    choose(OWN)
+    state(-1)
     t = 0
-    between = lambda: state(-1)
     for rnd in range(ROUNDS):
         nl = OWN if rnd == 0 else L
         for st in range(STEPS):
-            choose(nl, between)
             step(nl, t, st == STEPS - 1)
             if st < STEPS - 1:
                 digits(nl, "dc%d" % (1 - t % 2))
-
-                def between(nl=nl, t=t):
-                    kept(nl, t)
-                    state(t)
+                kept(nl, t)
+                state(t)
             elif rnd < ROUNDS - 1:
-                between = exchange(rnd, nl, t)
+                exchange(rnd, nl, t)
             t += 1
 
-    back(L, t - 1, R("cur"))
-    ts(R("s2"), R("cur"), ZR, A.is_equal, -float(REST + 1), A.mult)
-    ts(R("s3"), R("cur"), 16.0, A.mult, float(C0), A.subtract)
-    tt(R("yo"), R("s2"), R("s3"), A.add)
+    for z, a, b, c in ((slot(t - 2, sY), "s1", "s2", "yq"), (slot(t - 1, sY), "s3", "geo", "dy")):
+        ts(R(a), z, ZR, A.is_equal, -float(REST + 1), A.mult)
+        act(R(b), z, scale=16.0, bias=-float(C0))
+        tt(R(c), R(a), R(b), A.add)
+    kept(L, t - 1)
+    tt(R("pz"), R("dy"), R("yq"), A.subtract)
+    tt(R("lim"), R("pz"), R("nl"), A.mult)
+    tt(R("yo"), R("yq"), R("lim"), A.add)
     store("y", T.ya[:, :], R("yo"))
-
-    def out(lo, hi):
-        act(R("ab", lo, hi), R("ct", C0 + lo, C0 + hi), AF.Abs, bias=145.5, scale=cKI)
-        ts(R("outv", lo, hi), R("ab", lo, hi), -1.0, A.mult, 144.0, A.add)
-        store("y", T.yv[:, lo:hi], R("outv", lo, hi))
-    for lo, hi in zip(CUTS, CUTS[1:]):
-        out(lo, hi)
+    store("s", T.yv[:, :], R("outv", C0, C0 + W))
 
     ops[:] = arrange(ops)
     known = {e: 0 for e in Q}
@@ -542,7 +578,7 @@ def rank_program(g, core, T, topo):
         for j in waits[i]:
             q.wait_ge(T.sem[tok[j][0]], tok[j][1])
         if o["k"] == "w":
-            q.wait_ge(T.sem[o["ext"][0]], o["ext"][1])
+            q.wait_ge(T.sem["arr%d" % o["ext"]], 3 * ENG)
             continue
         ins = o["fn"]()
         if o["k"] == "d" or i in need:
@@ -555,5 +591,5 @@ def rank_program(g, core, T, topo):
     for i, o in enumerate(ops):
         if o["k"] == "d" and i not in need:
             g.sync.wait_ge(T.sem[tok[i][0]], 16)
-    for x in range(ROUNDS - 1):
+    for x in range(2 * ROUNDS - 2):
         g.wait_ge(T.sem["snt%d" % x], 3 * ENG)

@@ -8,40 +8,45 @@ L = OWN + DS
 REST = W
 C0 = 256
 CTW = C0 + W + 16
-U = 1.0 / 1024
+U = 1.0 / 64
 BASE, THR0, W0 = 256.0 / 150.0, 2.56, 1.0e25
-HUGE, FLOOR = 1.0e29, -512.0
-FIX, PEF, GATH, SCAT, ONEF = 0, 0.5, 1.56, 3.8, False
-WAKE, SAME = 220, 220
-ENG = 4
-PIECES = {OWN: ((96, 128), (32, 64), (0, 32)), L: ((160, 208), (64, 128), (0, 48))}
-SCUT = {OWN: 0, L: 0}
+HUGE, FLOOR = 1.0e29, -2048.0
 LIFT = 1.002
-HALVES = 2
+ENG = 4
+PIECES = {OWN: ((80, 120), (0, 48)), L: ((160, 208), (64, 128), (0, 48))}
+DECODE = {OWN: (80, 0), L: (160, 64, 0)}
 CUTS = [0, 256, 704, 1152, 1600, W]
+A0PE, TWOF, HOLEV, OFV, SVLATE = True, False, False, False, True
+OLDSEL, PPLATE, SCANF, SAME, COLF = True, True, 3, 220, False
+AFIX, PFIX, GGV, T1S = 0, 6, False, (0, 1, 2, 3)
+BFC, SGA, XHS, OUTS, YAF = True, 128, (0, 64, 80, 160), (), 800
+SUMS = ()
+WAKE, PEF, GATH, SCAT, DFIX, DCOL, RFIX, PASSES = 230, 0.55, 1.5, 3.5, 1000, 0.7, 2400, 2
 
 F, H, B, I, U16 = "float32", "float16", "bfloat16", "int32", "uint16"
 SB = {}
-for _t, _l in ((I, "agt 1936 rin 16 pc 8 pc2 8 m1 128 m2 128"),
+for _t, _l in ((I, "agt 1936 rin 16 pc 16 pc2 24 n0 264 n1 264"),
                (U16, "tn 16 th 16 tb 16 a0 16 ol 128"),
-               (H, "bl 152 bh 152 zx 152 zd 152 gg 256 mh 128 mn 128 mu 128 dec 128 mp 2048 vv 2048 rr 2048 rp 256 sv 256 pp 256 xu 256 tr 256 "
-                   "t1 1920 stg0 96 stg1 96 stg2 96 stg3 96 land0 96 land1 96 land2 96 land3 96 hm 96 x1 96 ta 96 tc 96 te 96 tm 96 x3 96 ones 480 md 128"),
-               (F, "ct %d col 40 gz 16 xm 16 pz4 16 dum 16 b0 48 bo 48 oh 16 geo 16 s1 16 s2 16 s3 16 wl0 16 wl 16 pz 16 pz3 16 lim 16 lim2 16 nl 16 cur 16 yq 16 dy 16 yo 16 of 128 xs 848 "
-                   "w0 848 w1 848 d0 128 f0 48 fo 48 dc0 256 dc1 256 ww 256 hr 160 dif 96 x2 96 x4 96" % CTW),
-               (B, "vin 1920 dt 2048 ab 1920 outv 2192 two 256 i0 256 i1 256 pm 152 gh 128 kb 256 zer 256 uu 256 u1 256 mi 128 mv 128 "
-                   "bw 128 pq 152 blo 128 bhi 128 dg 256 bm 128 pat 256 pat2 256 mk 256 mkx 256 thr0 256 thr 256 sg 256 ee 2176")):
+               (H, "bl 152 bh 152 zd 152 zx 152 gg 256 mh 128 mn 128 mu 128 dec 128 mp 768 vv 2048 rr 2048 rp 256 sv 256 pp 256 xu 256 tr 256 "
+                   "t1 1920 stg0 96 stg1 96 stg2 96 stg3 96 land0 96 land1 96 land2 96 land3 96 hm 96 x1 96 ta 96 tc 96 te 96 tm 96 x3 96 "
+                   "md 128 bd0 128 bd1 128 row0 128"),
+               (F, "ct %d col 48 gz 16 pa 48 xm 16 pz4 16 dum 16 b0 48 bo 48 oh 16 geo 16 s1 16 s2 16 s3 16 wl0 16 wl 16 pz 16 pz3 16 lim 16 "
+                   "lim2 16 nl 16 cur 16 yq 16 dy 16 yo 16 m1 256 xs 848 w0 848 w1 848 d0 64 f0 48 fo 48 dc0 256 dc1 256 ww 256 hr 160 "
+                   "dif 96 x2 96 x4 96 wj 16 of 128" % CTW),
+               (B, "vin 1920 dt 2048 ab 1920 outv %d two 256 big 256 c32 256 i0 256 i1 128 pm 152 gh 128 kb 256 zer 256 uu 256 u1 256 mi 128 "
+                   "hib 8 xh 16 xl 16 bwj 2048 mk4 128 bw 128 pq 152 blo 128 bhi 128 dg 256 bm 128 pat 256 pat2 256 mk 256 thr0 256 thr 256 sg 256 ee 2176" % CTW)):
     _w = _l.split()
     for _k in range(0, len(_w), 2):
         SB[_w[_k]] = (int(_w[_k + 1]), _t)
-SCRATCH = {k: ("sbuf", [128, v[0]], v[1]) for k, v in SB.items()}
+SCRATCH = {k: ("sbuf", [128, v[0]], v[1]) for k, v in SB.items() if not (OLDSEL and k in ("bd0", "bd1", "lim2", "big", "c32"))}
 for _k in range(8):
     SCRATCH["pb%d" % _k] = ("psum", [128, 512], F)
-POOL = {"v": 44, "s": 30, "p": 30, "g": 8, "d": 8}
+POOL = {"v": 44, "s": 30, "p": 30, "g": 10, "d": 8}
 SEMAPHORES = ["%s%d" % (e, k) for e in POOL for k in range(POOL[e])] + [w + str(k) for w in ("arr", "snt") for k in range(4)]
 A = AluOpType
 AF = ActivationFunctionType
 ID = AF.Identity
-bL, bLO, bHI, bF0, bF1, bR = 0, 1, 2, 5, 6, 7
+bL, bLO, bHI, bA, bF, bR = 0, 1, 2, 5, 6, 7
 DEC = ((3, 4), (1, 2))
 
 
@@ -53,8 +58,8 @@ def C(k):
     return ("col", k, k + 1, 1)
 
 
-def P(k, lo, hi):
-    return ("pb%d" % k, lo, hi, 1)
+def P(k, lo, hi, step=1):
+    return ("pb%d" % k, lo, hi, step)
 
 
 def ind(win, off):
@@ -72,9 +77,11 @@ def width(x):
 def cycles(eng, kind, ins, outs, both):
     if kind == "d":
         x = (outs or ins)[0]
-        return 50, 1300 + 0.85 * width(x) * (1 if SB[x[0]][1] == B else 2)
+        if x[0] == "yo":
+            return 50, DFIX + YAF
+        return 50, DFIX + DCOL * width(x) * (1 if SB[x[0]][1] == B else 2)
     if kind != "c":
-        return (300, 2800) if kind == "r" else (0, 0)
+        return (300, RFIX) if kind == "r" else (0, 0)
     n = width(outs[0])
     sides = [x for x in ins + outs if isinstance(x, tuple)]
     if eng == "g":
@@ -84,13 +91,15 @@ def cycles(eng, kind, ins, outs, both):
     elif any(x[0] == "ind" for x in sides):
         c = 70 + GATH * n
     elif eng == "p":
-        c = max(64, n) * PEF
+        c = max(64, n) * PEF + PFIX
     elif eng != "v":
-        c = max(64, n) + FIX
-    elif both:
-        c = max(64, n if any(x[0][:2] == "pb" for x in sides[:2]) else 2 * n) + FIX
+        c = max(64, n) + AFIX
+    elif both == 3:
+        c = max(64, 2 * n if any(x[0][:2] == "pb" for x in sides) else n if any(SB[x[0]][1] == F for x in sides) else n / 2)
+    elif both == 1:
+        c = max(64, n if any(x[0][:2] == "pb" for x in sides[:2]) else 2 * n)
     else:
-        c = max(64, n if any(x[0][:2] == "pb" or (SB[x[0]][1] in (F, I) and width(x) == n) for x in sides) else n / 2) + FIX
+        c = max(64, (n if any(x[0][:2] == "pb" or (SB[x[0]][1] in (F, I) and (width(x) == n or not COLF)) for x in sides) else n / 2) * (both or 1))
     return c, c
 
 
@@ -123,25 +132,52 @@ def arrange(ops):
 
     def lag(j, i):
         if ops[i]["k"] == "d" and ops[j]["k"] == "d":
-            return ops[j]["c"][1] - 1300
+            return ops[j]["c"][1] - DFIX
         return ops[j]["c"][1] + (0 if not deps[i][j] or ops[j]["k"] == "w" else SAME if ops[i]["e"] == ops[j]["e"] else WAKE)
+    n = range(len(ops))
     rest = [o["c"][1] for o in ops]
-    for i in range(len(ops) - 1, -1, -1):
+    after = [[] for _ in ops]
+    for i in reversed(n):
         for j in deps[i]:
             rest[j] = max(rest[j], lag(j, i) + rest[i])
-    rest = [r + (1e9 if o["k"] == "d" and o["w"] else 0) for r, o in zip(rest, ops)]
-    start, busy = {}, {}
-    for i in sorted(range(len(ops)), key=lambda i: (-rest[i], i)):
-        t, c = max([start[j] + lag(j, i) for j in deps[i]] + [0]), ops[i]["c"][0]
-        q = busy.setdefault(ops[i]["e"], [])
-        at = 0
-        for at in range(len(q) + 1):
-            if at == len(q) or t + c <= q[at][0]:
-                break
-            t = max(t, q[at][1])
-        q.insert(at, (t, t + c))
-        start[i] = t
-    return [ops[i] for i in sorted(range(len(ops)), key=lambda i: (start[i], i))]
+            after[j].append(i)
+
+    def place(order, earliest):
+        start, busy = {}, {}
+        for i in order:
+            t, c = earliest(i, start), ops[i]["c"][0]
+            q = busy.setdefault(ops[i]["e"], [])
+            at = max(bisect(q, t) - 1, 0)
+            while at < len(q) and t + c > q[at][0]:
+                t = max(t, q[at][1])
+                at += 1
+            q.insert(at, (t, t + c))
+            start[i] = t
+        return start
+
+    def forward(i, start):
+        return max([start[j] + lag(j, i) for j in deps[i]] + [0])
+
+    def backward(j, end):
+        c = ops[j]["c"]
+        return max([end[i] + ops[i]["c"][0] + lag(j, i) - c[0] for i in after[j]] + [c[1] - c[0]])
+    first = [1e9 if o["k"] == "d" and o["w"] else 0 for o in ops]
+    start = place(sorted(n, key=lambda i: (-rest[i] - first[i], i)), forward)
+    for _ in range(PASSES):
+        end = place(sorted(n, key=lambda i: (-start[i], -i)), backward)
+        start = place(sorted(n, key=lambda i: (-end[i] - ops[i]["c"][0] - first[i], i)), forward)
+    return [ops[i] for i in sorted(n, key=lambda i: (start[i], i))]
+
+
+def bisect(q, t):
+    lo, hi = 0, len(q)
+    while lo < hi:
+        mid = (lo + hi) // 2
+        if q[mid][0] <= t:
+            lo = mid + 1
+        else:
+            hi = mid
+    return lo
 
 
 def rank_program(g, core, T, topo):
@@ -183,7 +219,7 @@ def rank_program(g, core, T, topo):
         add("v", lambda: V.memset(ap(out), c), [], [out])
 
     def scan(out, d0, d1, init=0.0, op0=A.add, op1=A.max):
-        add("v", lambda: V.tensor_tensor_scan(ap(out), ap(d0), ap(d1), init, op0, op1), [d0, d1], [out])
+        add("v", lambda: V.tensor_tensor_scan(ap(out), ap(d0), ap(d1), init, op0, op1), [d0, d1], [out], both=SCANF)
 
     def act(out, a, f=ID, bias=0.0, scale=1.0):
         if out[0] == "ind":
@@ -213,7 +249,7 @@ def rank_program(g, core, T, topo):
     load("y", R("vin"), T.vals[:, :])
     load("y", R("agt", 0, W), T.ag[:, :])
 
-    cR, cG, cLO, cHI, cHB, cHR, cG2, cG21, cG16, cU, cR16, cK, cKI, cV0, cNV0, cMANY, cNMANY, cNKI, cVD, cVH, cVL = [C(k) for k in range(21)]
+    cR, cG, cLO, cHI, cHB, cHR, cG2, cG21, cG16, cU, cR16, cK, cKI, cV0, cNV0, cMANY, cVK, cNKI, cVD, cVH, cVL, cPP, cBIT = [C(k) for k in range(23)]
     cA, cD = 24, 32
     CT, CELLS, AG, DT = R("ct"), R("ct", C0, CTW), R("agt"), R("dt")
     ZR = (REST + C0) / 16.0
@@ -223,66 +259,77 @@ def rank_program(g, core, T, topo):
 
     def slot(t, at, lo=0, hi=16):
         return R("w%d" % (t % 2), 48 * lo + at, 48 * (hi - 1) + at + 1, 48)
-    sPAR, sCX, sX, sY, sDUM = 37, 49, 61, 62, 77
-    iota(R("pc", 0, 1), [[0, 1]], 0, 1)
-    iota(R("i0"), [[0, 16], [1, 16]], 0, 0)
-    iota(R("i1"), [[1, 16], [0, 16]], 0, 0)
+    sPAR, sCX, sX, sBACK, sRAW, sY, sDUM = 37, 49, 61, 73, 74, 65, 77
+    iota(R("pc"), [[-1, 16]], 16, 1)
+    iota(R("i0", 0, 16), [[1, 16]], 0, 0)
+    iota(R("n0", 0, 256), [[1, 256]], 0, 0)
+    iota(R("n0", 256, 264), [[256, 8]], 0, 0)
     iota(R("pm"), [[1, 152]], -15, -1)
+    iota(R("i0", 16, 256), [[0, 15], [1, 16]], 0, 0)
     iota(R("gh"), [[1, 16], [0, 8]], 0, 0)
+    iota(R("i1"), [[1, 8], [0, 16]], 0, 0)
     iota(R("pq"), [[1, 152]], -15, 0)
-    ts(R("pc2", 0, 1), R("pc", 0, 1), 15, A.bitwise_and)
-    ts(R("pc2", 1, 2), R("pc", 0, 1), 4, A.logical_shift_right)
-    ms(R("ones"), 1.0)
-    cp(R("col", 0, 2), R("pc2", 0, 2))
+    ts(R("pc2", 0, 16), R("pc"), 15, A.bitwise_and)
+    ts(R("pc2", 16, 17), R("pc", 0, 1), 4, A.logical_shift_right)
+    cp(cR, R("pc2", 0, 1))
+    ts(cG, R("pc2", 16, 17), -1.0, A.add)
     ms(R("agt", W, 1936), REST)
-    ms(R("mp", 0, 2048, 8), -4096.0)
-    for j in range(1, 8):
-        ms(R("mp", j, 2048, 8), 1.0 / 16)
-    ts(R("oh"), R("i0", 0, 16), cR, A.is_equal)
-    ts(R("uu"), R("i0"), OH(0), A.mult, U, A.mult)
-    ts(R("s3", 0, 8), R("i0", 1, 9), OH(2), A.mult, U, A.mult)
-    ts(R("u1"), R("i1"), OH(1), A.mult, U, A.mult)
-    ts(R("col", cA, cA + 8), R("s3", 0, 8), -1.0 / 32, A.add)
-    tt(R("uu"), R("uu"), R("u1"), A.add)
+    ms(R("mp"), 1.0 / 16)
+    ms(R("mp", 0, 768, 8), -4096.0)
+    ts(R("oh"), R("pc2", 0, 16), 0.0, A.is_equal)
+    ms(R("pa", 0, 16), 2.0)
+    ms(R("pa", 16, 32), 0.5)
+    scan(R("s2"), R("pa", 0, 16), R("oh"), 0.0, A.mult, A.add)
+    scan(R("s3"), R("pa", 16, 32), R("oh"), 0.0, A.mult, A.add)
+    ts(R("n1"), R("n0"), R("s2", 10, 11), A.mult)
+    ts(R("n0"), R("n1"), 10, A.logical_shift_right, 1, A.bitwise_and)
+    ts(R("uu"), R("n0", 0, 256), U, A.mult)
+    ts(R("hib"), R("n0", 256, 264), U, A.mult, -1.0 / 32, A.add)
     ts(R("mi"), R("pm", 15, 143), 0.0, A.is_equal)
     fill(R("ct", 0, C0), R("i0"), 0.0)
     fill(R("ct", C0 + W, CTW), R("i0", 0, 16), 0.0)
-    act(cK, OH(9), scale=2.0, bias=4.0)
-    act(cNV0, OH(9), scale=-579.0, bias=-1158.0)
-    act(cV0, OH(9), scale=579.0, bias=1158.0)
-    act(cKI, OH(9), scale=1.0 / 6 - 0.25, bias=0.25)
-    act(cMANY, OH(9), scale=15.0, bias=30.0)
-    act(cNMANY, OH(9), scale=-15.0, bias=-30.0)
-    act(cVD, OH(9), scale=579.0, bias=1158.0 - 1792.0)
-    act(cVH, OH(9), scale=579.0, bias=1158.0 + 5.0 / 128)
-    act(cVL, OH(9), scale=579.0, bias=1158.0 - 0.5)
-    act(cHB, OH(3), scale=8 * U, bias=cVH)
-    act(R("md"), R("mi"), scale=cVD)
+    for c, k4, k6 in ((cK, 4, 6), (cV0, 1158, 1737), (cNV0, -1158, -1737), (cKI, 0.25, 1.0 / 6), (cNKI, -0.25, -1.0 / 6), (cMANY, 30, 45),
+                      (cVD, 1158 - 1792, 1737 - 1792), (cVH, 1158 + 5.0 / 128, 1737 + 5.0 / 128), (cVL, 1157.5, 1736.5), (cVK, 1162, 1743),
+                      (cPP, 16 - 1.0 / 128 - 1158, 16 - 1.0 / 128 - 1737)):
+        act(c, OH(15), scale=float(k6 - k4), bias=float(k4))
+    act(cHB, OH(11), scale=U, bias=cVH)
     act(cG2, cG, scale=2.0)
     act(cG21, cG, scale=2.0, bias=1.0)
     act(cG16, cG, scale=16.0)
     act(cR16, cR, scale=1.0 / 16)
-    act(R("mv"), R("mi"), scale=-1792.0)
+    act(R("mh"), R("mi"))
     for a in range(8):
         if a in (5, 6):
-            act(R("dt", 256 * a, 256 * a + 256), R("uu"), bias=C(cA + a))
+            act(R("dt", 256 * a, 256 * a + 256), R("uu"), bias=R("hib", a, a + 1))
         else:
-            ts(R("dt", 256 * a, 256 * a + 256), R("uu"), C(cA + a), A.add)
-    for h in range(4):
-        mm(P(3 + h, 0, 480), R("md"), R("ones"), True, False)
-        mm(P(3 + h, 0, 480), R("mi"), R("dt", 480 * h, 480 * h + 480), False, False)
+            ts(R("dt", 256 * a, 256 * a + 256), R("uu"), R("hib", a, a + 1), A.add)
     ts(cLO, cR, 7.5, A.is_lt)
     ts(cHI, cR, 7.5, A.is_gt)
     tt(cHR, R("dt", REST, REST + 1), cHB, A.add)
-    ts(R("zx"), R("pm"), 0.0, A.is_equal, OH(0), A.mult)
+    cHR2 = C(cA)
+    act(cHR2, cHR, scale=0.5)
     ms(R("tn", 10, 16), REST)
     cp(R("tn", 0, 10), R("rin", 0, 10))
 
+    act(R("md"), R("mi"), scale=cNV0)
+    if SUMS:
+        act(R("mk4"), R("mi"), scale=cK)
     for h in range(4):
         lo, hi = 480 * h, 480 * h + 480
-        act(R("t1", lo, hi), R("vin", lo, hi), scale=cK)
-        mm(P(3 + h, 0, 480), R("mv"), R("vin", lo, hi), False, True)
-        tt(R("ct", C0 + lo, C0 + hi), P(3 + h, 0, 480), R("t1", lo, hi), A.max)
+        if h in SUMS:
+            mm(P(3 + h, 0, 480), R("mk4"), R("vin", lo, hi), True, False)
+            ts(R("t1", lo, hi), R("vin", lo, hi), 0.0, A.is_lt, cVK, A.mult)
+            mm(P(3 + h, 0, 480), R("mh"), R("t1", lo, hi), False, False)
+            mm(P(3 + h, 0, 480), R("mi"), R("dt", lo, hi), False, True)
+            act(R("ct", C0 + lo, C0 + hi), P(3 + h, 0, 480))
+        else:
+            mm(P(3 + h, 0, 480), R("md"), R("vin", lo, hi), True, False)
+            mm(P(3 + h, 0, 480), R("mi"), R("dt", lo, hi), False, True)
+            if h in T1S:
+                act(R("t1", lo, hi), R("vin", lo, hi), scale=cK)
+            else:
+                ts(R("t1", lo, hi), R("vin", lo, hi), cK, A.mult)
+            tt(R("ct", C0 + lo, C0 + hi), P(3 + h, 0, 480), R("t1", lo, hi), A.max)
     fill(R("hr"), R("i0", 0, 160), cHR)
     act(R("ct", C0 + REST, C0 + REST + 1), cHR)
     cp(ind(CELLS, R("tn", 0, 10)), R("hr"))
@@ -290,15 +337,25 @@ def rank_program(g, core, T, topo):
     ts(R("bh"), R("pm"), 0.0, A.is_equal, cHI, A.mult)
     ts(R("blo"), R("gh"), cG2, A.is_equal, 2048.0, A.mult)
     ts(R("bhi"), R("gh"), cG21, A.is_equal, 2048.0, A.mult)
-    chain = ((0, 64.0), (1, 1024.0), (2, 16384.0), (4, -17472.0), (3, -32768.0), (4, 32768.0), (8, -32768.0), (9, 32768.0))
+    cNM = C(cA + 1)
+    act(cNM, cMANY, scale=-1.0)
+    if not OLDSEL:
+        tt(R("bd0"), R("bl", 15, 143), R("bh", 23, 151), A.subtract)
+        tt(R("bd1"), R("bl", 7, 135), R("bh", 15, 143), A.subtract)
+        fill(R("big", 0, 128), R("i0", 0, 128), 1.5 * 2 ** 23)
+        fill(R("big", 128, 256), R("i0", 0, 128), -1.5 * 2 ** 23)
+        ms(R("c32", 0, 256, 2), 0.0)
+        ms(R("c32", 1, 256, 2), -1.0 / 32)
+    chain = ((13, -8188.0), (12, 1.0), (12, 32767.0), (11, -32768.0), (14, -8192.0), (15, 8192.0))
+    act(cBIT, R("s3", 10, 11), scale=4096.0)
     for j, (r, w) in enumerate(chain):
-        act(C(cD + j), OH(r), scale=w, bias=C(cD + j - 1) if j else 0.0)
-    cW2, cW = C(cD + 3), C(cD + 7)
-    act(cU, OH(4), AF.Silu, scale=8192.0)
+        act(C(cD + j), OH(r), scale=w, bias=C(cD + j - 1) if j else cBIT)
+    cW2, cW = C(cD + 1), C(cD + 5)
+    act(cU, OH(13), AF.Silu, scale=8192.0)
     fill(R("kb"), R("i0"), 1.0 / BASE)
     fill(R("zer"), R("i0"), 0.0)
     fill(R("geo"), R("i0", 0, 16), BASE)
-    fill(R("s2"), R("i0", 0, 16), BASE ** -16)
+    fill(R("yo"), R("i0", 0, 16), BASE ** -16)
     ts(R("pat"), R("i0"), 0.0, A.is_equal, -2 * HUGE, A.mult)
     ts(R("u1"), R("i0"), 0.0, A.is_gt, HUGE, A.mult)
     act(R("pat2"), R("u1"), bias=FLOOR)
@@ -307,125 +364,181 @@ def rank_program(g, core, T, topo):
     ts(R("zd"), R("pq"), cG16, A.is_equal, cW2, A.mult)
     scan(R("thr0"), R("kb"), R("zer"), -THR0 * W0 * BASE, A.mult, A.add)
     scan(R("s1"), R("geo"), R("oh"), 0.0, A.mult, A.add)
-    scan(R("wl0"), R("s2"), R("zer", 0, 16), W0 * BASE, A.mult, A.add)
+    scan(R("wl0"), R("yo"), R("zer", 0, 16), W0 * BASE, A.mult, A.add)
     act(R("mk"), R("dg"), scale=HUGE, bias=-HUGE)
-    act(R("mkx"), R("mk"), bias=-16.0)
     act(R("dec"), R("bm"), scale=cW)
-    act(R("bw"), R("bm"), scale=R("s1", 15, 16))
+    if not BFC:
+        act(R("bw"), R("bm"), scale=R("s1", 15, 16))
     mm(P(bR, 0, 256), R("mi"), R("thr0"), True, False)
     mm(P(bR, 0, 256), R("mi"), R("mk"), False, True)
     act(R("mn"), R("mi"), scale=-1.0)
     act(R("thr"), P(bR, 0, 256))
-    act(R("mh"), R("mi"))
+    if A0PE:
+        ts(R("zx"), R("pm"), 0.0, A.is_equal, OH(0), A.mult)
+    else:
+        act(R("row0"), R("bm"), scale=OH(0))
     act(R("mu"), R("bm"), scale=cU)
     ms(R("d0"), 0.0)
     ms(R("b0", 0, 48, 3), HUGE)
-    ms(R("b0", 2, 48, 3), -HUGE)
     act(R("dum"), R("i0", 0, 16), bias=cR16)
-    act(R("xs", 61, 782, 48), R("dum"), scale=-1.0, bias=-300.0)
-    fill(R("xs", 77, 798, 48), R("dum"), HUGE)
+    act(R("xs", 61, 782, 48), R("dum"), scale=-1.0, bias=-1200.0)
+    act(R("xs", 77, 798, 48), R("dum"), scale=-1.0, bias=-1200.0)
     ms(R("f0", 0, 48, 3), 0.0)
     ms(R("f0", 2, 48, 3), -1.0)
-    ts(R("dy"), R("wl0"), R("s1", 15, 16), A.mult)
-    add("v", lambda: V.reciprocal(ap(R("yq")), ap(R("dy"))), [R("dy")], [R("yq")])
+    ts(R("wj"), R("wl0"), R("s1", 15, 16), A.mult)
+    add("v", lambda: V.reciprocal(ap(R("yq")), ap(R("wj"))), [R("wj")], [R("yq")])
+    if BFC:
+        for j in range(16):
+            act(R("bwj", 128 * j, 128 * j + 128), R("bm"), scale=R("wj", j, j + 1))
     ts(R("f0", 1, 48, 3), R("yq"), -4000.0, A.mult)
     for t in range(2):
-        fill(slot(t, 73), R("dum"), 0.0)
         act(slot(t, sDUM), R("dum"), scale=-1.0)
         fill(slot(t, sY, 10, 16), R("i0", 0, 6), ZR)
-    act(slot(1, sY, 0, 10), R("rin", 0, 10), scale=1.0 / 16, bias=C0 / 16.0)
-    act(slot(0, sY, 0, 10), R("rin", 0, 10), scale=1.0 / 16, bias=C0 / 16.0)
+        act(slot(t, sY, 0, 10), R("rin", 0, 10), scale=1.0 / 16, bias=C0 / 16.0)
     ms(R("nl"), 1.0)
     ms(R("gz", 0, 10), 0.0)
     ts(R("gz", 10, 16), R("dum", 0, 6), -DS / 16.0, A.add)
-    act(cNKI, cKI, scale=-1.0)
     ms(R("two"), -2.0)
     ms(R("outv", 0, C0), 0.0)
     ms(R("outv", C0 + W, CTW), 0.0)
-
-    def args(nl):
-        act(R("gg", 0, nl), ind(AG, R("tn", 0, nl // 16)))
 
     def digits(nl, dc):
         act(R(dc, 0, nl), ind(DT, R("tn", 0, nl // 16)), bias=cHB)
 
     def lists(nl):
-        k, m = nl // 16, nl // 2
-        for r in range(16):
-            mm(P(bL, 0, k), R("zx", 15 - r, 143 - r), R("gg", r, nl, 16), r == 0, r == 15)
-        mm(P(bHI, 0, m), R("bh", 23, 151), R("gg", 0, nl, 2), True, False)
-        mm(P(bHI, 0, m), R("bh", 15, 143), R("gg", 1, nl, 2), False, True)
-        mm(P(bLO, 0, m), R("bl", 15, 143), R("gg", 0, nl, 2), True, False)
-        mm(P(bLO, 0, m), R("bl", 7, 135), R("gg", 1, nl, 2), False, False)
+        (cp if GGV else act)(R("gg", 0, nl), ind(AG, R("tn", 0, nl // 16)))
+        if A0PE:
+            for r in range(16):
+                mm(P(bL, 16, 16 + nl // 16), R("zx", 15 - r, 143 - r), R("gg", r, nl, 16), r == 0, r == 15)
+            cp(R("a0", 0, nl // 16), P(bL, 16, 16 + nl // 16))
+        else:
+            mm(P(bA, 0, nl), R("mi"), R("mk", 0, nl), True, False)
+            mm(P(bA, 0, nl), R("row0"), R("gg", 0, nl), False, True)
+            scan(R("m1", 0, nl), R("pat", 0, nl), P(bA, 0, nl))
+            cp(R("a0", 0, nl // 16), R("m1", 15, nl, 16))
+        if OLDSEL:
+            m = nl // 2
+            mm(P(bHI, 0, m), R("bh", 23, 151), R("gg", 0, nl, 2), True, False)
+            mm(P(bHI, 0, m), R("bh", 15, 143), R("gg", 1, nl, 2), False, True)
+            mm(P(bLO, 0, m), R("bl", 15, 143), R("gg", 0, nl, 2), True, False)
+            mm(P(bLO, 0, m), R("bl", 7, 135), R("gg", 1, nl, 2), False, False)
+            c = min(SGA, nl) // 2
+            if c:
+                act(R("of", 0, c), P(bHI, 0, c), bias=2048.0)
+            if c < m:
+                act(R("of", c, m), P(bHI, c, m), bias=17 * 2048.0)
+            return
+        mm(P(bHI, 0, nl, 2), R("bd0"), R("gg", 0, nl, 2), True, False)
+        mm(P(bHI, 0, nl, 2), R("bd1"), R("gg", 1, nl, 2), False, True)
+        mm(P(bHI, 1, nl, 2), R("bh", 23, 151), R("gg", 0, nl, 2), True, False)
+        mm(P(bHI, 1, nl, 2), R("bh", 15, 143), R("gg", 1, nl, 2), False, True)
+        mm(P(bLO, 0, nl), R("mi"), R("c32", 0, nl), True, False)
+        (cp if OFV else act)(R("of", 0, nl), P(bHI, 0, nl))
 
     def state(t):
-        tt(R("wl"), R("wl0"), R("nl"), A.mult)
-        act(R("pz4"), R("nl"), scale=-10000.0, bias=9700.0)
-        tt(R("b0", 1, 48, 3), R("pz4"), slot(t, sY), A.subtract)
+        if not BFC:
+            tt(R("wl"), R("wl0"), R("nl"), A.mult)
+        elif t >= 0 and t % STEPS == STEPS - 1:
+            act(R("wl"), R("nl"), scale=512.0, bias=-512.0)
+        act(R("b0", 1, 48, 3), slot(t, sY), scale=-1.0, bias=-1200.0)
+        act(R("b0", 2, 48, 3), R("nl"), scale=-10000.0, bias=5000.0)
         act(R("pz"), R("nl"), scale=1024.0, bias=-1008.0)
-        act(R("pz3"), R("nl"), scale=-4096.0, bias=4080.0)
-        act(R("lim"), R("nl"), scale=9500.0, bias=-10000.0)
-        act(R("lim2"), R("nl"), scale=(DS - 0.5) / 16 - 1024.0, bias=1024.0)
-        act(R("yq"), slot(t - 1, sY), bias=1008.0)
-        tt(R("dy"), slot(t, sY), R("pz3"), A.add)
-        tt(R("cur"), R("dy"), R("yq"), A.min)
+        act(R("pz3"), R("nl"), scale=-1024.0, bias=1024.0)
+        act(R("d0", 3, 64, 4), R("nl"))
+        act(R("cur"), slot(t, sY), bias=-16.0)
+        tt(slot(t + 1, sBACK), slot(t - 1, sY), R("pz3"), A.min)
 
     def choose(nl):
-        k, m, sc = nl // 16, nl // 2, SCUT[nl]
-        cp(R("a0", 0, k), P(bL, 0, k))
-        if sc:
-            act(R("sg", 0, sc), ind(CELLS, R("a0", 0, sc // 16)), AF.Sign, bias=cNMANY)
-            act(R("of", 0, sc // 2), P(bHI, 0, sc // 2), bias=2048.0)
-        ts(R("sg", sc, nl), ind(CELLS, R("a0", sc // 16, k)), cMANY, A.is_gt, 2.0, A.mult)
-        act(R("of", sc // 2, m), P(bHI, sc // 2, m), bias=17 * 2048.0)
-        mm(P(bLO, 0, m), R("blo"), R("sg", 0, nl, 2), False, False)
-        mm(P(bLO, 0, m), R("bhi"), R("sg", 1, nl, 2), False, True)
-        act(R("sv", 0, nl), ind(CELLS, R("a0", 0, k)), bias=cNV0)
-        for lo, hi in ([(m // 2, m), (0, m // 2)] if HALVES == 2 else [(0, m)]):
-            tt(R("m1", lo, hi), P(bLO, lo, hi), R("of", lo, hi), A.max)
-            ts(R("m2", lo, hi), R("m1", lo, hi), 2047, A.bitwise_and)
-            cp(R("ol", lo, hi), R("m2", lo, hi))
+        k, m = nl // 16, nl // 2
+        c = min(SGA, nl)
+        if c:
+            act(R("sg", 0, c), ind(CELLS, R("a0", 0, c // 16)), AF.Sign, bias=cNM)
+        if c < nl:
+            ts(R("sg", c, nl), ind(CELLS, R("a0", c // 16, k)), cMANY, A.is_gt, 2.0, A.mult)
+        if not SVLATE:
+            act(R("sv", 0, nl), ind(CELLS, R("a0", 0, k)), bias=cNV0)
+        if OLDSEL:
+            mm(P(bLO, 0, m), R("blo"), R("sg", 0, nl, 2), False, False)
+            mm(P(bLO, 0, m), R("bhi"), R("sg", 1, nl, 2), False, True)
+            for lo, hi in ((m // 2, m), (0, m // 2)):
+                tt(R("n0", lo, hi), P(bLO, lo, hi), R("of", lo, hi), A.max)
+                ts(R("n1", lo, hi), R("n0", lo, hi), 2047, A.bitwise_and)
+                cp(R("ol", lo, hi), R("n1", lo, hi))
+            return
+        mm(P(bLO, 1, nl, 2), R("blo"), R("sg", 0, nl, 2), False, False)
+        mm(P(bLO, 1, nl, 2), R("bhi"), R("sg", 1, nl, 2), False, False)
+        mm(P(bLO, 1, nl, 2), R("mi"), R("big", 0, m), False, False)
+        mm(P(bLO, 1, nl, 2), R("mi"), R("big", 128, 128 + m), False, True)
+        for lo, hi in ((m // 2, m), (0, m // 2)):
+            scan(R("m1", 2 * lo, 2 * hi), P(bLO, 2 * lo, 2 * hi), R("of", 2 * lo, 2 * hi), 0.0, A.mult, A.add)
+            cp(R("ol", lo, hi), R("m1", 2 * lo + 1, 2 * hi, 2))
+
+    def parents(nl, t, late=False):
+        k = nl // 16
+        if PPLATE != late:
+            return
+        act(R("pp", 0, nl), ind(CELLS, R("tn", 0, k)), bias=cPP)
+        for r in range(16):
+            mm(P(bL, 0, k), R("zd", 15 - r, 143 - r), R("pp", r, nl, 16), r == 0, r == 15)
+        if late:
+            return tt(slot(t + 1, sPAR, 0, k), P(bL, 0, k), slot(t, sY, 0, k), A.subtract)
+        tt(R("pa", 0, k), P(bL, 0, k), slot(t - 1, sY, 0, k), A.subtract)
+        tt(R("pa", 16, 16 + k), slot(t - 1, sY, 0, k), slot(t, sY, 0, k), A.subtract)
+        tt(R("pa", 32, 32 + k), R("pa", 0, k), R("d0", 2, 4 * k, 4), A.mult)
+        tt(slot(t + 1, sPAR, 0, k), R("pa", 32, 32 + k), R("pa", 16, 16 + k), A.add)
 
     def step(nl, t, last):
         k = nl // 16
-        h = 0 if ONEF else 16 * (k // 2)
         wb = "w%d" % (t % 2)
+        final = t == ROUNDS * STEPS - 1
+        h = 16 * (k // 2) if TWOF else 0
+        if t:
+            parents(nl, t - 1, True)
+        mm(P(bF, h, nl), R("mi"), R("thr", h, nl), True, False)
         if h:
-            mm(P(bF0, 0, h), R("mi"), R("thr", 0, h), True, False)
-        mm(P(bF1, h, nl), R("mi"), R("thr", h, nl), True, False)
+            mm(P(bA, 0, h), R("mi"), R("thr", 0, h), True, False)
+        if SVLATE:
+            act(R("sv", 0, nl), ind(CELLS, R("a0", 0, k)), bias=cNV0)
         mm(P(bR, 0, nl), R("mn"), R("sv", 0, nl), True, False)
-        act(R("pp", 0, nl), ind(CELLS, R("tn", 0, k)), bias=cNV0)
-        for r in range(16):
-            mm(P(bL, 16, 16 + k), R("zd", 15 - r, 143 - r), R("pp", r, nl, 16), r == 0, r == 15)
-        tt(slot(t, sPAR, 0, k), P(bL, 16, 16 + k), slot(t - 1, sY, 0, k), A.subtract)
-        at, hi = 0, nl
-        for i, (lo, cut) in enumerate(PIECES[nl]):
-            bM, bX = DEC[i % len(DEC)]
-            for e, a, b in (("s", lo, cut), ("v", cut, hi)):
+        at, hi, top = 0, nl, nl
+        for lo, cut in PIECES[nl]:
+            for e, a, b in (("s", lo, cut), ("v", cut, top)):
                 if a < b:
                     if e == "s":
                         act(R("vv", 8 * a, 8 * b), ind(CELLS, R("ol", a // 2, b // 2)), bias=cNV0)
                     else:
                         ts(R("vv", 8 * a, 8 * b), ind(CELLS, R("ol", a // 2, b // 2)), cNV0, A.add)
                     scan(R("rr", 8 * a, 8 * b), R("mp", 0, 8 * (b - a)), R("vv", 8 * a, 8 * b))
+            top = lo
+            if lo not in DECODE[nl]:
+                continue
+            bM, bX = DEC[DECODE[nl].index(lo) % len(DEC)]
             RR = R("rr", 8 * lo + 7, 8 * hi, 8)
-            mm(P(bM, lo, hi), R("mi"), R("mkx", lo, hi), True, False)
+            mm(P(bM, lo, hi), R("mi"), R("mk", lo, hi), True, False)
             mm(P(bM, lo, hi), R("dec"), RR, False, True)
             mm(P(bX, lo, hi), R("dec"), RR, True, True)
             scan(R("xs", 3 * lo, 3 * hi, 3), R("pat2", lo, hi), P(bM, lo, hi), FLOOR, A.min, A.max)
-            act(R("xu", lo, hi), P(bX, lo, hi), AF.Relu, bias=-16.0)
+            act(R("xu", lo, hi), P(bX, lo, hi), AF.Relu)
+            if BFC:
+                if t and t % STEPS == 0 and hi > OWN:
+                    a = max(lo, OWN)
+                    tt(R("xs", 3 * a + 45, 3 * hi, 48), R("xs", 3 * a + 45, 3 * hi, 48), R("wl", a // 16, hi // 16), A.add)
+                (act if lo in XHS else cp)(R("xh", lo // 16, hi // 16), R("xs", 3 * lo + 45, 3 * hi, 48))
+                tt(R("xl", lo // 16, hi // 16), R("xs", 3 * lo + 45, 3 * hi, 48), R("xh", lo // 16, hi // 16), A.subtract)
             for j in range(hi // 16 - 1, lo // 16 - 1, -1):
                 w = nl - 16 * j
-                ts(R("ee", at, at + w), R("xu", 16 * j, nl), R("xs", 48 * j + 45, 48 * j + 46), A.is_equal, R("wl", j, j + 1), A.mult)
-                if 16 * j < h:
-                    mm(P(bF1, h, nl), R("bw"), R("ee", at + h - 16 * j, at + w), False, j == 0)
-                    mm(P(bF0, 16 * j, h), R("bw"), R("ee", at, at + h - 16 * j), False, j == 0)
+                bw = R("bwj", 128 * j, 128 * j + 128) if BFC else R("bw")
+                if BFC:
+                    ts(R("ee", at, at + w), R("xu", 16 * j, nl), R("xh", j, j + 1), A.subtract, R("xl", j, j + 1), A.is_equal)
                 else:
-                    mm(P(bF1, 16 * j, nl), R("bw"), R("ee", at, at + w), False, j == 0)
+                    ts(R("ee", at, at + w), R("xu", 16 * j, nl), R("xs", 48 * j + 45, 48 * j + 46), A.is_equal, R("wl", j, j + 1), A.mult)
+                c = max(h - 16 * j, 0)
+                mm(P(bF, 16 * j + c, nl), bw, R("ee", at + c, at + w), False, j == 0)
+                if c:
+                    mm(P(bA, 16 * j, h), bw, R("ee", at, at + c), False, j == 0)
                 at += w
             hi = lo
         RR = R("rr", 7, 8 * nl, 8)
-        final = t == ROUNDS * STEPS - 1
         mm(P(bR, 0, nl), R("mh"), RR, False, True)
         scan(R("bo", 0, 3 * k), R("b0", 0, 3 * k), R("xs", 45, 45 + 48 * k, 16), 0.0, A.max, A.min)
         if final:
@@ -434,36 +547,44 @@ def rank_program(g, core, T, topo):
             mm(P(bR, 0, nl), R("mn"), R("tr", 0, nl), True, False)
             mm(P(bR, 0, nl), R("mu"), R("rp", 0, nl), False, True)
             act(R("sg", 0, nl), P(bR, 0, nl), AF.Relu, bias=2.0, scale=cNKI)
-            ts(slot(t, sDUM), R("bo", 1, 3 * k, 3), 300.0, A.add)
+            ts(slot(t, sDUM), R("bo", 2, 3 * k, 3), 1200.0, A.add)
         else:
             act(R("ww", 0, nl), P(bR, 0, nl), AF.Relu)
-            ts(R("tb", 0, k), R("bo", 1, 3 * k, 3), -16.0, A.mult, 4800.0, A.subtract)
+            ts(R("tb", 0, k), R("bo", 2, 3 * k, 3), -16.0, A.mult, 19200.0, A.subtract)
             act(ind(CT, R("tb", 0, k)), R("ww", 0, nl), AF.Silu)
         XS = R("xs", 45, 48 * k, 48)
         tt(slot(t, sX, 0, k), XS, R("pz", 0, k), A.add)
         tt(slot(t, sCX, 0, k), R("cur", 0, k), XS, A.subtract)
-        tt(R("d0", 1, 4 * k, 4), XS, R("lim", 0, k), A.is_lt)
-        tt(R("d0", 2, 4 * k, 4), XS, R("lim2", 0, k), A.is_lt)
+        ts(R("d0", 1, 4 * k, 4), XS, -1500.0, A.is_lt)
+        ts(R("d0", 2, 4 * k, 4), XS, (DS - 0.5) / 16, A.is_lt)
         scan(R(wb, 38, 38 + 48 * k, 12), R("d0", 0, 4 * k), R(wb, 37, 37 + 48 * k, 12), 0.0, A.mult, A.add)
         if not last:
-            ts(R("tn", 0, k), slot(t, sY, 0, k), 16.0, A.mult, float(C0), A.subtract)
-            args(nl)
+            ts(R("tn", 0, k), slot(t, sRAW, 0, k), 16.0, A.mult, float(C0), A.subtract)
+        act(R("lim", 0, k), slot(t, sRAW, 0, k), scale=16.0, bias=1.5 * 2 ** 23)
+        act(slot(t, sY, 0, k), R("lim", 0, k), scale=1.0 / 16, bias=-1.5 * 2 ** 19)
+        if not last:
             lists(nl)
+            parents(nl, t)
             choose(nl)
         elif not final:
             before(t // STEPS, t)
-        scan(R(wb, 3 * h, 3 * nl, 3), R("pat", h, nl), P(bF1, h, nl))
+        scan(R(wb, 3 * h, 3 * nl, 3), R("pat", h, nl), P(bF, h, nl))
         if h:
-            scan(R(wb, 0, 3 * h, 3), R("pat", 0, h), P(bF0, 0, h))
+            scan(R(wb, 0, 3 * h, 3), R("pat", 0, h), P(bA, 0, h))
         scan(R("fo", 0, 3 * k), R("f0", 0, 3 * k), R(wb, 45, 45 + 48 * k, 16), 0.0, A.mult, A.min)
         ts(R("th", 0, k), R("fo", 2, 3 * k, 3), -16.0, A.mult)
         if final:
             for lo, hi in zip(CUTS, CUTS[1:]):
                 act(R("ab", lo, hi), R("ct", C0 + lo, C0 + hi), AF.Abs, bias=-144.0, scale=cKI)
-                ts(R("outv", C0 + lo, C0 + hi), R("ab", lo, hi), -1.0, A.mult, 144.0, A.add)
+                if lo in OUTS:
+                    act(R("outv", C0 + lo, C0 + hi), R("ab", lo, hi), scale=-1.0, bias=144.0)
+                else:
+                    ts(R("outv", C0 + lo, C0 + hi), R("ab", lo, hi), -1.0, A.mult, 144.0, A.add)
             tt(ind(R("outv"), R("th", 0, k)), R("sg", 0, nl), R("two"), A.add)
-        else:
+        elif HOLEV:
             cp(ind(CT, R("th", 0, k)), R("dc%d" % (t % 2), 0, nl))
+        else:
+            act(ind(CT, R("th", 0, k)), R("dc%d" % (t % 2), 0, nl), AF.Silu)
 
     def kept(nl, t):
         k = nl // 16
@@ -501,11 +622,15 @@ def rank_program(g, core, T, topo):
         tt(slot(t, sY), slot(t, sY), R("s2"), A.add)
         tt(slot(t - 1, sY), slot(t - 1, sY), R("s1"), A.max)
         ts(R("tn"), slot(t, sY), 16.0, A.mult, float(C0), A.subtract)
-        args(L)
         lists(L)
+        if x == 0:
+            ms(R("d0", 42, 64, 4), 0.0)
+        else:
+            tt(R("d0", 2, 64, 4), R("d0", 2, 64, 4), R("s3"), A.is_gt)
+        parents(L, t)
 
     def exchange(x, nl, t):
-        ts(R("stg%d" % (2 * x + 1)), SI, cV0, A.is_gt)
+        act(R("stg%d" % (2 * x + 1)), SI, AF.Sign, bias=cNV0)
         send(2 * x + 1, (0, 1, 2))
         kept(nl, t)
         tt(R("s2", 10, 16), R("nl", 10, 16), R("s3", 10, 16), A.subtract)
@@ -513,9 +638,10 @@ def rank_program(g, core, T, topo):
         ts(R("tc"), EX, cV0, A.is_gt)
         tt(R("te"), R("ta"), R("tc"), A.subtract)
         tt(R("tm"), R("te"), R("dg", 0, DS), A.mult)
-        ts(R("x2"), EX, -1.0, A.mult, cHR, A.add)
+        act(R("x2"), EX, scale=-0.5, bias=cHR2)
         ts(R("hm"), SI, cV0, A.is_le, 4096.0, A.mult)
         tt(R("dif"), R("te"), R("x2"), A.mult)
+        tt(R("hr", 0, DS), EX, R("dif"), A.add)
         digits(L, "dc%d" % (1 - t % 2))
         tt(R("x1"), arrived(2 * x), R("hm"), A.add)
         tt(SI, SI, R("x1"), A.min)
@@ -523,15 +649,15 @@ def rank_program(g, core, T, topo):
         ASK = arrived(2 * x + 1)
         tt(R("x2"), ASK, R("dif"), A.mult)
         tt(R("x3"), R("tm"), ASK, A.mult)
-        tt(EX, EX, R("x2"), A.add)
+        tt(EX, R("hr", 0, DS), R("x2"), A.add)
         scan(R("x4"), R("pat", 0, DS), R("x3"))
         tt(R("nl", 10, 16), R("x4", 15, DS, 16), R("s2", 10, 16), A.add)
         state(t)
 
-    args(OWN)
     lists(OWN)
     digits(OWN, "dc0")
     choose(OWN)
+    act(slot(0, sPAR, 0, 10), slot(1, sY, 0, 10), scale=-1.0, bias=ZR)
     state(-1)
     t = 0
     for rnd in range(ROUNDS):

import math
from concourse.bass import DstId, RemoteDMATransfer
from concourse.mybir import AluOpType, ActivationFunctionType

W, OWN, S, D, STEPS, ROUNDS = 1920, 160, 32, 3, 3, 3
DS = S * D
L = OWN + DS
REST = W
C0 = 256
CTW = C0 + W + 16
U = 1.0 / 64
BASE, THR0, W0 = 256.0 / 150.0, 2.56, 1.0e25
HUGE, FLOOR = 1.0e29, -2048.0
LIFT = 1.002
ENG = 4
PIECES = {OWN: ((80, 120), (0, 48)), L: ((160, 208), (64, 128), (0, 48))}
DECODE = {OWN: (80, 0), L: (160, 64, 0)}
CUTS = [0, 256, 704, 1152, 1600, W]
A0PE, TWOF, HOLEV, OFV, SVLATE = True, False, False, False, True
OLDSEL, PPLATE, SCANF, SAME, COLF = True, True, 3, 220, False
AFIX, PFIX, GGV, T1S = 0, 6, False, (0, 1, 2, 3)
BFC, SGA, XHS, OUTS, YAF = True, 128, (0, 64, 80, 160), (), 800
SUMS = ()
WAKE, PEF, GATH, SCAT, DFIX, DCOL, RFIX, PASSES = 230, 0.55, 1.5, 3.5, 1000, 0.7, 2400, 2

F, H, B, I, U16 = "float32", "float16", "bfloat16", "int32", "uint16"
SB = {}
for _t, _l in ((I, "agt 1936 rin 16 pc 16 pc2 24 n0 264 n1 264"),
               (U16, "tn 16 th 16 tb 16 a0 16 ol 128"),
               (H, "bl 152 bh 152 zd 152 zx 152 gg 256 mh 128 mn 128 mu 128 dec 128 mp 768 vv 2048 rr 2048 rp 256 sv 256 pp 256 xu 256 tr 256 "
                   "t1 1920 stg0 96 stg1 96 stg2 96 stg3 96 land0 96 land1 96 land2 96 land3 96 hm 96 x1 96 ta 96 tc 96 te 96 tm 96 x3 96 "
                   "md 128 bd0 128 bd1 128 row0 128"),
               (F, "ct %d col 48 gz 16 pa 48 xm 16 pz4 16 dum 16 b0 48 bo 48 oh 16 geo 16 s1 16 s2 16 s3 16 wl0 16 wl 16 pz 16 pz3 16 lim 16 "
                   "lim2 16 nl 16 cur 16 yq 16 dy 16 yo 16 m1 256 xs 848 w0 848 w1 848 d0 64 f0 48 fo 48 dc0 256 dc1 256 ww 256 hr 160 "
                   "dif 96 x2 96 x4 96 wj 16 of 128" % CTW),
               (B, "vin 1920 dt 2048 ab 1920 outv %d two 256 big 256 c32 256 i0 256 i1 128 pm 152 gh 128 kb 256 zer 256 uu 256 u1 256 mi 128 "
                   "hib 8 xh 16 xl 16 bwj 2048 mk4 128 bw 128 pq 152 blo 128 bhi 128 dg 256 bm 128 pat 256 pat2 256 mk 256 thr0 256 thr 256 sg 256 ee 2176" % CTW)):
    _w = _l.split()
    for _k in range(0, len(_w), 2):
        SB[_w[_k]] = (int(_w[_k + 1]), _t)
SCRATCH = {k: ("sbuf", [128, v[0]], v[1]) for k, v in SB.items() if not (OLDSEL and k in ("bd0", "bd1", "lim2", "big", "c32"))}
for _k in range(8):
    SCRATCH["pb%d" % _k] = ("psum", [128, 512], F)
POOL = {"v": 44, "s": 30, "p": 30, "g": 10, "d": 8}
SEMAPHORES = ["%s%d" % (e, k) for e in POOL for k in range(POOL[e])] + [w + str(k) for w in ("arr", "snt") for k in range(4)]
A = AluOpType
AF = ActivationFunctionType
ID = AF.Identity
bL, bLO, bHI, bA, bF, bR = 0, 1, 2, 5, 6, 7
DEC = ((3, 4), (1, 2))


def R(name, lo=0, hi=None, step=1):
    return (name, lo, SB[name][0] if hi is None else hi, step)


def C(k):
    return ("col", k, k + 1, 1)


def P(k, lo, hi, step=1):
    return ("pb%d" % k, lo, hi, step)


def ind(win, off):
    return ("ind", win, off)


def overlap(a, b):
    return a[1] < b[2] and b[1] < a[2] and (a[1] - b[1]) % math.gcd(a[3], b[3]) == 0


def width(x):
    return 16 * width(x[2]) if x[0] == "ind" else len(range(x[1], x[2], x[3]))


def cycles(eng, kind, ins, outs, both):
    if kind == "d":
        x = (outs or ins)[0]
        if x[0] == "yo":
            return 50, DFIX + YAF
        return 50, DFIX + DCOL * width(x) * (1 if SB[x[0]][1] == B else 2)
    if kind != "c":
        return (300, RFIX) if kind == "r" else (0, 0)
    n = width(outs[0])
    sides = [x for x in ins + outs if isinstance(x, tuple)]
    if eng == "g":
        c = 160 + 2 * n
    elif outs[0][0] == "ind":
        c = 60 + SCAT * n
    elif any(x[0] == "ind" for x in sides):
        c = 70 + GATH * n
    elif eng == "p":
        c = max(64, n) * PEF + PFIX
    elif eng != "v":
        c = max(64, n) + AFIX
    elif both == 3:
        c = max(64, 2 * n if any(x[0][:2] == "pb" for x in sides) else n if any(SB[x[0]][1] == F for x in sides) else n / 2)
    elif both == 1:
        c = max(64, n if any(x[0][:2] == "pb" for x in sides[:2]) else 2 * n)
    else:
        c = max(64, (n if any(x[0][:2] == "pb" or (SB[x[0]][1] in (F, I) and (width(x) == n or not COLF)) for x in sides) else n / 2) * (both or 1))
    return c, c


def conflicts(ops):
    hist, out = {}, []
    for i, o in enumerate(ops):
        deps, e = {}, o["e"]
        for x, wr in [(x, False) for x in o["r"]] + [(x, True) for x in o["w"]]:
            for j, y, jw in hist.get(x[0], []):
                hit = (wr or jw) and overlap(x, y)
                if x[0].startswith("pb"):
                    deps[j] = deps.get(j, False) or ops[j]["e"] != e or (hit and not o["acc"])
                elif hit:
                    deps[j] = True
        out.append(deps)
        for x in o["r"]:
            hist.setdefault(x[0], []).append((i, x, False))
        for x in o["w"]:
            hist.setdefault(x[0], []).append((i, x, True))
    return out


def arrange(ops):
    deps = conflicts(ops)
    for i, o in enumerate(ops):
        if o["k"] == "w":
            deps[i][max(j for j in range(i) if ops[j]["k"] == "r" and ops[j]["ext"] == o["ext"])] = True
        if o["k"] == "d" and o["w"]:
            deps[i].update({j: False for j in range(i) if ops[j]["k"] == "d"})

    def lag(j, i):
        if ops[i]["k"] == "d" and ops[j]["k"] == "d":
            return ops[j]["c"][1] - DFIX
        return ops[j]["c"][1] + (0 if not deps[i][j] or ops[j]["k"] == "w" else SAME if ops[i]["e"] == ops[j]["e"] else WAKE)
    n = range(len(ops))
    rest = [o["c"][1] for o in ops]
    after = [[] for _ in ops]
    for i in reversed(n):
        for j in deps[i]:
            rest[j] = max(rest[j], lag(j, i) + rest[i])
            after[j].append(i)

    def place(order, earliest):
        start, busy = {}, {}
        for i in order:
            t, c = earliest(i, start), ops[i]["c"][0]
            q = busy.setdefault(ops[i]["e"], [])
            at = max(bisect(q, t) - 1, 0)
            while at < len(q) and t + c > q[at][0]:
                t = max(t, q[at][1])
                at += 1
            q.insert(at, (t, t + c))
            start[i] = t
        return start

    def forward(i, start):
        return max([start[j] + lag(j, i) for j in deps[i]] + [0])

    def backward(j, end):
        c = ops[j]["c"]
        return max([end[i] + ops[i]["c"][0] + lag(j, i) - c[0] for i in after[j]] + [c[1] - c[0]])
    first = [1e9 if o["k"] == "d" and o["w"] else 0 for o in ops]
    start = place(sorted(n, key=lambda i: (-rest[i] - first[i], i)), forward)
    for _ in range(PASSES):
        end = place(sorted(n, key=lambda i: (-start[i], -i)), backward)
        start = place(sorted(n, key=lambda i: (-end[i] - ops[i]["c"][0] - first[i], i)), forward)
    return [ops[i] for i in sorted(n, key=lambda i: (start[i], i))]


def bisect(q, t):
    lo, hi = 0, len(q)
    while lo < hi:
        mid = (lo + hi) // 2
        if q[mid][0] <= t:
            lo = mid + 1
        else:
            hi = mid
    return lo


def rank_program(g, core, T, topo):
    rank = T.rank_of(core)
    if rank is None:
        return
    Q = {"v": g.vector, "s": g.scalar, "p": g.tensor, "g": g, "y": g.sync}
    V = g.vector
    ops = []

    def ap(x):
        if isinstance(x, tuple):
            if x[0] == "ind":
                return ap(x[1]).indirect(ap(x[2]))
            return T[x[0]][:, x[1]:x[2]:x[3]] if x[3] > 1 else T[x[0]][:, x[1]:x[2]]
        return x

    def add(eng, fn, ins, outs, kind="c", acc=False, ext=None, both=False):
        rd = [x[2] for x in outs if x[0] == "ind"]
        for x in ins:
            if isinstance(x, tuple):
                rd += [x[1], x[2]] if x[0] == "ind" else [x]
        ops.append({"e": eng, "fn": fn, "c": cycles(eng, kind, ins, outs, both), "r": rd,
                    "w": [x[1] if x[0] == "ind" else x for x in outs], "k": kind, "acc": acc, "ext": ext})

    def ts(out, in0, s1, op0, s2=None, op1=None):
        if op1 is None:
            add("v", lambda: V.tensor_scalar(ap(out), ap(in0), ap(s1), None, op0), [in0, s1], [out])
        else:
            add("v", lambda: V.tensor_scalar(ap(out), ap(in0), ap(s1), ap(s2), op0, op1), [in0, s1, s2], [out])

    def tt(out, a, b, op):
        add("v", lambda: V.tensor_tensor(ap(out), ap(a), ap(b), op), [a, b], [out], both=True)

    def cp(out, a):
        add("v", lambda: V.tensor_copy(ap(out), ap(a)), [a], [out])

    def ms(out, c):
        add("v", lambda: V.memset(ap(out), c), [], [out])

    def scan(out, d0, d1, init=0.0, op0=A.add, op1=A.max):
        add("v", lambda: V.tensor_tensor_scan(ap(out), ap(d0), ap(d1), init, op0, op1), [d0, d1], [out], both=SCANF)

    def act(out, a, f=ID, bias=0.0, scale=1.0):
        if out[0] == "ind":
            add("s", lambda: g.scalar.activation(ap(out), ap(a), f), [a], [out])
        else:
            add("s", lambda: g.scalar.activation(ap(out), ap(a), f, bias=ap(bias), scale=ap(scale)), [a, bias, scale], [out])

    def fill(out, src, c):
        act(out, src, bias=c, scale=0.0)

    def mm(out, lt, rhs, start, stop):
        add("p", lambda: g.tensor.matmul(ap(out), ap(lt), ap(rhs), start, stop), [lt, rhs], [out], acc=not start)

    def iota(out, pat, base, cm):
        if SB[out[0]][1] == I:
            add("g", lambda: g.iota(ap(out), pat, base, cm), [], [out])
        else:
            add("g", lambda: g.iota(ap(out), pat, base, cm, allow_small_or_imprecise_dtypes=True), [], [out])

    def load(q, out, src):
        add(q, lambda: Q[q].dma_start(ap(out), src), [], [out], kind="d")

    def store(q, dst, a):
        add(q, lambda: Q[q].dma_start(dst, ap(a)), [a], [], kind="d")

    load("s", R("rin", 0, 10), T.rts[:, :])
    load("y", R("vin"), T.vals[:, :])
    load("y", R("agt", 0, W), T.ag[:, :])

    cR, cG, cLO, cHI, cHB, cHR, cG2, cG21, cG16, cU, cR16, cK, cKI, cV0, cNV0, cMANY, cVK, cNKI, cVD, cVH, cVL, cPP, cBIT = [C(k) for k in range(23)]
    cA, cD = 24, 32
    CT, CELLS, AG, DT = R("ct"), R("ct", C0, CTW), R("agt"), R("dt")
    ZR = (REST + C0) / 16.0

    def OH(j):
        return R("oh", j, j + 1)

    def slot(t, at, lo=0, hi=16):
        return R("w%d" % (t % 2), 48 * lo + at, 48 * (hi - 1) + at + 1, 48)
    sPAR, sCX, sX, sBACK, sRAW, sY, sDUM = 37, 49, 61, 73, 74, 65, 77
    iota(R("pc"), [[-1, 16]], 16, 1)
    iota(R("i0", 0, 16), [[1, 16]], 0, 0)
    iota(R("n0", 0, 256), [[1, 256]], 0, 0)
    iota(R("n0", 256, 264), [[256, 8]], 0, 0)
    iota(R("pm"), [[1, 152]], -15, -1)
    iota(R("i0", 16, 256), [[0, 15], [1, 16]], 0, 0)
    iota(R("gh"), [[1, 16], [0, 8]], 0, 0)
    iota(R("i1"), [[1, 8], [0, 16]], 0, 0)
    iota(R("pq"), [[1, 152]], -15, 0)
    ts(R("pc2", 0, 16), R("pc"), 15, A.bitwise_and)
    ts(R("pc2", 16, 17), R("pc", 0, 1), 4, A.logical_shift_right)
    cp(cR, R("pc2", 0, 1))
    ts(cG, R("pc2", 16, 17), -1.0, A.add)
    ms(R("agt", W, 1936), REST)
    ms(R("mp"), 1.0 / 16)
    ms(R("mp", 0, 768, 8), -4096.0)
    ts(R("oh"), R("pc2", 0, 16), 0.0, A.is_equal)
    ms(R("pa", 0, 16), 2.0)
    ms(R("pa", 16, 32), 0.5)
    scan(R("s2"), R("pa", 0, 16), R("oh"), 0.0, A.mult, A.add)
    scan(R("s3"), R("pa", 16, 32), R("oh"), 0.0, A.mult, A.add)
    ts(R("n1"), R("n0"), R("s2", 10, 11), A.mult)
    ts(R("n0"), R("n1"), 10, A.logical_shift_right, 1, A.bitwise_and)
    ts(R("uu"), R("n0", 0, 256), U, A.mult)
    ts(R("hib"), R("n0", 256, 264), U, A.mult, -1.0 / 32, A.add)
    ts(R("mi"), R("pm", 15, 143), 0.0, A.is_equal)
    fill(R("ct", 0, C0), R("i0"), 0.0)
    fill(R("ct", C0 + W, CTW), R("i0", 0, 16), 0.0)
    for c, k4, k6 in ((cK, 4, 6), (cV0, 1158, 1737), (cNV0, -1158, -1737), (cKI, 0.25, 1.0 / 6), (cNKI, -0.25, -1.0 / 6), (cMANY, 30, 45),
                      (cVD, 1158 - 1792, 1737 - 1792), (cVH, 1158 + 5.0 / 128, 1737 + 5.0 / 128), (cVL, 1157.5, 1736.5), (cVK, 1162, 1743),
                      (cPP, 16 - 1.0 / 128 - 1158, 16 - 1.0 / 128 - 1737)):
        act(c, OH(15), scale=float(k6 - k4), bias=float(k4))
    act(cHB, OH(11), scale=U, bias=cVH)
    act(cG2, cG, scale=2.0)
    act(cG21, cG, scale=2.0, bias=1.0)
    act(cG16, cG, scale=16.0)
    act(cR16, cR, scale=1.0 / 16)
    act(R("mh"), R("mi"))
    for a in range(8):
        if a in (5, 6):
            act(R("dt", 256 * a, 256 * a + 256), R("uu"), bias=R("hib", a, a + 1))
        else:
            ts(R("dt", 256 * a, 256 * a + 256), R("uu"), R("hib", a, a + 1), A.add)
    ts(cLO, cR, 7.5, A.is_lt)
    ts(cHI, cR, 7.5, A.is_gt)
    tt(cHR, R("dt", REST, REST + 1), cHB, A.add)
    cHR2 = C(cA)
    act(cHR2, cHR, scale=0.5)
    ms(R("tn", 10, 16), REST)
    cp(R("tn", 0, 10), R("rin", 0, 10))

    act(R("md"), R("mi"), scale=cNV0)
    if SUMS:
        act(R("mk4"), R("mi"), scale=cK)
    for h in range(4):
        lo, hi = 480 * h, 480 * h + 480
        if h in SUMS:
            mm(P(3 + h, 0, 480), R("mk4"), R("vin", lo, hi), True, False)
            ts(R("t1", lo, hi), R("vin", lo, hi), 0.0, A.is_lt, cVK, A.mult)
            mm(P(3 + h, 0, 480), R("mh"), R("t1", lo, hi), False, False)
            mm(P(3 + h, 0, 480), R("mi"), R("dt", lo, hi), False, True)
            act(R("ct", C0 + lo, C0 + hi), P(3 + h, 0, 480))
        else:
            mm(P(3 + h, 0, 480), R("md"), R("vin", lo, hi), True, False)
            mm(P(3 + h, 0, 480), R("mi"), R("dt", lo, hi), False, True)
            if h in T1S:
                act(R("t1", lo, hi), R("vin", lo, hi), scale=cK)
            else:
                ts(R("t1", lo, hi), R("vin", lo, hi), cK, A.mult)
            tt(R("ct", C0 + lo, C0 + hi), P(3 + h, 0, 480), R("t1", lo, hi), A.max)
    fill(R("hr"), R("i0", 0, 160), cHR)
    act(R("ct", C0 + REST, C0 + REST + 1), cHR)
    cp(ind(CELLS, R("tn", 0, 10)), R("hr"))
    ts(R("bl"), R("pm"), 0.0, A.is_equal, cLO, A.mult)
    ts(R("bh"), R("pm"), 0.0, A.is_equal, cHI, A.mult)
    ts(R("blo"), R("gh"), cG2, A.is_equal, 2048.0, A.mult)
    ts(R("bhi"), R("gh"), cG21, A.is_equal, 2048.0, A.mult)
    cNM = C(cA + 1)
    act(cNM, cMANY, scale=-1.0)
    if not OLDSEL:
        tt(R("bd0"), R("bl", 15, 143), R("bh", 23, 151), A.subtract)
        tt(R("bd1"), R("bl", 7, 135), R("bh", 15, 143), A.subtract)
        fill(R("big", 0, 128), R("i0", 0, 128), 1.5 * 2 ** 23)
        fill(R("big", 128, 256), R("i0", 0, 128), -1.5 * 2 ** 23)
        ms(R("c32", 0, 256, 2), 0.0)
        ms(R("c32", 1, 256, 2), -1.0 / 32)
    chain = ((13, -8188.0), (12, 1.0), (12, 32767.0), (11, -32768.0), (14, -8192.0), (15, 8192.0))
    act(cBIT, R("s3", 10, 11), scale=4096.0)
    for j, (r, w) in enumerate(chain):
        act(C(cD + j), OH(r), scale=w, bias=C(cD + j - 1) if j else cBIT)
    cW2, cW = C(cD + 1), C(cD + 5)
    act(cU, OH(13), AF.Silu, scale=8192.0)
    fill(R("kb"), R("i0"), 1.0 / BASE)
    fill(R("zer"), R("i0"), 0.0)
    fill(R("geo"), R("i0", 0, 16), BASE)
    fill(R("yo"), R("i0", 0, 16), BASE ** -16)
    ts(R("pat"), R("i0"), 0.0, A.is_equal, -2 * HUGE, A.mult)
    ts(R("u1"), R("i0"), 0.0, A.is_gt, HUGE, A.mult)
    act(R("pat2"), R("u1"), bias=FLOOR)
    ts(R("bm"), R("i1", 0, 128), cG, A.is_equal)
    ts(R("dg"), R("i0"), cR, A.is_equal)
    ts(R("zd"), R("pq"), cG16, A.is_equal, cW2, A.mult)
    scan(R("thr0"), R("kb"), R("zer"), -THR0 * W0 * BASE, A.mult, A.add)
    scan(R("s1"), R("geo"), R("oh"), 0.0, A.mult, A.add)
    scan(R("wl0"), R("yo"), R("zer", 0, 16), W0 * BASE, A.mult, A.add)
    act(R("mk"), R("dg"), scale=HUGE, bias=-HUGE)
    act(R("dec"), R("bm"), scale=cW)
    if not BFC:
        act(R("bw"), R("bm"), scale=R("s1", 15, 16))
    mm(P(bR, 0, 256), R("mi"), R("thr0"), True, False)
    mm(P(bR, 0, 256), R("mi"), R("mk"), False, True)
    act(R("mn"), R("mi"), scale=-1.0)
    act(R("thr"), P(bR, 0, 256))
    if A0PE:
        ts(R("zx"), R("pm"), 0.0, A.is_equal, OH(0), A.mult)
    else:
        act(R("row0"), R("bm"), scale=OH(0))
    act(R("mu"), R("bm"), scale=cU)
    ms(R("d0"), 0.0)
    ms(R("b0", 0, 48, 3), HUGE)
    act(R("dum"), R("i0", 0, 16), bias=cR16)
    act(R("xs", 61, 782, 48), R("dum"), scale=-1.0, bias=-1200.0)
    act(R("xs", 77, 798, 48), R("dum"), scale=-1.0, bias=-1200.0)
    ms(R("f0", 0, 48, 3), 0.0)
    ms(R("f0", 2, 48, 3), -1.0)
    ts(R("wj"), R("wl0"), R("s1", 15, 16), A.mult)
    add("v", lambda: V.reciprocal(ap(R("yq")), ap(R("wj"))), [R("wj")], [R("yq")])
    if BFC:
        for j in range(16):
            act(R("bwj", 128 * j, 128 * j + 128), R("bm"), scale=R("wj", j, j + 1))
    ts(R("f0", 1, 48, 3), R("yq"), -4000.0, A.mult)
    for t in range(2):
        act(slot(t, sDUM), R("dum"), scale=-1.0)
        fill(slot(t, sY, 10, 16), R("i0", 0, 6), ZR)
        act(slot(t, sY, 0, 10), R("rin", 0, 10), scale=1.0 / 16, bias=C0 / 16.0)
    ms(R("nl"), 1.0)
    ms(R("gz", 0, 10), 0.0)
    ts(R("gz", 10, 16), R("dum", 0, 6), -DS / 16.0, A.add)
    ms(R("two"), -2.0)
    ms(R("outv", 0, C0), 0.0)
    ms(R("outv", C0 + W, CTW), 0.0)

    def digits(nl, dc):
        act(R(dc, 0, nl), ind(DT, R("tn", 0, nl // 16)), bias=cHB)

    def lists(nl):
        (cp if GGV else act)(R("gg", 0, nl), ind(AG, R("tn", 0, nl // 16)))
        if A0PE:
            for r in range(16):
                mm(P(bL, 16, 16 + nl // 16), R("zx", 15 - r, 143 - r), R("gg", r, nl, 16), r == 0, r == 15)
            cp(R("a0", 0, nl // 16), P(bL, 16, 16 + nl // 16))
        else:
            mm(P(bA, 0, nl), R("mi"), R("mk", 0, nl), True, False)
            mm(P(bA, 0, nl), R("row0"), R("gg", 0, nl), False, True)
            scan(R("m1", 0, nl), R("pat", 0, nl), P(bA, 0, nl))
            cp(R("a0", 0, nl // 16), R("m1", 15, nl, 16))
        if OLDSEL:
            m = nl // 2
            mm(P(bHI, 0, m), R("bh", 23, 151), R("gg", 0, nl, 2), True, False)
            mm(P(bHI, 0, m), R("bh", 15, 143), R("gg", 1, nl, 2), False, True)
            mm(P(bLO, 0, m), R("bl", 15, 143), R("gg", 0, nl, 2), True, False)
            mm(P(bLO, 0, m), R("bl", 7, 135), R("gg", 1, nl, 2), False, False)
            c = min(SGA, nl) // 2
            if c:
                act(R("of", 0, c), P(bHI, 0, c), bias=2048.0)
            if c < m:
                act(R("of", c, m), P(bHI, c, m), bias=17 * 2048.0)
            return
        mm(P(bHI, 0, nl, 2), R("bd0"), R("gg", 0, nl, 2), True, False)
        mm(P(bHI, 0, nl, 2), R("bd1"), R("gg", 1, nl, 2), False, True)
        mm(P(bHI, 1, nl, 2), R("bh", 23, 151), R("gg", 0, nl, 2), True, False)
        mm(P(bHI, 1, nl, 2), R("bh", 15, 143), R("gg", 1, nl, 2), False, True)
        mm(P(bLO, 0, nl), R("mi"), R("c32", 0, nl), True, False)
        (cp if OFV else act)(R("of", 0, nl), P(bHI, 0, nl))

    def state(t):
        if not BFC:
            tt(R("wl"), R("wl0"), R("nl"), A.mult)
        elif t >= 0 and t % STEPS == STEPS - 1:
            act(R("wl"), R("nl"), scale=512.0, bias=-512.0)
        act(R("b0", 1, 48, 3), slot(t, sY), scale=-1.0, bias=-1200.0)
        act(R("b0", 2, 48, 3), R("nl"), scale=-10000.0, bias=5000.0)
        act(R("pz"), R("nl"), scale=1024.0, bias=-1008.0)
        act(R("pz3"), R("nl"), scale=-1024.0, bias=1024.0)
        act(R("d0", 3, 64, 4), R("nl"))
        act(R("cur"), slot(t, sY), bias=-16.0)
        tt(slot(t + 1, sBACK), slot(t - 1, sY), R("pz3"), A.min)

    def choose(nl):
        k, m = nl // 16, nl // 2
        c = min(SGA, nl)
        if c:
            act(R("sg", 0, c), ind(CELLS, R("a0", 0, c // 16)), AF.Sign, bias=cNM)
        if c < nl:
            ts(R("sg", c, nl), ind(CELLS, R("a0", c // 16, k)), cMANY, A.is_gt, 2.0, A.mult)
        if not SVLATE:
            act(R("sv", 0, nl), ind(CELLS, R("a0", 0, k)), bias=cNV0)
        if OLDSEL:
            mm(P(bLO, 0, m), R("blo"), R("sg", 0, nl, 2), False, False)
            mm(P(bLO, 0, m), R("bhi"), R("sg", 1, nl, 2), False, True)
            for lo, hi in ((m // 2, m), (0, m // 2)):
                tt(R("n0", lo, hi), P(bLO, lo, hi), R("of", lo, hi), A.max)
                ts(R("n1", lo, hi), R("n0", lo, hi), 2047, A.bitwise_and)
                cp(R("ol", lo, hi), R("n1", lo, hi))
            return
        mm(P(bLO, 1, nl, 2), R("blo"), R("sg", 0, nl, 2), False, False)
        mm(P(bLO, 1, nl, 2), R("bhi"), R("sg", 1, nl, 2), False, False)
        mm(P(bLO, 1, nl, 2), R("mi"), R("big", 0, m), False, False)
        mm(P(bLO, 1, nl, 2), R("mi"), R("big", 128, 128 + m), False, True)
        for lo, hi in ((m // 2, m), (0, m // 2)):
            scan(R("m1", 2 * lo, 2 * hi), P(bLO, 2 * lo, 2 * hi), R("of", 2 * lo, 2 * hi), 0.0, A.mult, A.add)
            cp(R("ol", lo, hi), R("m1", 2 * lo + 1, 2 * hi, 2))

    def parents(nl, t, late=False):
        k = nl // 16
        if PPLATE != late:
            return
        act(R("pp", 0, nl), ind(CELLS, R("tn", 0, k)), bias=cPP)
        for r in range(16):
            mm(P(bL, 0, k), R("zd", 15 - r, 143 - r), R("pp", r, nl, 16), r == 0, r == 15)
        if late:
            return tt(slot(t + 1, sPAR, 0, k), P(bL, 0, k), slot(t, sY, 0, k), A.subtract)
        tt(R("pa", 0, k), P(bL, 0, k), slot(t - 1, sY, 0, k), A.subtract)
        tt(R("pa", 16, 16 + k), slot(t - 1, sY, 0, k), slot(t, sY, 0, k), A.subtract)
        tt(R("pa", 32, 32 + k), R("pa", 0, k), R("d0", 2, 4 * k, 4), A.mult)
        tt(slot(t + 1, sPAR, 0, k), R("pa", 32, 32 + k), R("pa", 16, 16 + k), A.add)

    def step(nl, t, last):
        k = nl // 16
        wb = "w%d" % (t % 2)
        final = t == ROUNDS * STEPS - 1
        h = 16 * (k // 2) if TWOF else 0
        if t:
            parents(nl, t - 1, True)
        mm(P(bF, h, nl), R("mi"), R("thr", h, nl), True, False)
        if h:
            mm(P(bA, 0, h), R("mi"), R("thr", 0, h), True, False)
        if SVLATE:
            act(R("sv", 0, nl), ind(CELLS, R("a0", 0, k)), bias=cNV0)
        mm(P(bR, 0, nl), R("mn"), R("sv", 0, nl), True, False)
        at, hi, top = 0, nl, nl
        for lo, cut in PIECES[nl]:
            for e, a, b in (("s", lo, cut), ("v", cut, top)):
                if a < b:
                    if e == "s":
                        act(R("vv", 8 * a, 8 * b), ind(CELLS, R("ol", a // 2, b // 2)), bias=cNV0)
                    else:
                        ts(R("vv", 8 * a, 8 * b), ind(CELLS, R("ol", a // 2, b // 2)), cNV0, A.add)
                    scan(R("rr", 8 * a, 8 * b), R("mp", 0, 8 * (b - a)), R("vv", 8 * a, 8 * b))
            top = lo
            if lo not in DECODE[nl]:
                continue
            bM, bX = DEC[DECODE[nl].index(lo) % len(DEC)]
            RR = R("rr", 8 * lo + 7, 8 * hi, 8)
            mm(P(bM, lo, hi), R("mi"), R("mk", lo, hi), True, False)
            mm(P(bM, lo, hi), R("dec"), RR, False, True)
            mm(P(bX, lo, hi), R("dec"), RR, True, True)
            scan(R("xs", 3 * lo, 3 * hi, 3), R("pat2", lo, hi), P(bM, lo, hi), FLOOR, A.min, A.max)
            act(R("xu", lo, hi), P(bX, lo, hi), AF.Relu)
            if BFC:
                if t and t % STEPS == 0 and hi > OWN:
                    a = max(lo, OWN)
                    tt(R("xs", 3 * a + 45, 3 * hi, 48), R("xs", 3 * a + 45, 3 * hi, 48), R("wl", a // 16, hi // 16), A.add)
                (act if lo in XHS else cp)(R("xh", lo // 16, hi // 16), R("xs", 3 * lo + 45, 3 * hi, 48))
                tt(R("xl", lo // 16, hi // 16), R("xs", 3 * lo + 45, 3 * hi, 48), R("xh", lo // 16, hi // 16), A.subtract)
            for j in range(hi // 16 - 1, lo // 16 - 1, -1):
                w = nl - 16 * j
                bw = R("bwj", 128 * j, 128 * j + 128) if BFC else R("bw")
                if BFC:
                    ts(R("ee", at, at + w), R("xu", 16 * j, nl), R("xh", j, j + 1), A.subtract, R("xl", j, j + 1), A.is_equal)
                else:
                    ts(R("ee", at, at + w), R("xu", 16 * j, nl), R("xs", 48 * j + 45, 48 * j + 46), A.is_equal, R("wl", j, j + 1), A.mult)
                c = max(h - 16 * j, 0)
                mm(P(bF, 16 * j + c, nl), bw, R("ee", at + c, at + w), False, j == 0)
                if c:
                    mm(P(bA, 16 * j, h), bw, R("ee", at, at + c), False, j == 0)
                at += w
            hi = lo
        RR = R("rr", 7, 8 * nl, 8)
        mm(P(bR, 0, nl), R("mh"), RR, False, True)
        scan(R("bo", 0, 3 * k), R("b0", 0, 3 * k), R("xs", 45, 45 + 48 * k, 16), 0.0, A.max, A.min)
        if final:
            act(R("rp", 0, nl), RR, AF.Relu, bias=0.25)
            act(R("tr", 0, nl), P(bR, 0, nl), AF.Relu)
            mm(P(bR, 0, nl), R("mn"), R("tr", 0, nl), True, False)
            mm(P(bR, 0, nl), R("mu"), R("rp", 0, nl), False, True)
            act(R("sg", 0, nl), P(bR, 0, nl), AF.Relu, bias=2.0, scale=cNKI)
            ts(slot(t, sDUM), R("bo", 2, 3 * k, 3), 1200.0, A.add)
        else:
            act(R("ww", 0, nl), P(bR, 0, nl), AF.Relu)
            ts(R("tb", 0, k), R("bo", 2, 3 * k, 3), -16.0, A.mult, 19200.0, A.subtract)
            act(ind(CT, R("tb", 0, k)), R("ww", 0, nl), AF.Silu)
        XS = R("xs", 45, 48 * k, 48)
        tt(slot(t, sX, 0, k), XS, R("pz", 0, k), A.add)
        tt(slot(t, sCX, 0, k), R("cur", 0, k), XS, A.subtract)
        ts(R("d0", 1, 4 * k, 4), XS, -1500.0, A.is_lt)
        ts(R("d0", 2, 4 * k, 4), XS, (DS - 0.5) / 16, A.is_lt)
        scan(R(wb, 38, 38 + 48 * k, 12), R("d0", 0, 4 * k), R(wb, 37, 37 + 48 * k, 12), 0.0, A.mult, A.add)
        if not last:
            ts(R("tn", 0, k), slot(t, sRAW, 0, k), 16.0, A.mult, float(C0), A.subtract)
        act(R("lim", 0, k), slot(t, sRAW, 0, k), scale=16.0, bias=1.5 * 2 ** 23)
        act(slot(t, sY, 0, k), R("lim", 0, k), scale=1.0 / 16, bias=-1.5 * 2 ** 19)
        if not last:
            lists(nl)
            parents(nl, t)
            choose(nl)
        elif not final:
            before(t // STEPS, t)
        scan(R(wb, 3 * h, 3 * nl, 3), R("pat", h, nl), P(bF, h, nl))
        if h:
            scan(R(wb, 0, 3 * h, 3), R("pat", 0, h), P(bA, 0, h))
        scan(R("fo", 0, 3 * k), R("f0", 0, 3 * k), R(wb, 45, 45 + 48 * k, 16), 0.0, A.mult, A.min)
        ts(R("th", 0, k), R("fo", 2, 3 * k, 3), -16.0, A.mult)
        if final:
            for lo, hi in zip(CUTS, CUTS[1:]):
                act(R("ab", lo, hi), R("ct", C0 + lo, C0 + hi), AF.Abs, bias=-144.0, scale=cKI)
                if lo in OUTS:
                    act(R("outv", C0 + lo, C0 + hi), R("ab", lo, hi), scale=-1.0, bias=144.0)
                else:
                    ts(R("outv", C0 + lo, C0 + hi), R("ab", lo, hi), -1.0, A.mult, 144.0, A.add)
            tt(ind(R("outv"), R("th", 0, k)), R("sg", 0, nl), R("two"), A.add)
        elif HOLEV:
            cp(ind(CT, R("th", 0, k)), R("dc%d" % (t % 2), 0, nl))
        else:
            act(ind(CT, R("th", 0, k)), R("dc%d" % (t % 2), 0, nl), AF.Silu)

    def kept(nl, t):
        k = nl // 16
        act(R("xm", 0, k), slot(t, sX, 0, k), bias=-(DS + C0 - 0.5) / 16)
        tt(R("nl", 0, k), R("fo", 1, 3 * k, 3), R("xm", 0, k), A.is_ge)

    SI, EX = R("ct", C0, C0 + DS), R("ct", C0 + W - DS, C0 + W)
    peers = [T.cores[(rank + d) % 4] for d in range(1, 4)]
    masks, used = {}, []
    for j in sorted(range(3), key=lambda j: len(topo.engines(core, peers[j]))):
        es = [e for e in topo.engines(core, peers[j]) if e not in used][:ENG]
        used += es
        masks[j] = sum(1 << e for e in es)

    def send(x, blocks):
        def call():
            tr = []
            for j, b in enumerate(blocks):
                rid, pid = topo.addr(peers[j], core)
                tr.append(RemoteDMATransfer(dst_ids=[DstId(rid=rid, pnc=pid)], dma_engine_mask=masks[j], remote_sem=T.sem["arr%d" % x],
                                            src=ap(R("stg%d" % x, S * b, S * b + S)), dst=ap(R("land%d" % x, S * b, S * b + S))))
            return g.remote_dma_fused(tr, local_sem=T.sem["snt%d" % x])
        add("g", call, [R("stg%d" % x)], [], kind="r", ext=x)

    def arrived(x):
        add("v", None, [], [R("land%d" % x)], kind="w", ext=x)
        return R("land%d" % x)

    def before(x, t):
        act(R("stg%d" % (2 * x)), EX, scale=LIFT)
        send(2 * x, (2, 1, 0))
        ts(R("s3"), slot(t, sY), ZR, A.is_equal)
        tt(R("s2"), R("s3"), R("gz"), A.mult)
        act(R("s1"), R("s3"), scale=ZR)
        tt(slot(t, sY), slot(t, sY), R("s2"), A.add)
        tt(slot(t - 1, sY), slot(t - 1, sY), R("s1"), A.max)
        ts(R("tn"), slot(t, sY), 16.0, A.mult, float(C0), A.subtract)
        lists(L)
        if x == 0:
            ms(R("d0", 42, 64, 4), 0.0)
        else:
            tt(R("d0", 2, 64, 4), R("d0", 2, 64, 4), R("s3"), A.is_gt)
        parents(L, t)

    def exchange(x, nl, t):
        act(R("stg%d" % (2 * x + 1)), SI, AF.Sign, bias=cNV0)
        send(2 * x + 1, (0, 1, 2))
        kept(nl, t)
        tt(R("s2", 10, 16), R("nl", 10, 16), R("s3", 10, 16), A.subtract)
        ts(R("ta"), EX, cVL, A.is_gt)
        ts(R("tc"), EX, cV0, A.is_gt)
        tt(R("te"), R("ta"), R("tc"), A.subtract)
        tt(R("tm"), R("te"), R("dg", 0, DS), A.mult)
        act(R("x2"), EX, scale=-0.5, bias=cHR2)
        ts(R("hm"), SI, cV0, A.is_le, 4096.0, A.mult)
        tt(R("dif"), R("te"), R("x2"), A.mult)
        tt(R("hr", 0, DS), EX, R("dif"), A.add)
        digits(L, "dc%d" % (1 - t % 2))
        tt(R("x1"), arrived(2 * x), R("hm"), A.add)
        tt(SI, SI, R("x1"), A.min)
        choose(L)
        ASK = arrived(2 * x + 1)
        tt(R("x2"), ASK, R("dif"), A.mult)
        tt(R("x3"), R("tm"), ASK, A.mult)
        tt(EX, R("hr", 0, DS), R("x2"), A.add)
        scan(R("x4"), R("pat", 0, DS), R("x3"))
        tt(R("nl", 10, 16), R("x4", 15, DS, 16), R("s2", 10, 16), A.add)
        state(t)

    lists(OWN)
    digits(OWN, "dc0")
    choose(OWN)
    act(slot(0, sPAR, 0, 10), slot(1, sY, 0, 10), scale=-1.0, bias=ZR)
    state(-1)
    t = 0
    for rnd in range(ROUNDS):
        nl = OWN if rnd == 0 else L
        for st in range(STEPS):
            step(nl, t, st == STEPS - 1)
            if st < STEPS - 1:
                digits(nl, "dc%d" % (1 - t % 2))
                kept(nl, t)
                state(t)
            elif rnd < ROUNDS - 1:
                exchange(rnd, nl, t)
            t += 1

    for z, a, b, c in ((slot(t - 2, sY), "s1", "s2", "yq"), (slot(t - 1, sY), "s3", "geo", "dy")):
        ts(R(a), z, ZR, A.is_equal, -float(REST + 1), A.mult)
        act(R(b), z, scale=16.0, bias=-float(C0))
        tt(R(c), R(a), R(b), A.add)
    kept(L, t - 1)
    tt(R("pz"), R("dy"), R("yq"), A.subtract)
    tt(R("lim"), R("pz"), R("nl"), A.mult)
    tt(R("yo"), R("yq"), R("lim"), A.add)
    store("y", T.ya[:, :], R("yo"))
    store("s", T.yv[:, :], R("outv", C0, C0 + W))

    ops[:] = arrange(ops)
    known = {e: 0 for e in Q}
    prev = {e: 0 for e in Q}
    done, waits, need = [], [], set()
    for i, (o, cf) in enumerate(zip(ops, conflicts(ops))):
        deps, e = [j for j in cf if cf[j]], o["e"]
        waits.append([])
        for j in sorted(deps, reverse=True):
            if ops[j]["k"] not in "rw" and not known[e] >> j & 1:
                waits[i].append(j)
                need.add(j)
                known[e] |= done[j]
        if o["k"] == "c":
            prev[e] |= 1 << i
        done.append(known[e] | (prev[e] if o["k"] == "c" else 1 << i))
    tok, cnt, nxt = {}, {}, {e: 0 for e in POOL}
    for i, o in enumerate(ops):
        q = Q[o["e"]]
        for j in waits[i]:
            q.wait_ge(T.sem[tok[j][0]], tok[j][1])
        if o["k"] == "w":
            q.wait_ge(T.sem["arr%d" % o["ext"]], 3 * ENG)
            continue
        ins = o["fn"]()
        if o["k"] == "d" or i in need:
            e, by = ("d", 16) if o["k"] == "d" else (o["e"], 1)
            s = "%s%d" % (e, nxt[e] % POOL[e])
            nxt[e] += 1
            cnt[s] = cnt.get(s, 0) + by
            ins.then_inc(T.sem[s], by)
            tok[i] = (s, cnt[s])
    for i, o in enumerate(ops):
        if o["k"] == "d" and i not in need:
            g.sync.wait_ge(T.sem[tok[i][0]], 16)
    for x in range(2 * ROUNDS - 2):
        g.wait_ge(T.sem["snt%d" % x], 3 * ENG)
